import numpy as np, ml_dtypes
CORES = [10,34,74,98]
N = 4
BF = ml_dtypes.bfloat16
def gentries(a):
    return np.ascontiguousarray(a.reshape(8, 16, -1).transpose(0, 2, 1)).reshape(8, -1)
def gtable(e):
    e = np.asarray(e); return np.ascontiguousarray(e.reshape(8, -1, 16).transpose(0, 2, 1)).reshape(128, -1).astype(np.int32)
M, FAR, S, F, RO = 4096, 1, 512, 2048, 5
def trees(rng, top, share):
    on = ((np.arange(M) < top) | (rng.random((N, 8, M)) < share)).astype(np.int64)
    c = np.add.accumulate(on, axis=2) - 1; inner = (on == 1) & (2 * c + 2 <= M - 1)
    pi = np.concatenate([np.zeros((N, 8, 1), np.int64), 1 + np.argsort(rng.random((N, 8, M - 1)), axis=2)], axis=2)
    kl = np.zeros((N, 8, M), np.int64); kr = np.zeros((N, 8, M), np.int64)
    np.put_along_axis(kl, pi, np.where(inner, np.take_along_axis(pi, np.minimum(2 * c + 1, M - 1), 2), 0), 2)
    np.put_along_axis(kr, pi, np.where(inner, np.take_along_axis(pi, np.minimum(2 * c + 2, M - 1), 2), 0), 2)
    return kl, kr, pi
def starts(rng, pi, ia, ib):
    far = np.stack([np.concatenate([d * M + pi[(q + 1 + d) % N] for d in range(FAR)], axis=1) for q in range(N)])
    return np.take_along_axis(pi, ia, 2), np.take_along_axis(far, rng.integers(0, FAR, (N, 8, S)) * M + ib, 2)
def near(rng):
    return (M * rng.random((N, 8, S)) ** 3).astype(np.int64)
def signs(rng, v):
    q = rng.choice(np.array([0.004, 0.015, 0.03, 0.05]), (N, 8, 1, 1))
    return np.where(rng.random(v.shape) < 2 * q * rng.random((N, 8, 1, M)), -v, v)
def parts(rng):
    kl, kr, pi = trees(rng, M // 8, 0.75); a, b = starts(rng, pi, near(rng), near(rng))
    return signs(rng, rng.integers(0, 4097, (N, 8, 16, M))), kl, kr, pi, a, b
def pack(h, kl, kr, a, b):
    return {"h": np.ascontiguousarray(h.reshape(N, 128, M)).astype(np.float32).astype(BF), "kl": kl.astype(np.int32), "kr": kr.astype(np.int32),
            "sa": np.stack([gtable(x) for x in a]), "sb": np.stack([gtable(x) for x in b])}
def setup_inputs(rng):
    h, kl, kr, pi, a, b = parts(rng)
    return pack(h, kl, kr, a, b)
def setup_inputs_alike(rng):
    h, kl, kr, pi, a, b = parts(rng)
    a[:, 0] = np.tile(a[:, 0, :4], (1, S // 4)); b[:, 0] = np.tile(b[:, 0, :4], (1, S // 4))
    a[:, 1] = rng.choice(np.array([0, M - 1]), (N, S)); b[:, 1] = rng.choice(np.array([0, FAR * M - 1]), (N, S))
    a[:, 1, 0] = 0; b[:, 1, 0] = 0; kl[:, 1, 0] = 0; kr[:, 1, 0] = 0; h[:, 1, :, 0] = np.abs(h[:, 1, :, 0])
    la, lb = starts(rng, pi, M - 1 - rng.integers(0, M // 8, (N, 8, S)), M - 1 - rng.integers(0, M // 8, (N, 8, S)))
    a[:, 2] = la[:, 2]; b[:, 2] = lb[:, 2]
    inner = kl > 0; own = np.maximum(np.arange(M), 1)
    kl[:, 4] = np.where(inner[:, 4], own, 0); kr[:, 4] = np.where(inner[:, 4], own, 0)
    few = np.array([1, M // 2, M - 1])
    kl[:, 6] = np.where(inner[:, 6], rng.choice(few, (N, M)), 0); kr[:, 6] = np.where(inner[:, 6], rng.choice(few, (N, M)), 0)
    return pack(h, kl, kr, a, b)
def setup_inputs_cold(rng):
    h, kl, kr, pi, a, b = parts(rng); o = [int(x) for x in rng.permutation(8)]
    h[:, o[0]] = -1 - np.abs(h[:, o[0]])
    h[:, o[1]] = np.where(rng.random((N, 16, M)) < 0.1, -1, 1) * np.abs(h[:, o[1]])
    for g in (o[2], o[4], o[5]):
        h[:, g] = np.abs(h[:, g]); z = pi[:, g, M - 1]
        h[np.arange(N), g, 0, z] = -65536; a[:, g] = z[:, None]
    one = np.array([7, 9, 10, 11, 12, 13, 14]); level = np.arange(31, 63)
    for q in range(N):
        nx = (q + 1) % N
        h[q, o[4], 0, pi[q, o[4], one]] = -65536; h[q, o[5], 0, pi[q, o[5], level]] = -65536
        j = (0, S - 1)[q % 2]; a[q, o[2], j] = pi[q, o[2], 1]; b[q, o[2], j] = pi[nx, o[2], 1]
        j = (0, S - 1, S // 2, 17)[q % 4]
        a[q, o[4], j] = pi[q, o[4], M - 3]; b[q, o[4], j] = pi[nx, o[4], (M - 3, 1)[q % 2]]
        a[q, o[5], j] = pi[q, o[5], M - 3]; b[q, o[5], j] = pi[nx, o[5], (7, 3, 1, 0)[q % 4]]
    q = int(rng.integers(0, N)); h[q, o[3]] = -1 - np.abs(h[q, o[3]])
    return pack(h, kl, kr, a, b)
def setup_inputs_room(rng):
    kl, kr, pi = trees(rng, M, 1.0); h = rng.integers(0, 4097, (N, 8, 16, M))
    h[np.arange(N)[:, None], np.arange(8)[None, :], rng.integers(0, 16, (N, 8)), pi[:, :, M - 1]] = -65536
    ia = near(rng); ib = near(rng); w = S // 8; o = rng.permutation(8); low = M // 2 - 1; safe = low + M // 16
    for q in range(N):
        for g in range(8):
            c = int(o[g])
            if c == 7: continue
            leaf = rng.integers(low, M - 1, S); deep = rng.integers(0, M // 8 - 1, S)
            if c < 3: deep = rng.integers(M // 16 - 1, M // 8 - 1, S)
            if c == 4 or c == 5:
                t = M // 16 if c == 4 else M // 32
                deep = rng.integers(t - 1, 2 * t - 1, S); leaf = rng.integers(low, safe, S)
                dead = safe + np.flatnonzero(rng.random(M - 1 - safe) < 0.75)
                h[q, g, rng.integers(0, 16, len(dead)), pi[q, g, dead]] = -65536
            u = deep
            if c < 4:
                n = 3 * S + w + (0, 1, -1, (0, 1, -1)[q % 3])[c]; x = n // 7; y = n - 7 * x
                u = np.concatenate([deep[:x], rng.integers(M // 4 - 1, M // 2 - 1, y), np.full(w, M - 1, np.int64), rng.integers(M // 2 - 1, M - 1, S - x - y - w)])
                u = rng.permutation(u)
            flip = rng.random(S) < 0.5
            ia[q, g] = np.where(flip, leaf, u); ib[q, g] = np.where(flip, u, leaf)
    a, b = starts(rng, pi, ia, ib)
    return pack(h, kl, kr, a, b)
def setup_inputs_spread(rng):
    kl, kr, pi = trees(rng, 32, 0.55); a, b = starts(rng, pi, near(rng), near(rng))
    v = np.floor(np.exp2(16 * rng.random((N, 8, 1, M))) * rng.random((N, 8, 16, M))).astype(np.int64)
    v = np.where(rng.random(v.shape) < 0.01, 65536, v)
    return pack(signs(rng, v), kl, kr, a, b)
def setup_inputs_ties(rng):
    h, kl, kr, pi, a, b = parts(rng)
    u = rng.random((N, 8, 16, M)); h = np.where(u < 0.05, -1, np.where(u < 0.15, 0, 1)) * np.array([1, 128, 32768, 65536, 1, 2, 1, 4]).reshape(1, 8, 1, 1)
    h[:, 6, :8] = 65536
    q = np.arange(N); nx = (q + 1) % N
    h[q, 0, :, pi[q, 0, 1]] = -65536
    for j, v in ((3, 1), (4, 1), (M - 1, 1), (2, -2), (5, 0), (6, 0), (9, -1), (M - 2, 4), (M - 3, 4)): h[q, 0, :, pi[q, 0, j]] = v
    kl[q, 0, pi[q, 0, 9]] = pi[q, 0, M - 2]; kr[q, 0, pi[q, 0, 9]] = pi[q, 0, M - 3]
    a[q, 0, 0] = pi[q, 0, M - 1]; b[q, 0, 0] = pi[nx, 0, 1]
    a[q, 0, 1] = pi[q, 0, 1]; b[q, 0, 1] = pi[nx, 0, M - 1]
    a[q, 0, 2] = pi[q, 0, 2]; b[q, 0, 2] = pi[nx, 0, 9]
    d = pack(h, kl, kr, a, b); x = d["h"].astype(np.float32)
    d["h"] = np.where((x == 0) & (rng.random(x.shape) < 0.5), np.float32(-0.0), x).astype(BF)
    return d
def check_inputs(d):
    bad = []
    x = np.asarray(d["h"]).astype(np.float32)
    if not np.all(x == np.floor(x)): bad.append("whole numbers in h")
    if not np.max(np.abs(x)) <= 65536: bad.append("range of h")
    for k, hi in (("kl", M - 1), ("kr", M - 1), ("sa", M - 1), ("sb", FAR * M - 1)):
        if np.min(d[k]) < 0 or np.max(d[k]) > hi: bad.append("range of " + k)
    if not np.all((np.asarray(d["kl"]) == 0) == (np.asarray(d["kr"]) == 0)): bad.append("two kids or none")
    return bad
def reference(h, kl, kr, sa, sb):
    hw = h.astype(np.float32).astype(np.int64).reshape(N, 8, 16, M); left = kl.astype(np.int64); right = kr.astype(np.int64)
    ya = np.full((N, 8, F), -1.0, np.float32); yb = np.full((N, 8, F), -1.0, np.float32); ys = np.zeros((N, 8, F), np.float32)
    swap = np.arange(16) ^ 1
    for r in range(N):
        far = [(r + 1 + d) % N for d in range(FAR)]; first = gentries(sa[r]).astype(np.int64); second = gentries(sb[r]).astype(np.int64)
        for g in range(8):
            ha = hw[r, g]; hb = np.concatenate([hw[q, g] for q in far], axis=1); hs = hb[swap]
            la, ra = left[r, g], right[r, g]
            lb = np.concatenate([np.where(left[q, g] > 0, left[q, g] + d * M, 0) for d, q in enumerate(far)])
            rb = np.concatenate([np.where(right[q, g] > 0, right[q, g] + d * M, 0) for d, q in enumerate(far)])
            za = np.add.reduce(ha, axis=0); zb = np.add.reduce(hb, axis=0)
            a, b = first[g], second[g]
            for rnd in range(RO):
                fa = la[a] == 0; fb = lb[b] == 0
                oa = ~fa & (fb | (za[a] >= zb[b])); ob = ~fb & ~oa
                ca = np.stack([np.where(oa, la[a], a), np.where(oa, ra[a], a)], axis=1).reshape(-1)
                cb = np.stack([np.where(ob, lb[b], b), np.where(ob, rb[b], b)], axis=1).reshape(-1)
                there = np.stack([np.ones(len(a), bool), oa | ob], axis=1).reshape(-1)
                keep = there & np.all(ha[:, ca] + hs[:, cb] >= 0, axis=0)
                a = ca[keep][:F]; b = cb[keep][:F]
            ya[r, g, :len(a)] = a; yb[r, g, :len(a)] = b; ys[r, g, :len(a)] = za[a] + zb[b]
    return {"ya": ya, "yb": yb, "ys": ys}

@@ -1,0 +1,615 @@
+from concourse.mybir import AluOpType as A, ActivationFunctionType as AF
+
+M = 4096
+SO = 4112
+HALF = 2048
+COL = HALF + 0.25
+PEN = 16384.0
+BIG = 16384.0
+OPT = {"route": "abxx", "order": "k012s3", "first": 8, "spath": 1}
+NDMA = 48
+
+
+def _sb(n, dt):
+    return ("sbuf", [128, n], dt)
+
+
+SCRATCH = {}
+for _dt, _list in (
+        ("bfloat16", dict(H=2 * SO, relay=4096, Z=1032, WF=144, WS=144, IB=128, BM=128, LT=128, UGE=128, UGT=128,
+                          NF=3584, FL=7168, KB=1024, S=144, F12=192)),
+        ("float16", dict(W16=2064, X16=2064, CK16=512, FK16=512, WM=720, WN=720, WB=864, WC=864, WT=640, WU=1280,
+                         E=320, I16=128, ISO=128, MD=2048, P=1024, Q=768, INV=128)),
+        ("float32", dict(TA=SO, TB=SO, W=6288, W2=6288, CK=768, FK=768, tmpk=768, SZ=256, FSZ=256, SZU=256,
+                         FSZU=256, IDN=256, IDR=256, J=160, JG=128, CD=128, TT=128, col=64, col2=32, MB=2048,
+                         OUT=2048, K=512, ZZ=384, D=2048)),
+        ("int32", dict(kli=256, kri=256, sai=64, pci=8)),
+        ("uint16", dict(UAB=256, UL=768, UP=128))):
+    for _k, _n in _list.items():
+        SCRATCH[_k] = _sb(_n, _dt)
+for _b in range(8):
+    SCRATCH["ps%d" % _b] = ("psum", [128, 512], "float32")
+SEMAPHORES = (["cV", "cS", "cP", "cG", "sent", "rk", "rs", "hout"] + ["rh%d" % k for k in range(4)]
+              + ["hi%d" % k for k in range(4)] + ["d%d" % i for i in range(NDMA)])
+
+
+def routes(src, dst, T, topo):
+    ok = [c for c in topo.cores_of(src) if c != src and T.rank_of(c) is None and topo.may_write(c, dst)]
+    other = [c for c in ok if topo.die(c) != topo.die(src)]
+    same = [c for c in ok if topo.die(c) == topo.die(src)]
+    pick = {"d": None, "a": other[0], "b": other[-1], "x": same[0] if same else None}
+    return [pick[c] for c in OPT["route"]]
+
+
+def bits(m):
+    return bin(m).count("1")
+
+
+def helper_program(g, core, T, topo):
+    n = len(T.cores)
+    out = 0
+    for r in range(n):
+        src, dst = T.cores[r], T.cores[(r - 1) % n]
+        for k, h in enumerate(routes(src, dst, T, topo)):
+            if h == core:
+                g.wait_ge(T.sem["hi%d" % k], bits(topo.mask(src, core)))
+                rid, pid, _ = topo.addr(dst)
+                m = topo.mask(core, dst)
+                g.remote_dma(T.H[:, SO + 1024 * k:SO + 1024 * (k + 1)], T.relay[:, 1024 * k:1024 * (k + 1)],
+                             T.sem["rh%d" % k], T.sem.hout, pid, rid, m)
+                out += bits(m)
+    if out:
+        g.wait_ge(T.sem.hout, out)
+
+
+def rank_program(g, core, T, topo):
+    rank = T.rank_of(core)
+    if rank is None:
+        helper_program(g, core, T, topo)
+        return
+    n = len(T.cores)
+    dst, src = T.cores[(rank - 1) % n], T.cores[(rank + 1) % n]
+    V, S = g.vector, g.scalar
+    eng = {"V": V, "S": S, "P": g.tensor, "G": g, "Y": g.sync}
+    ps = [T["ps%d" % b] for b in range(8)]
+    cnt = {"V": 0, "S": 0, "P": 0, "G": 0}
+    seen = {e: {} for e in eng}
+    wr, rd, bank, ends = {}, {}, {}, {}
+    ndma, sent = [0], [0]
+
+    def need(e, reads, writes=(), banks=()):
+        ev = []
+        for k in reads:
+            ev += wr.get(k, [])
+        for k in writes:
+            ev += wr.get(k, []) + rd.get(k, [])
+        for b in banks:
+            ev += [x for o, x in bank.get(b, {}).items() if o != e]
+        top = {}
+        for s, v in ev:
+            top[s] = max(top.get(s, 0), v)
+        for s, v in top.items():
+            if seen[e].get(s, 0) < v:
+                eng[e].wait_ge(T.sem[s], v)
+                seen[e][s] = v
+
+    def done(e, ev, reads, writes, banks):
+        for k in reads:
+            rd.setdefault(k, []).append(ev)
+        for k in writes:
+            wr[k] = [ev]
+            rd[k] = []
+        for b in banks:
+            bank.setdefault(b, {})[e] = ev
+        ends[ev[0]] = max(ends.get(ev[0], 0), ev[1])
+
+    def op(e, fn, reads, writes, banks=()):
+        need(e, reads, writes, banks)
+        cnt[e] += 1
+        fn().then_inc(T.sem["c" + e], 1)
+        done(e, ("c" + e, cnt[e]), reads, writes, banks)
+
+    def mm(groups, reads, b, opens=True, closes=True):
+        need("P", reads, [], [b])
+        for grp in groups:
+            for j, (o, l, r) in enumerate(grp):
+                last = g.tensor.matmul(o, l, r, opens and j == 0, closes and j == len(grp) - 1)
+        cnt["P"] += 1
+        last.then_inc(T.sem.cP, 1)
+        done("P", ("cP", cnt["P"]), reads, [], [b])
+
+    def dma(e, out, in_, reads, writes):
+        need(e, reads, writes)
+        s = "d%d" % ndma[0]
+        ndma[0] += 1
+        eng[e].dma_start(out, in_).then_inc(T.sem[s], 16)
+        done(e, (s, 16), reads, writes, [])
+
+    def send(to, out, in_, sem, reads):
+        need("G", reads)
+        rid, pid, _ = topo.addr(to)
+        g.remote_dma(out, in_, T.sem[sem], T.sem.sent, pid, rid, topo.mask(core, to))
+        sent[0] += bits(topo.mask(core, to))
+
+    def arrives(key, sem, frm):
+        wr[key] = [(sem, bits(topo.mask(frm, core)))]
+        ends[sem] = wr[key][0][1]
+
+    def ts(out, in0, s1, s2, o0, o1, reads, writes, banks=()):
+        if s2 is None:
+            op("V", lambda: V.tensor_scalar(out, in0, s1, None, o0), reads, writes, banks)
+        else:
+            op("V", lambda: V.tensor_scalar(out, in0, s1, s2, o0, o1), reads, writes, banks)
+
+    def t1(out, in0, s1, o0, reads, writes, banks=()):
+        ts(out, in0, s1, None, o0, None, reads, writes, banks)
+
+    def tt(out, in0, in1, o, reads, writes, banks=()):
+        op("V", lambda: V.tensor_tensor(out, in0, in1, o), reads, writes, banks)
+
+    def cp(out, in_, reads, writes):
+        op("V", lambda: V.tensor_copy(out, in_), reads, writes)
+
+    def act(out, in_, scale, reads, writes, banks=()):
+        op("S", lambda: S.activation(out, in_, AF.Copy, scale=scale), reads, writes, banks)
+
+    def fill(out, c, key):
+        op("V", lambda: V.memset(out, c), [], [key])
+
+    def keys(name, lo, hi):
+        return ["%s_%d" % (name, k) for k in range(lo // 8, (hi + 7) // 8)]
+
+    def num(name, js):
+        return [name + str(j) for j in js]
+
+    arrives("FK16", "rk", src)
+    arrives("FSZ", "rs", src)
+    for k, h in enumerate(routes(src, core, T, topo)):
+        arrives("Hf%d" % k, "rh%d" % k, src if h is None else h)
+    HALL = num("Ho", range(4)) + num("Hf", range(4)) + ["Hd0", "Hd1"]
+
+    dma("S", T.kli[:], T.kl[:], [], ["kli"])
+    dma("Y", T.kri[:], T.kr[:], [], ["kri"])
+    for k in range(4):
+        c = slice(1024 * k, 1024 * (k + 1))
+        if rank % 2 == 0:
+            dma("Y", T.H[:, c], T.h[:, c], [], ["Ho%d" % k])
+        else:
+            dma("Y", T.H[0::2, c], T.h[1::2, c], [], ["Hx"])
+            dma("Y", T.H[1::2, c], T.h[0::2, c], [], ["Ho%d" % k])
+            wr["Ho%d" % k] = wr["Ho%d" % k] + wr.pop("Hx")
+    dma("S", T.sai[:, 0:32], T.sa[:], [], ["sa"])
+    dma("S", T.sai[:, 32:64], T.sb[:], [], ["sb"])
+
+    op("G", lambda: g.iota(T.pci[:, 0:1], [[1, 1]], 0, 1), [], ["pci0"])
+    for t, pat, base, mult, key in ((T.IDR, [[1, 256]], 0, 256, "IDR"), (T.J, [[1, 160]], 0, 0, "J"),
+                                    (T.JG, [[1, 8], [0, 16]], 0, 0, "JG"), (T.CD, [[16, 128]], M, 1, "CD")):
+        op("G", lambda: g.iota(t[:], pat, base, mult, allow_small_or_imprecise_dtypes=True), [], [key])
+    fill(T.Z[:], 0.0, "Z")
+    for t, key in ((T.TA, "TA"), (T.TB, "TB")):
+        for k in range(4):
+            act(t[:, 1028 * k:1028 * (k + 1)], T.Z[:, 0:1028], 1.0, ["Z"], [key + str(k)])
+    TAZ, TBZ = num("TA", range(4)), num("TB", range(4))
+    col, c2, pci, J = T.col, T.col2, T.pci, T.J
+    SH, AND = A.arith_shift_right, A.bitwise_and
+    cp(col[:, 0:1], pci[:, 0:1], ["pci0"], ["c_p"])
+    t1(pci[:, 1:2], pci[:, 0:1], 15, AND, ["pci0"], ["pci1"])
+    t1(pci[:, 2:3], pci[:, 0:1], 4, SH, ["pci0"], ["pci2"])
+    ts(pci[:, 3:4], pci[:, 0:1], 2, 3, SH, AND, ["pci0"], ["pci3"])
+    t1(pci[:, 4:5], pci[:, 0:1], 3, AND, ["pci0"], ["pci4"])
+    ts(pci[:, 5:6], pci[:, 0:1], 1, 7, SH, AND, ["pci0"], ["pci5"])
+    t1(pci[:, 6:7], pci[:, 0:1], 1, AND, ["pci0"], ["pci6"])
+    t1(pci[:, 7:8], pci[:, 0:1], 2, AND, ["pci0"], ["pci7"])
+    cp(col[:, 1:5], pci[:, 1:5], num("pci", range(1, 5)), ["c_4"])
+    cp(c2[:, 0:3], pci[:, 5:8], num("pci", range(5, 8)), ["c2a"])
+    c_p, c_pm, c_g, c_q, c_r, c_g15, c_gm = (col[:, j:j + 1] for j in range(7))
+    ts(c_g15, c_g, 16.0, 15.0, A.mult, A.add, ["c_4"], ["c_g15"])
+    t1(c_gm, c_g, -float(M), A.mult, ["c_4"], ["c_gm"])
+    t1(c2[:, 3:4], c_p, 14.0, A.add, ["c_p"], ["c2b"])
+    t1(col[:, 40:41], c_p, 13.0, A.add, ["c_p"], ["c_p13"])
+    t1(T.IDN[:], T.IDR[:], c_gm, A.add, ["IDR", "c_gm"], ["IDN"])
+    ts(T.WS[:], J[:, 0:144], c_g15, 1.0 / 256, A.is_equal, A.mult, ["J", "c_g15"], ["WS"])
+    t1(col[:, 8:24], J[:, 0:16], c_pm, A.is_equal, ["J", "c_4"], ["oh"])
+    t1(col[:, 24:28], J[:, 0:4], c_q, A.is_equal, ["J", "c_4"], ["oq"])
+    t1(col[:, 28:32], J[:, 0:4], c_r, A.is_equal, ["J", "c_4"], ["or"])
+    t1(col[:, 7:8], c_g15, 1.0, A.add, ["c_g15"], ["c_g16"])
+    lf, x0, x1, x2 = T.CK[:, 512:768], T.tmpk[:, 0:256], T.tmpk[:, 256:512], T.tmpk[:, 512:768]
+    t1(x0, T.kli[:], 0.0, A.is_equal, ["kli"], ["t0"])
+    t1(x1, T.kli[:], -float(HALF), A.add, ["kli"], ["t1"])
+    ts(x2, x0, float(M), -float(HALF), A.mult, A.add, ["t0"], ["t2"])
+    t1(lf, x0, -PEN, A.mult, ["t0"], ["lf"])
+    tt(x0, x0, T.IDN[:], A.mult, ["t0", "IDN"], ["t0"])
+    tt(T.CK[:, 256:512], x2, T.kri[:], A.add, ["t2", "kri"], ["CKr"])
+    tt(T.CK[:, 0:256], x0, x1, A.add, ["t0", "t1"], ["CKl"])
+    cp(T.CK16[:], T.CK[:, 0:512], ["CKl", "CKr"], ["CK16"])
+    for j, r in enumerate((4, 0, 1, 2, 3)):
+        ts(T.WM[:, 144 * j:144 * (j + 1)], J[:, 0:144], c_g15, col[:, 8 + r:9 + r], A.is_equal, A.mult,
+           ["J", "c_g15", "oh"], ["WM%d" % j])
+
+    need("P", ["WS"])
+    for i in range(16):
+        need("P", ["Ho%d" % (i // 4)])
+        last = g.tensor.matmul(ps[7][:, 0:256], T.WS[:, 15 - i:143 - i], T.H[:, 256 * i:256 * (i + 1)], i == 0, i == 15)
+    cnt["P"] += 1
+    last.then_inc(T.sem.cP, 1)
+    done("P", ("cP", cnt["P"]), [], [], [7])
+    tt(T.SZ[:], ps[7][:, 0:256], lf, A.add, ["lf"], ["SZ"], [7])
+    act(T.SZU[:], ps[7][:, 0:256], 256.0, [], ["SZU"], [7])
+    rt = routes(core, dst, T, topo)
+    for x in OPT["order"]:
+        if x == "k":
+            send(dst, T.FK16[:], T.CK16[:], "rk", ["CK16"])
+        elif x == "s":
+            send(dst, T.FSZ[:], T.SZ[:], "rs", ["SZ"])
+        else:
+            k = int(x)
+            c = slice(1024 * k, 1024 * (k + 1))
+            if rt[k] is None:
+                send(dst, T.H[:, SO + 1024 * k:SO + 1024 * (k + 1)], T.H[:, c], "rh" + x, ["Ho" + x])
+            else:
+                send(rt[k], T.relay[:, c], T.H[:, c], "hi" + x, ["Ho" + x])
+
+    def row(tab, r, tile, reads, key, zero=()):
+        need("Y", zero)
+        dma("Y", tab[r::16, 0:M], tile, reads, [key])
+    row(T.TA, 0, T.CK[:, 0:256], ["CKl"], "TAr0", TAZ)
+    row(T.TA, 1, T.CK[:, 256:512], ["CKr"], "TAr1")
+    row(T.TA, 4, T.SZ[:], ["SZ"], "TAr4")
+    t1(T.I16[:], J[:, 0:128], c_p, A.is_equal, ["J", "c_p"], ["I16"])
+    ts(T.ISO[:], J[:, 0:128], c_p, float(SO), A.is_equal, A.mult, ["J", "c_p"], ["ISO"])
+    t1(T.WN[:], T.WM[:], -1.0, A.mult, num("WM", range(5)), ["WN"])
+    cp(T.UAB[:, 0:32], T.sai[:, 0:32], ["sa"], ["UA0"])
+    cp(T.UAB[:, 64:96], T.sai[:, 32:64], ["sb"], ["UB0"])
+    t1(ps[0][:, 64:96], T.sai[:, 0:32], -float(HALF), A.add, ["sa"], ["v0"], [0])
+    t1(ps[2][:, 448:480], T.sai[:, 32:64], -float(HALF), A.add, ["sb"], ["v1"], [2])
+    t1(col[:, 42:43], col[:, 12:13], -2 * PEN, A.mult, ["oh"], ["dd0"])
+    fill(T.H[:, M:SO], -262144.0, "Hd0")
+    fill(T.H[:, SO + M:2 * SO], -262144.0, "Hd1")
+    cp(T.TA[:, M:M + 1], col[:, 42:43], ["dd0", "TA3"], ["TAd"])
+    cp(T.TB[:, M:M + 1], col[:, 42:43], ["dd0", "TB3"], ["TBd"])
+    t1(T.FK[:, 0:512], T.FK16[:], -1.0, A.mult, ["FK16"], ["FK"])
+    row(T.TB, 2, T.FK[:, 0:256], ["FK"], "TBr2", TBZ)
+    row(T.TB, 3, T.FK[:, 256:512], ["FK"], "TBr3")
+    row(T.TB, 4, T.FSZ[:], ["FSZ"], "TBr4")
+    ts(T.FK[:, 512:768], T.FK16[:, 256:512], float(HALF), -PEN, A.is_equal, A.mult, ["FK16"], ["FKl"])
+    TAK = TAZ + ["TAr0", "TAr1", "TAr4", "TAd"]
+    TBK = TBZ + ["TBr2", "TBr3", "TBr4", "TBd"]
+    ts(T.WF[:], J[:, 0:144], c_g15, BIG, A.is_equal, A.mult, ["J", "c_g15"], ["WF"])
+    t1(T.IB[:], J[:, 0:128], c_p, A.is_equal, ["J", "c_p"], ["IB"])
+    ts(col[:, 32:36], col[:, 24:28], col[:, 7:8], -1.0, A.mult, A.add, ["oq", "c_g16"], ["cf"])
+    ts(col[:, 36:40], col[:, 24:28], col[:, 40:41], -1.0, A.mult, A.add, ["oq", "c_p13"], ["ck"])
+    t1(T.BM[:], T.JG[:], c_g, A.is_equal, ["JG", "c_4"], ["BM"])
+    t1(T.UGT[:], J[:, 0:128], c_p, A.is_gt, ["J", "c_p"], ["UGT"])
+    for j in range(4):
+        t1(T.WB[:, 144 * j:144 * (j + 1)], J[:, 0:144], col[:, 32 + j:33 + j], A.is_equal, ["J", "cf"], ["WB%d" % j])
+    tt(T.LT[:], T.UGT[:], T.BM[:], A.mult, ["UGT", "BM"], ["LT"])
+    for j in range(2):
+        tt(T.WB[:, 144 * j + 577:144 * j + 720], T.WB[:, 144 * j + 1:144 * j + 144],
+           T.WB[:, 144 * j + 288:144 * j + 431], A.add, num("WB", (j, j + 2)), ["WB%d" % (4 + j)])
+    tt(T.UGE[:], T.BM[:], T.LT[:], A.subtract, ["BM", "LT"], ["UGE"])
+
+    def consts_a():
+        tt(x0, T.FSZ[:], T.FK[:, 512:768], A.subtract, ["FSZ", "FKl"], ["t0"])
+
+    def consts_b():
+        t1(T.E[:, 0:160], J[:], c2[:, 3:4], A.is_equal, ["J", "c2b"], ["E0"])
+        t1(c2[:, 8:16], J[:, 0:8], c2[:, 0:1], A.is_equal, ["J", "c2a"], ["o8"])
+        ts(c2[:, 6:7], c2[:, 2:3], -1.0, 1.0, A.mult, A.add, ["c2a"], ["sg"])
+        tt(T.E[:, 162:320], T.E[:, 2:160], T.E[:, 0:158], A.subtract, ["E0"], ["E1"])
+
+    def consts_c():
+        for u in range(8):
+            t1(T.WU[:, 160 * u + 2:160 * u + 160], T.E[:, 162:320], c2[:, 8 + u:9 + u], A.mult, ["E1", "o8"],
+               ["WU%d" % u])
+
+    def consts_d():
+        t1(T.WC[:, 0:576], T.WB[:, 0:576], c2[:, 6:7], A.mult, ["sg"] + num("WB", range(4)), ["WC0"])
+        for j in (4, 5):
+            t1(T.WC[:, 144 * j + 1:144 * j + 144], T.WB[:, 144 * j + 1:144 * j + 144], c2[:, 6:7], A.mult,
+               ["sg", "WB%d" % j], ["WC%d" % j])
+
+    def consts_e():
+        t1(c2[:, 4:6], J[:, 0:2], c2[:, 1:2], A.is_equal, ["J", "c2a"], ["o2"])
+        ts(T.TT[:], T.CD[:], c_g15, 15.0 - M, A.subtract, A.add, ["CD", "c_g15"], ["TT"])
+        tt(T.UGT[:], T.UGE[:], T.IB[:], A.subtract, ["UGE", "IB"], ["UGT"])
+        fill(T.S[:, 0:16], 0.0, "S0")
+    for j in range(4):
+        t1(T.WT[:, 160 * j:160 * (j + 1)], J[:], col[:, 36 + j:37 + j], A.is_equal, ["J", "ck"], ["WT%d" % j])
+
+    def zero_w(j):
+        for k in range(2):
+            dma("G", (T.W2, T.W)[j][:, 1032 * k:1032 * (k + 1)], T.Z[:], ["Z"], ["Wz%d_%d" % (j, k)])
+
+    def gb(ch, lo, hi, scale=-1.0):
+        o = 1024 * ch
+        act(T.MB[:, o + 16 * lo:o + 16 * hi], T.TB[:, :].indirect(T.UAB[:, 128 * ch + 64 + lo:128 * ch + 64 + hi]),
+            scale, TBK + ["UB%d" % ch], keys("MB%d" % ch, lo, hi))
+
+    def ga(ch, lo, hi, out=T.MD, key="MD"):
+        o = 1024 * ch
+        tt(out[:, o + 16 * lo:o + 16 * hi], T.TA[:, :].indirect(T.UAB[:, 128 * ch + lo:128 * ch + hi]),
+           T.MB[:, o + 16 * lo:o + 16 * hi], A.add, TAK + ["UA%d" % ch] + keys("MB%d" % ch, lo, hi),
+           keys("%s%d" % (key, ch), lo, hi))
+
+    MP = ((0, 0), (4, 0), (4, 64), (6, 0), (6, 64))
+
+    def meta(ch, nc, js, w=T.WM, wk=None):
+        o = 1024 * ch
+        for jj in js:
+            mm([[(ps[MP[j][0] + ch][:, MP[j][1]:MP[j][1] + nc], w[:, 144 * j + 15 - i:144 * j + 143 - i],
+                  T.MD[:, o + i:o + 16 * nc:16]) for i in range(16)] for j in jj],
+               keys("MD%d" % ch, 0, nc) + (wk or num("WM", jj)), MP[jj[0]][0] + ch)
+
+    def pt(ch, nc, j):
+        return T.P[:, 512 * ch + nc * j:512 * ch + nc * (j + 1)]
+
+    def dec(ch, nc, part):
+        k = "P%d_" % ch
+        if part == 0:
+            t1(pt(ch, nc, 6), ps[ch][:, 0:nc], 0.0, A.is_ge, [], [k + "6"], [ch])
+            t1(pt(ch, nc, 7), ps[ch][:, 0:nc], 0.0, A.is_lt, [], [k + "7"], [ch])
+        for j, b, c, m in (((5, 2, 448, 6), (4, 0, 64, 7)), ((0, 4, 0, 6), (1, 4, 64, 6)),
+                           ((2, 6, 0, 7), (3, 6, 64, 7)))[part]:
+            tt(pt(ch, nc, j), ps[b + ch][:, c:c + nc], pt(ch, nc, m), A.mult, [k + str(m), "v0", "v1"],
+               [k + str(j)], [b + ch])
+
+    def lists(ch, nc):
+        mm([[(ps[2 + ch][:, x * nc:(x + 1) * nc], w, pt(ch, nc, j))
+             for w, j in ((T.ISO[:], 7), (T.I16[:], x), (T.I16[:], 2 + x))] for x in range(2)],
+           num("P%d_" % ch, (0, 1, 2, 3, 7)) + ["I16", "ISO"], 2 + ch)
+
+    def decide(ch, nc, slot, fx, w=T.WM, wk=None, a=None, b=None, c=None, begun=False):
+        if not begun:
+            meta(ch, nc, ((0,), (1, 2)), w, wk)
+        if a:
+            a()
+        dec(ch, nc, 0)
+        out = ps[ch][:, 128:128 + nc]
+        mm([[(out, T.I16[:], pt(ch, nc, 4)), (out, T.I16[:], pt(ch, nc, 5)), (out, T.ISO[:], pt(ch, nc, 6))]],
+           num("P%d_" % ch, (4, 5, 6)) + ["I16", "ISO"], ch)
+        meta(ch, nc, ((3, 4),), w, wk)
+        if b:
+            b()
+        dec(ch, nc, 1)
+        t1(T.UL[:, 192 * slot + 2 * nc:192 * slot + 3 * nc], out, COL, A.add, [], ["UF%d" % slot], [ch])
+        for lo, hi in fx:
+            fixed(slot, nc, lo, hi)
+        if c:
+            c()
+        dec(ch, nc, 2)
+
+    CAND = ((0, 4), (2, 5), (1, 4), (3, 5))
+
+    def cands(ch):
+        mm([[(ps[2 + ch][:, 64 * (3 + j):64 * (4 + j)], T.I16[:], pt(ch, 64, x)) for x in CAND[j]] for j in range(4)],
+           num("P%d_" % ch, range(6)) + ["I16"], 2 + ch)
+
+    def grow(nc, lo, to):
+        for b, c, js in ((2, 448, (1, 3)), (0, 64, (0, 2))):
+            mm([[(ps[b + to][:, c + par:c + 64:2], T.I16[:], T.P[:, nc * x + lo:nc * x + lo + 32]) for x in CAND[j]]
+                for par, j in enumerate(js)], num("P0_", range(6)) + ["I16"], b + to)
+
+    def ua(ch):
+        t1(T.UAB[:, 128 * ch:128 * ch + 64], ps[ch][:, 64:128], COL, A.add, [], ["UA%d" % ch], [ch])
+
+    def ub(ch):
+        t1(T.UAB[:, 128 * ch + 64:128 * ch + 128], ps[2 + ch][:, 448:512], COL, A.add, [], ["UB%d" % ch], [2 + ch])
+
+    def ul(ch, nc, slot):
+        t1(T.UL[:, 192 * slot:192 * slot + 2 * nc], ps[2 + ch][:, 0:2 * nc], COL, A.add, [], ["UL%d" % slot], [2 + ch])
+
+    NFO, FLO = (0, 1024, 2048, 2560), (0, 2048, 4096, 5120)
+
+    def fixed(slot, nc, lo, hi):
+        o, u = NFO[slot], 192 * slot + 2 * nc
+        act(T.NF[:, o + 16 * lo:o + 16 * hi], T.H[:, :].indirect(T.UL[:, u + lo:u + hi]), -1.0,
+            HALL + ["UF%d" % slot], keys("NF%d" % slot, lo, hi))
+
+    def kids(slot, side, lo, nc=64):
+        o, u, f = NFO[slot] + 16 * lo, 192 * slot + side * nc + lo, FLO[slot] + 16 * (side * nc + lo)
+        tt(T.FL[:, f:f + 512], T.H[:, :].indirect(T.UL[:, u:u + 32]), T.NF[:, o:o + 512], A.is_lt,
+           HALL + ["UL%d" % slot] + keys("NF%d" % slot, lo, lo + 32), keys("FL%d_%d" % (slot, side), lo, lo + 32))
+
+    def kids_s(j, slot, side, lo):
+        o, u, f = NFO[slot] + 16 * lo, 192 * slot + side * 64 + lo, FLO[slot] + 16 * (side * 64 + lo)
+        kb, out = T.KB[:, 512 * j:512 * (j + 1)], ps[j][:, 0:512]
+        act(kb, T.H[:, :].indirect(T.UL[:, u:u + 32]), -1.0, HALL + ["UL%d" % slot], ["KB%d" % j])
+        mm([[(out, T.IB[:], kb), (out, T.IB[:], T.NF[:, o:o + 512])]],
+           ["KB%d" % j, "IB"] + keys("NF%d" % slot, lo, lo + 32), j)
+        op("S", lambda: S.activation(T.FL[:, f:f + 512], out, AF.Relu), [],
+           keys("FL%d_%d" % (slot, side), lo, lo + 32), [j])
+
+    def fails(slot, nc, outs, b, carry, ckey, sides=(0, 1)):
+        grp = []
+        for side in sides:
+            f = FLO[slot] + side * 16 * nc
+            x = [(outs[side], T.WF[:, 15 - i:143 - i], T.FL[:, f + i:f + 16 * nc:16]) for i in range(16)]
+            grp.append(x + ([(outs[side], T.IB[:], carry)] if ckey else []))
+        mm(grp, [k for x in sides for k in keys("FL%d_%d" % (slot, x), 0, nc)] + ["WF", "IB"] + ckey, b)
+
+    def fails_full(ch, rnd, sides):
+        b = ps[4 + ch]
+        fails(ch, 64, [b[:, 0:64], b[:, 64:128]], 4 + ch, T.F12[:, 64 + 64 * ch:128 + 64 * ch],
+              ["F2"] if rnd == 3 else [], sides)
+
+    def post_a(ch, rnd):
+        f, c = ps[4 + ch], ps[2 + ch]
+        k0, z0, s0, kk = 256 * ch, 192 * ch, 16 + 64 * ch, "K%d_" % ch
+        kL, kR, nL, both = (T.K[:, k0 + 64 * j:k0 + 64 * (j + 1)] for j in range(4))
+        t1(T.K[:, k0:k0 + 128], f[:, 0:128], 0.0, A.is_equal, [], [kk + "0"], [4 + ch])
+        t1(nL, f[:, 0:64], 0.0, A.is_gt, [], [kk + "2"], [4 + ch])
+        tt(T.ZZ[:, z0:z0 + 64], f[:, 0:64], T.CD[:, 64 * ch:64 * ch + 64], A.min, ["CD"], ["Z%d_0" % ch], [4 + ch])
+        op("V", lambda: V.tensor_tensor_scan(T.S[:, s0:s0 + 64], kL, kR, T.S[:, s0 - 1:s0], A.add, A.add),
+           [kk + "0", "S%d" % ch], ["S%d" % (ch + 1)])
+        tt(both, f[:, 64:128], kL, A.is_lt, [kk + "0"], [kk + "3"], [4 + ch])
+        tt(T.ZZ[:, z0 + 64:z0 + 128], f[:, 64:128], T.ZZ[:, z0:z0 + 64], A.min, ["Z%d_0" % ch], ["Z%d_1" % ch],
+           [4 + ch])
+        if rnd == 3:
+            grp = [[(f[:, 128 + u:192:4], T.LT[:], T.S[:, s0 + 3:s0 + 64:4]),
+                    (f[:, 128 + u:192:4], T.UGT[:], T.S[:, s0 - 1:s0 + 63:4]),
+                    (f[:, 128 + u:192:4], T.IB[:], T.S[:, s0 - 1 + u:s0 + 63:4])] for u in range(4)]
+        else:
+            grp = [[(f[:, 128:192], T.LT[:], T.S[:, s0:s0 + 64]), (f[:, 128:192], T.UGE[:], T.S[:, s0 - 1:s0 + 63])]]
+        if ch == 1:
+            grp.append([(f[:, 192:193], T.BM[:], T.S[:, 143:144])])
+        mm(grp, num("S", (ch, ch + 1)) + ["LT", "UGT", "UGE", "IB", "BM"], 4 + ch)
+        for j, (s, m, mk) in enumerate(((3, kL, "0"), (4, kL, "0"), (5, nL, "2"), (6, nL, "2"), (5, both, "3"),
+                                        (6, both, "3"))):
+            tt(T.Q[:, 384 * ch + 64 * j:384 * ch + 64 * (j + 1)], c[:, 64 * s:64 * (s + 1)], m, A.mult, [kk + mk],
+               ["Q%d_%d" % (ch, j)], [2 + ch])
+        nu, w, wk, o0 = ((8, T.WU, "WU", 14), (4, T.WT, "WT", 12))[ch]
+        st = 160 + 16 // nu
+        mm([[(ps[6 + ch][:, u:64 * nu:nu], w[:, st * u + o0 - 4 * q:st * u + 128 + o0 - 4 * q],
+              T.Q[:, 384 * ch + 64 * j:384 * ch + 64 * (j + 1)]) for j, q in enumerate((0, 1, 0, 1, 2, 3))]
+            for u in range(nu)], num("Q%d_" % ch, range(6)) + num(wk, range(nu)), 6 + ch)
+
+    def post_b(ch):
+        f, z0 = ps[4 + ch], 192 * ch
+        tt(T.ZZ[:, z0 + 128:z0 + 192], f[:, 128:192], T.ZZ[:, z0 + 64:z0 + 128], A.max, ["Z%d_1" % ch],
+           ["Z%d_2" % ch], [4 + ch])
+        if ch == 1:
+            ts(T.INV[:], T.TT[:], f[:, 192:193], float(HALF), A.is_ge, A.mult, ["TT"], ["INV"], [5])
+        t1(T.UP[:, 64 * ch:64 * ch + 64], T.ZZ[:, z0 + 128:z0 + 192], 16.0, A.add, ["Z%d_2" % ch], ["UP%d" % ch])
+
+    def lay(ch):
+        if ch == 0:
+            for r in range(2):
+                act(T.D[:, r:1024:2], ps[6][:, 0:512], c2[:, 4 + r:5 + r], ["o2"], ["D0_%d" % r], [6])
+        else:
+            for r in range(4):
+                t1(T.D[:, 1024 + r:2048:4], ps[7][:, 0:256], col[:, 28 + r:29 + r], A.mult, ["or"], ["D1_%d" % r], [7])
+
+    def scatter(ch):
+        rk = ["UP%d" % ch] + num("D%d_" % ch, range(4)) + num("Wz%d_" % ch, range(2))
+        if ch == 0:
+            op("S", lambda: S.activation(T.W2[:, :].indirect(T.UP[:, 0:64]), T.D[:, 0:1024], AF.Silu), rk, ["W2"])
+        else:
+            cp(T.W[:, :].indirect(T.UP[:, 64:128]), T.D[:, 1024:2048], rk, ["W"])
+
+    def conv(k):
+        lo, hi = (16 + 512 * k if k else 0), 528 + 512 * k
+        if k % 2:
+            act(T.W16[:, lo:hi], T.W[:, lo:hi], 1.0, ["W", "Wz1_0", "Wz1_1"], ["W16_%d" % k])
+        else:
+            cp(T.W16[:, lo:hi], T.W[:, lo:hi], ["W", "Wz1_0", "Wz1_1"], ["W16_%d" % k])
+
+    def back(ch, first):
+        o = 16 + 1024 * ch
+        win, wt = (T.X16, T.WC) if first else (T.W16, T.WB)
+        if first:
+            lo = o if ch else 0
+            act(T.X16[:, lo:o + 1024], T.W2[:, lo:o + 1024], 1.0, ["W2", "Wz0_0", "Wz0_1"], ["X16_%d" % ch])
+            rk = num("X16_", range(ch + 1)) + ["WC0", "WC4", "WC5", "INV", "I16"]
+        else:
+            rk = num("W16_", range(max(2 * ch - 1, 0), 2 * ch + 2)) + num("WB", range(6))
+        for j, b, c in ((1, 2, 448), (0, 0, 64)):
+            out = ps[b + ch][:, c:c + 64]
+            x = [(out, wt[:, 144 * (4 + j) + 15 - i:144 * (4 + j) + 143 - i], win[:, o + i:o + 1024:16])
+                 for i in range(15)]
+            x.append((out, wt[:, 144 * j:144 * j + 128], win[:, o + 15:o + 1024:16]))
+            x.append((out, wt[:, 144 * (j + 2) + 15:144 * (j + 2) + 143], win[:, o - 1:o + 1023:16]))
+            if first:
+                x.append((out, T.I16[:], T.INV[:, 64 * ch:64 * ch + 64]))
+            mm([x], rk, b + ch, first, not first)
+
+    F0 = OPT["first"]
+
+    def gather0(scale, out, key, both=True):
+        gb(0, 0, F0, scale); gb(0, F0, 32, scale); gb(0, 32, 64, scale)
+        ua(0)
+        ga(0, 0, F0, out, key)
+        if both:
+            ub(1)
+            gb(1, 0, 32, scale); gb(1, 32, 64, scale)
+        ga(0, F0, 32, out, key); ga(0, 32, 64, out, key)
+        if both:
+            ua(1)
+
+    def reopen(rnd, scale, out, key):
+        for k in range(4):
+            conv(k)
+        if rnd < 5:
+            zero_w(0); zero_w(1)
+        back(0, False); back(1, False)
+        ub(0)
+        gather0(scale, out, key)
+
+    def both_chunks(rnd, ks):
+        decide(0, 64, 0, ((0, 32), (32, 64)), a=lambda: ga(1, 0, 32), c=lambda: ga(1, 32, 64))
+        lists(0, 64)
+        meta(1, 64, ((0,), (1, 2)))
+        if rnd == 3:
+            kids(3, 0, 0)
+            kids_s(0, 3, 1, 32)
+        ul(0, 64, 0)
+        kids(*ks[0])
+        decide(1, 64, 1, ((0, 32), (32, 64)), c=lambda: kids(*ks[1]), begun=True)
+        lists(1, 64); cands(0); cands(1)
+        if rnd == 3:
+            fails(3, 64, [ps[7][:, 256:384:2], ps[7][:, 257:384:2]], 7, T.F12[:, 0:64], ["F1"])
+            act(T.F12[:, 64:192], ps[7][:, 256:384], 1.0, [], ["F2"], [7])
+        kids(*ks[2])
+        ul(1, 64, 1)
+        for x in ks[3:]:
+            kids(*x)
+        fails_full(0, rnd, (0, 1))
+        if OPT["spath"]:
+            kids_s(0, 1, 0, 0)
+        else:
+            kids(1, 0, 0)
+        kids(1, 0, 32)
+        post_a(0, rnd); lay(0)
+        kids(1, 1, 0)
+        post_b(0)
+        scatter(0)
+        fails_full(1, rnd, (0,))
+        kids(1, 1, 32)
+        fails_full(1, rnd, (1,))
+        post_a(1, rnd); post_b(1); lay(1)
+        scatter(1)
+        back(0, True); back(1, True)
+
+    act(T.MB[:, 0:512], T.TA[:, :].indirect(T.UAB[:, 0:32]), -1.0, TAK + ["UA0"], keys("MB0", 0, 32))
+    tt(T.MD[:, 0:512], T.TB[:, :].indirect(T.UAB[:, 64:96]), T.MB[:, 0:512], A.add,
+       TBK + ["UB0"] + keys("MB0", 0, 32), keys("MD0", 0, 32))
+    decide(0, 32, 2, (), T.WN, ["WN"], consts_a, consts_b, consts_c)
+    grow(32, 0, 0)
+    consts_d()
+    ub(0); lists(0, 32)
+    gather0(-1.0, T.MD, "MD", False)
+    ul(0, 32, 2)
+    fixed(2, 32, 0, 32)
+    decide(0, 64, 3, (), a=consts_e, b=lambda: kids(2, 0, 0, 32), c=lambda: kids(2, 1, 0, 32))
+    grow(64, 0, 0)
+    ub(0); grow(64, 32, 1); lists(0, 64)
+    fails(2, 32, [ps[7][:, 256:320:2], ps[7][:, 257:320:2]], 7, None, [])
+    gather0(-1.0, T.MD, "MD")
+    ul(0, 64, 3)
+    need("G", ["UL3"])
+    zero_w(0); zero_w(1)
+    fixed(3, 64, 0, 32); fixed(3, 64, 32, 64)
+    act(T.F12[:, 0:64], ps[7][:, 256:320], 1.0, [], ["F1"], [7])
+    K0 = [(0, 0, 0), (0, 1, 0), (0, 0, 32), (0, 1, 32)]
+    both_chunks(3, [(3, 1, 0), (3, 0, 32)] + K0)
+    act(T.FSZU[:], x0, 256.0, ["t0"], ["FSZU"])
+    for rnd in (4, 5):
+        reopen(rnd - 1, -1.0, T.MD, "MD")
+        both_chunks(rnd, K0)
+    row(T.TA, 4, T.SZU[:], ["SZU"], "TAr4")
+    row(T.TB, 4, T.FSZU[:], ["FSZU"], "TBr4")
+    row(T.TA, 6, T.IDN[:], ["IDN"], "TAr0")
+    row(T.TB, 7, T.IDN[:], ["IDN"], "TBr2")
+    t1(T.TA[:, M:M + 1], col[:, 14:15], -1.0, A.mult, ["oh"], ["TAd"])
+    t1(T.TB[:, M:M + 1], col[:, 15:16], -1.0, A.mult, ["oh"], ["TBd"])
+
+    def put(ch, qs):
+        for e, y, r in zip(qs, (T.ya, T.yb, T.ys), (6, 7, 4)):
+            dma(e, y[:, 1024 * ch:1024 * (ch + 1)], T.OUT[r::16, 1024 * ch:1024 * (ch + 1)],
+                keys("OUT%d" % ch, 0, 64), [])
+    reopen(5, 1.0, T.OUT, "OUT")
+    put(0, "YYY")
+    ga(1, 0, 32, T.OUT, "OUT"); ga(1, 32, 64, T.OUT, "OUT")
+    put(1, "YSG")
+    ends["sent"] = sent[0]
+    for s, v in ends.items():
+        g.wait_ge(T.sem[s], v)

@@ -5,32 +5,42 @@ SO = 4112
 HALF = 2048
 COL = HALF + 0.25
 PEN = 16384.0
-BIG = 16384.0
-OPT = {"route": "abxx", "order": "k012s3", "first": 8, "spath": 1}
+BIG = 16.0
+LIFT = 4096.0
+MAGIC = 1.5 * 2.0 ** 27
+SC = 2.0 ** -13
+OPT = {"route": "axbd", "order": "k01s23"}
 NDMA = 48
 
 
 def _sb(n, dt):
-    return ("sbuf", [128, n], dt)
+    return ("sbuf", [128] + (n if isinstance(n, list) else [n]), dt)
 
 
 SCRATCH = {}
 for _dt, _list in (
-        ("bfloat16", dict(H=2 * SO, relay=4096, Z=1032, WF=144, WS=144, IB=128, BM=128, LT=128, UGE=128, UGT=128,
-                          NF=3584, FL=7168, KB=1024, S=144, F12=192)),
-        ("float16", dict(W16=2064, X16=2064, CK16=512, FK16=512, WM=720, WN=720, WB=864, WC=864, WT=640, WU=1280,
-                         E=320, I16=128, ISO=128, MD=2048, P=1024, Q=768, INV=128)),
-        ("float32", dict(TA=SO, TB=SO, W=6288, W2=6288, CK=768, FK=768, tmpk=768, SZ=256, FSZ=256, SZU=256,
-                         FSZU=256, IDN=256, IDR=256, J=160, JG=128, CD=128, TT=128, col=64, col2=32, MB=2048,
-                         OUT=2048, K=512, ZZ=384, D=2048)),
-        ("int32", dict(kli=256, kri=256, sai=64, pci=8)),
-        ("uint16", dict(UAB=256, UL=768, UP=128))):
+        ("bfloat16", dict(H=2 * SO, relay=SO, Z=1312, IB=128, SF=8, SZ=8, NF=3584, FL=7168, F1=64, F2=[16, 8],
+                          S2=512, ONE=512, CODE=128, J=160, J2=128, J4=128, JT=64)),
+        ("float16", dict(W16=2064, MA=2048, MB=2048, I16=128, I8=128, R2=128, R2S=128, R4=128, R4S=128, R4W=128,
+                         LT=128, ON=128, IP=128, IN=128, SA=32, SB=32, OA=128, OB=128, BK=2 * 908, M4=128, M16=128,
+                         CDS=32, C25=32, ZERO=512, PQ=[163, 8], PC0=[81, 16], PC1=[81, 16], ZQ=[128, 8], ZP=[35, 4],
+                         GQ=[65, 8], GC=512,
+                         K=128, C4=128, C16=256, MR=512, E=32, Ua=512, Ub=512, La=512, Lb=512, Na=512, Nb=512,
+                         Sa=256, Sb=256, Ca=1024, Cb=1024, Za=[136, 16], Zb=[136, 16])),
+        ("float32", dict(TA=4104, TB=4104, W=5152, IDR=256, IDT=256, CD=32, col=64, ZC=516, D=1024, OUT=2048,
+                         st=64)),
+        ("int32", dict(ki=512, sai=64, pci=8)),
+        ("uint16", dict(UAB=256, UL=768, UP=64))):
     for _k, _n in _list.items():
         SCRATCH[_k] = _sb(_n, _dt)
 for _b in range(8):
     SCRATCH["ps%d" % _b] = ("psum", [128, 512], "float32")
 SEMAPHORES = (["cV", "cS", "cP", "cG", "sent", "rk", "rs", "hout"] + ["rh%d" % k for k in range(4)]
               + ["hi%d" % k for k in range(4)] + ["d%d" % i for i in range(NDMA)])
+
+
+def quarter(k):
+    return slice(1024 * k, 1024 * (k + 1) if k < 3 else SO)
 
 
 def routes(src, dst, T, topo):
@@ -52,11 +62,11 @@ def helper_program(g, core, T, topo):
         src, dst = T.cores[r], T.cores[(r - 1) % n]
         for k, h in enumerate(routes(src, dst, T, topo)):
             if h == core:
+                q = quarter(k)
                 g.wait_ge(T.sem["hi%d" % k], bits(topo.mask(src, core)))
                 rid, pid, _ = topo.addr(dst)
                 m = topo.mask(core, dst)
-                g.remote_dma(T.H[:, SO + 1024 * k:SO + 1024 * (k + 1)], T.relay[:, 1024 * k:1024 * (k + 1)],
-                             T.sem["rh%d" % k], T.sem.hout, pid, rid, m)
+                g.remote_dma(T.H[:, SO + q.start:SO + q.stop], T.relay[:, q], T.sem["rh%d" % k], T.sem.hout, pid, rid, m)
                 out += bits(m)
     if out:
         g.wait_ge(T.sem.hout, out)
@@ -80,7 +90,7 @@ def rank_program(g, core, T, topo):
     def need(e, reads, writes=(), banks=()):
         ev = []
         for k in reads:
-            ev += wr.get(k, [])
+            ev += wr[k]
         for k in writes:
             ev += wr.get(k, []) + rd.get(k, [])
         for b in banks:
@@ -111,7 +121,7 @@ def rank_program(g, core, T, topo):
 
     def mm(groups, reads, b, opens=True, closes=True):
         need("P", reads, [], [b])
-        for grp in groups:
+        for i, grp in enumerate(groups):
             for j, (o, l, r) in enumerate(grp):
                 last = g.tensor.matmul(o, l, r, opens and j == 0, closes and j == len(grp) - 1)
         cnt["P"] += 1
@@ -136,22 +146,31 @@ def rank_program(g, core, T, topo):
         ends[sem] = wr[key][0][1]
 
     def ts(out, in0, s1, s2, o0, o1, reads, writes, banks=()):
-        if s2 is None:
-            op("V", lambda: V.tensor_scalar(out, in0, s1, None, o0), reads, writes, banks)
-        else:
-            op("V", lambda: V.tensor_scalar(out, in0, s1, s2, o0, o1), reads, writes, banks)
+        op("V", lambda: V.tensor_scalar(out, in0, s1, s2, o0, o1), reads, writes, banks)
 
     def t1(out, in0, s1, o0, reads, writes, banks=()):
-        ts(out, in0, s1, None, o0, None, reads, writes, banks)
+        op("V", lambda: V.tensor_scalar(out, in0, s1, None, o0), reads, writes, banks)
 
     def tt(out, in0, in1, o, reads, writes, banks=()):
         op("V", lambda: V.tensor_tensor(out, in0, in1, o), reads, writes, banks)
 
-    def cp(out, in_, reads, writes):
-        op("V", lambda: V.tensor_copy(out, in_), reads, writes)
+    def cp(out, in_, reads, writes, banks=()):
+        op("V", lambda: V.tensor_copy(out, in_), reads, writes, banks)
 
     def act(out, in_, scale, reads, writes, banks=()):
         op("S", lambda: S.activation(out, in_, AF.Copy, scale=scale), reads, writes, banks)
+
+    def add(e, out, in_, c, reads, writes, banks=()):
+        if e == "V":
+            t1(out, in_, c, A.add, reads, writes, banks)
+        else:
+            op("S", lambda: S.activation(out, in_, AF.Identity, bias=bias[c]), reads + ["bias"], writes, banks)
+
+    def move(e, out, in_, reads, writes, banks=()):
+        if e == "V":
+            cp(out, in_, reads, writes, banks)
+        else:
+            act(out, in_, 1.0, reads, writes, banks)
 
     def fill(out, c, key):
         op("V", lambda: V.memset(out, c), [], [key])
@@ -162,14 +181,18 @@ def rank_program(g, core, T, topo):
     def num(name, js):
         return [name + str(j) for j in js]
 
-    arrives("FK16", "rk", src)
-    arrives("FSZ", "rs", src)
+    def clear(b, w=448):
+        mm([[(ps[b][:, 0:w], T.ZERO[:, 0:128], T.ZERO[:, 0:w])]], ["ZERO"], b, True, False)
+
+    arrives("Ub", "rk", src)
+    arrives("Cb2", "rs", src)
+    wr["Cb3"] = wr["Cb2"]
     for k, h in enumerate(routes(src, core, T, topo)):
         arrives("Hf%d" % k, "rh%d" % k, src if h is None else h)
-    HALL = num("Ho", range(4)) + num("Hf", range(4)) + ["Hd0", "Hd1"]
+    HALL = num("Ho", range(4)) + num("Hf", range(4)) + ["Hd"]
 
-    dma("S", T.kli[:], T.kl[:], [], ["kli"])
-    dma("Y", T.kri[:], T.kr[:], [], ["kri"])
+    dma("S", T.ki[:, 0:256], T.kl[:], [], ["kl"])
+    dma("Y", T.ki[:, 256:512], T.kr[:], [], ["kr"])
     for k in range(4):
         c = slice(1024 * k, 1024 * (k + 1))
         if rank % 2 == 0:
@@ -182,434 +205,494 @@ def rank_program(g, core, T, topo):
     dma("S", T.sai[:, 32:64], T.sb[:], [], ["sb"])
 
     op("G", lambda: g.iota(T.pci[:, 0:1], [[1, 1]], 0, 1), [], ["pci0"])
-    for t, pat, base, mult, key in ((T.IDR, [[1, 256]], 0, 256, "IDR"), (T.J, [[1, 160]], 0, 0, "J"),
-                                    (T.JG, [[1, 8], [0, 16]], 0, 0, "JG"), (T.CD, [[16, 128]], M, 1, "CD")):
-        op("G", lambda: g.iota(t[:], pat, base, mult, allow_small_or_imprecise_dtypes=True), [], [key])
-    fill(T.Z[:], 0.0, "Z")
-    for t, key in ((T.TA, "TA"), (T.TB, "TB")):
-        for k in range(4):
-            act(t[:, 1028 * k:1028 * (k + 1)], T.Z[:, 0:1028], 1.0, ["Z"], [key + str(k)])
-    TAZ, TBZ = num("TA", range(4)), num("TB", range(4))
-    col, c2, pci, J = T.col, T.col2, T.pci, T.J
+    for t, pat, base, mult, key in (
+            (T.J[:], [[1, 160]], 0, 0, "J"), (T.IDR[:], [[1, 256]], -HALF, 256, "IDR"),
+            (T.IDT[:], [[128, 2], [0, 8], [256, 16]], -HALF, 1, "IDT"),
+            (T.JT[:, 0:32], [[1, 4], [16, 8]], 0, 0, "JA"), (T.JT[:, 32:64], [[-1, 4], [16, 8]], 3, 0, "JB"),
+            (T.J2[:], [[1, 2], [2, 64]], 0, 0, "J2"), (T.J4[:], [[1, 4], [4, 32]], 0, 0, "J4"),
+            (T.CD[:], [[0, 8], [2, 4]], HALF + 16, 8, "CD")):
+        op("G", lambda: g.iota(t, pat, base, mult, allow_small_or_imprecise_dtypes=True), [], [key])
+    fill(T.ZERO[:], 0.0, "ZERO")
+    clear(6, 512); clear(7, 256)
+    col, pci, J = T.col, T.pci, T.J
     SH, AND = A.arith_shift_right, A.bitwise_and
-    cp(col[:, 0:1], pci[:, 0:1], ["pci0"], ["c_p"])
+    bias = {}
+    for j, c in enumerate((COL, COL + 16, LIFT, -LIFT)):
+        bias[c] = col[:, 56 + j:57 + j]
+        fill(bias[c], c, "bias%d" % j)
     t1(pci[:, 1:2], pci[:, 0:1], 15, AND, ["pci0"], ["pci1"])
     t1(pci[:, 2:3], pci[:, 0:1], 4, SH, ["pci0"], ["pci2"])
-    ts(pci[:, 3:4], pci[:, 0:1], 2, 3, SH, AND, ["pci0"], ["pci3"])
-    t1(pci[:, 4:5], pci[:, 0:1], 3, AND, ["pci0"], ["pci4"])
-    ts(pci[:, 5:6], pci[:, 0:1], 1, 7, SH, AND, ["pci0"], ["pci5"])
-    t1(pci[:, 6:7], pci[:, 0:1], 1, AND, ["pci0"], ["pci6"])
-    t1(pci[:, 7:8], pci[:, 0:1], 2, AND, ["pci0"], ["pci7"])
-    cp(col[:, 1:5], pci[:, 1:5], num("pci", range(1, 5)), ["c_4"])
-    cp(c2[:, 0:3], pci[:, 5:8], num("pci", range(5, 8)), ["c2a"])
-    c_p, c_pm, c_g, c_q, c_r, c_g15, c_gm = (col[:, j:j + 1] for j in range(7))
-    ts(c_g15, c_g, 16.0, 15.0, A.mult, A.add, ["c_4"], ["c_g15"])
-    t1(c_gm, c_g, -float(M), A.mult, ["c_4"], ["c_gm"])
-    t1(c2[:, 3:4], c_p, 14.0, A.add, ["c_p"], ["c2b"])
-    t1(col[:, 40:41], c_p, 13.0, A.add, ["c_p"], ["c_p13"])
-    t1(T.IDN[:], T.IDR[:], c_gm, A.add, ["IDR", "c_gm"], ["IDN"])
-    ts(T.WS[:], J[:, 0:144], c_g15, 1.0 / 256, A.is_equal, A.mult, ["J", "c_g15"], ["WS"])
-    t1(col[:, 8:24], J[:, 0:16], c_pm, A.is_equal, ["J", "c_4"], ["oh"])
-    t1(col[:, 24:28], J[:, 0:4], c_q, A.is_equal, ["J", "c_4"], ["oq"])
-    t1(col[:, 28:32], J[:, 0:4], c_r, A.is_equal, ["J", "c_4"], ["or"])
-    t1(col[:, 7:8], c_g15, 1.0, A.add, ["c_g15"], ["c_g16"])
-    lf, x0, x1, x2 = T.CK[:, 512:768], T.tmpk[:, 0:256], T.tmpk[:, 256:512], T.tmpk[:, 512:768]
-    t1(x0, T.kli[:], 0.0, A.is_equal, ["kli"], ["t0"])
-    t1(x1, T.kli[:], -float(HALF), A.add, ["kli"], ["t1"])
-    ts(x2, x0, float(M), -float(HALF), A.mult, A.add, ["t0"], ["t2"])
-    t1(lf, x0, -PEN, A.mult, ["t0"], ["lf"])
-    tt(x0, x0, T.IDN[:], A.mult, ["t0", "IDN"], ["t0"])
-    tt(T.CK[:, 256:512], x2, T.kri[:], A.add, ["t2", "kri"], ["CKr"])
-    tt(T.CK[:, 0:256], x0, x1, A.add, ["t0", "t1"], ["CKl"])
-    cp(T.CK16[:], T.CK[:, 0:512], ["CKl", "CKr"], ["CK16"])
-    for j, r in enumerate((4, 0, 1, 2, 3)):
-        ts(T.WM[:, 144 * j:144 * (j + 1)], J[:, 0:144], c_g15, col[:, 8 + r:9 + r], A.is_equal, A.mult,
-           ["J", "c_g15", "oh"], ["WM%d" % j])
+    t1(pci[:, 3:4], pci[:, 0:1], 3, AND, ["pci0"], ["pci3"])
+    ts(pci[:, 4:5], pci[:, 0:1], 3, 1, SH, AND, ["pci0"], ["pci4"])
+    fill(T.Z[:], 0.0, "Z")
+    cp(col[:, 0:5], pci[:, 0:5], num("pci", range(5)) + num("bias", range(4)), ["c_p", "bias"])
+    c_p, c_pm, c_g, c_r, c_v, c_g15, c_gm, c_pp = (col[:, j:j + 1] for j in range(8))
+    oh = [col[:, 8 + j:9 + j] for j in range(16)]
+    fill(T.H[:, M:SO], -262144.0, "Hpad")
+    t1(c_gm, c_g, -float(M), A.mult, ["c_p"], ["c_gm"])
+    t1(col[:, 8:24], J[:, 0:16], c_pm, A.is_equal, ["J", "c_p"], ["oh"])
+    t1(T.I16[:], J[:, 0:128], c_p, A.is_equal, ["J", "c_p"], ["I16"])
+    ts(T.SZ[:], J[:, 0:8], c_g, 1.0 / 256, A.is_equal, A.mult, ["J", "c_p"], ["SZ"])
+    ts(T.I8[:], J[:, 0:128], c_p, -PEN / HALF, A.is_equal, A.mult, ["J", "c_p"], ["I8"])
+    ts(ps[5][:, 0:256], T.IDR[:], c_gm, 1.0 / HALF, A.add, A.mult, ["IDR", "c_gm"], ["own"], [5])
+    for t, w in ((T.PQ, 1304), (T.PC0, 656), (T.PC1, 656)):
+        act(t[:] if t is T.PQ else t[:, 0::2, :], T.Z[:, 0:w], 1.0, ["Z"], [t.name + "z"])
+    act(T.GQ[:, 0::2, :], T.Z[:, 0:264], 1.0, ["Z"], ["GQz"])
+    for z in (T.Za, T.Zb):
+        fill(z[:, 5::8, :], float(HALF), z.name + "5")
+        fill(z[:, 7::8, :], 0.0, z.name + "7")
+        fill(z[:, 128:133, :], 0.0, z.name + "p")
+        fill(z[:, 134:135, :], 0.0, z.name + "q")
+    tt(ps[5][:, 0:1], ps[5][:, 0:1], oh[8], A.add, ["own", "oh"], ["own"], [5])
 
-    need("P", ["WS"])
-    for i in range(16):
-        need("P", ["Ho%d" % (i // 4)])
-        last = g.tensor.matmul(ps[7][:, 0:256], T.WS[:, 15 - i:143 - i], T.H[:, 256 * i:256 * (i + 1)], i == 0, i == 15)
-    cnt["P"] += 1
-    last.then_inc(T.sem.cP, 1)
-    done("P", ("cP", cnt["P"]), [], [], [7])
-    tt(T.SZ[:], ps[7][:, 0:256], lf, A.add, ["lf"], ["SZ"], [7])
-    act(T.SZU[:], ps[7][:, 0:256], 256.0, [], ["SZU"], [7])
+    def kids(x):
+        U, L, N, Sf = T["U" + x], T["L" + x], T["N" + x], T["S" + x]
+
+        def over(t, key, sides, closes):
+            mm([[(ps[6][:, 256 * s + 128 * h:256 * s + 128 * h + 128], t[:, 256 * s + 128 * h:256 * s + 128 * h + 128],
+                  T.I16[:]) for s in sides for h in range(2)]], [key, "I16"], 6, False, closes)
+        over(U, "U" + x, (0, 1), False)
+        ts(L[:], U[:], -float(HALF), float(HALF), A.is_equal, A.mult, ["U" + x], ["L" + x])
+        ts(N[:], U[:], 0.0, float(HALF), A.is_equal, A.mult, ["U" + x], ["N" + x])
+        tt(Sf[:], ps[5][:, 0:256], L[:, 0:256], A.mult, ["own", "L" + x], ["S" + x], [5])
+        over(L, "L" + x, (0, 1), False); over(N, "N" + x, (0, 1), False); over(Sf, "S" + x, (0,), True)
+        act(T["C" + x][:, 0:512], ps[6][:, 0:512], 1.0, [], ["C%s0" % x, "C%s1" % x], [6])
+
+    def zrow(x, r, h):
+        return T["Z" + x][:, 8 * h + r:128:16, :]
+
+    def spread(e, x, j):
+        for h in range(2):
+            move(e, zrow(x, j + 1, h), T["C" + x][:, 256 * j + 128 * h:256 * j + 128 * h + 128], ["C%s%d" % (x, j)],
+                 ["Z%s%d_%d" % (x, j + 1, h)])
+
+    def pen(x):
+        for h in range(2):
+            ts(zrow(x, 6, h), T["C" + x][:, 256 + 128 * h:384 + 128 * h], 0.0, -PEN, A.is_equal, A.mult, ["C%s1" % x],
+               ["Z%s6_%d" % (x, h)])
+
+    TAB = {"a": T.TA, "b": T.TB}
+
+    def table(x, banks, es, qs=range(8)):
+        z, t = T["Z" + x], TAB[x]
+        rk = ["Z%s%d_%d" % (x, r, h) for r in (0, 1, 2, 3, 4, 6) for h in range(2)] + num(z.name, "57pq") + ["I16"]
+        for q in qs:
+            mm([[(ps[banks[q]][:, 128 * j:128 * (j + 1)], z[:, 8 * (j % 2):8 * (j % 2) + 128, 2 * q + j // 2], T.I16[:])]
+                for j in range(4)], rk, banks[q])
+            move(es[q], t[:, 512 * q:512 * (q + 1)], ps[banks[q]][:, 0:512], [], ["T%s%d" % (x, q)], [banks[q]])
+            if q == 5:
+                t1(t[:, M:M + 1], t[:, HALF:HALF + 1], col[:, 25:26], A.add, ["T%s4" % x, "fix"], ["T%sd" % x])
+                t1(t[:, HALF:HALF + 1], oh[5], -1.0, A.mult, ["oh"], ["T%s4" % x])
+    TK = {x: num("T" + x, range(8)) + ["T%sd" % x] for x in "ab"}
+
+    def sizes(k):
+        mm([[(ps[7][:, 128 * h + i:128 * h + 128:16], T.H[:, 256 * i + 128 * h:256 * i + 128 * h + 128], T.SZ[:])
+             for i in range(4 * k, 4 * k + 4) for h in range(2)]], ["SZ", "Ho%d" % k], 7, False, k == 3)
+
+    t1(T.Ua[:], T.ki[:], -float(HALF), A.add, ["kl", "kr"], ["Ua"])
+    for x in "ab":
+        for h in range(2):
+            act(zrow(x, 0, h), T.IDT[:, 128 * h:128 * h + 128], 1.0, ["IDT"], ["Z%s0_%d" % (x, h)])
+    kids("a")
+    clear(6, 512)
+    sizes(0)
+    mm([[(ps[7][:, 128 * h:128 * h + 128], T.La[:, 128 * h:128 * h + 128], T.I8[:]) for h in range(2)]], ["La", "I8"], 7,
+       False, False)
+    sizes(1)
+    ts(T.st[:], T.sai[:], float(HALF), float(HALF), A.is_equal, A.mult, ["sa", "sb"], ["st"])
+    tt(c_pp, c_p, oh[4], A.subtract, ["c_p", "oh"], ["c_pp"])
+    ts(col[:, 24:25], c_pm, 2.5, -2.0, A.is_gt, A.mult, ["c_p"], ["sg"])
+    tt(col[:, 25:26], oh[0], oh[5], A.subtract, ["oh"], ["fix"])
+    tt(T.st[:], T.st[:], T.sai[:], A.add, ["st"], ["st"])
+    t1(col[:, 24:25], col[:, 24:25], 1.0, A.add, ["sg"], ["sg"])
+    t1(col[:, 25:26], col[:, 25:26], float(HALF), A.mult, ["fix"], ["fix"])
+    t1(T.SA[:], T.JT[:, 0:32], c_pp, A.is_equal, ["JA", "c_pp"], ["SA"])
+    cp(T.UAB[:, 0:32], T.st[:, 0:32], ["st"], ["Ua0"])
+    cp(T.UAB[:, 128:160], T.st[:, 32:64], ["st"], ["Ub0"])
+    ts(T.SB[:], T.JT[:, 32:64], c_pp, col[:, 24:25], A.is_equal, A.mult, ["JB", "c_pp", "sg"], ["SB"])
+    spread("S", "a", 0); spread("S", "a", 1)
+    op("S", lambda: S.activation(T.ZC[:], T.Z[:, 0:516], AF.Silu, bias=bias[LIFT]), ["Z", "bias"], ["ZC"])
+    pen("a")
+    sizes(2)
+    cp(T.H[:, M:M + 1], T.H[:, HALF:HALF + 1], ["Ho2", "Hpad"], ["Hd"])
+    for t, j, w in ((T.R2, T.J2, 1.0), (T.R2S, T.J2, SO), (T.R4, T.J4, 1.0), (T.R4S, T.J4, SO), (T.R4W, T.J4, 1 / SC)):
+        ts(t[:], j[:], c_p, float(w), A.is_equal, A.mult, [j.name, "c_p"], [t.name])
+    fill(T.H[:, HALF:HALF + 1], -262144.0, "Ho2")
+    sizes(3)
+    ts(T.Ca[:, 512:768], ps[7][:, 0:256], MAGIC, -MAGIC, A.add, A.add, [], ["Ca2"], [7])
+    ts(T.SF[:], J[:, 0:8], c_g, BIG, A.is_equal, A.mult, ["J", "c_p"], ["SF"])
+    t1(T.IB[:], J[:, 0:128], c_p, A.is_equal, ["J", "c_p"], ["IB"])
+    tt(T.Ca[:, 768:1024], ps[7][:, 0:256], T.Ca[:, 512:768], A.subtract, ["Ca2"], ["Ca3"], [7])
     rt = routes(core, dst, T, topo)
     for x in OPT["order"]:
         if x == "k":
-            send(dst, T.FK16[:], T.CK16[:], "rk", ["CK16"])
+            send(dst, T.Ub[:], T.Ua[:], "rk", ["Ua"])
         elif x == "s":
-            send(dst, T.FSZ[:], T.SZ[:], "rs", ["SZ"])
+            send(dst, T.Cb[:, 512:1024], T.Ca[:, 512:1024], "rs", ["Ca2", "Ca3"])
         else:
-            k = int(x)
-            c = slice(1024 * k, 1024 * (k + 1))
-            if rt[k] is None:
-                send(dst, T.H[:, SO + 1024 * k:SO + 1024 * (k + 1)], T.H[:, c], "rh" + x, ["Ho" + x])
+            q = quarter(int(x))
+            rk = ["Ho" + x] + (["Hd"] if x == "3" else [])
+            if rt[int(x)] is None:
+                send(dst, T.H[:, SO + q.start:SO + q.stop], T.H[:, q], "rh" + x, rk)
             else:
-                send(rt[k], T.relay[:, c], T.H[:, c], "hi" + x, ["Ho" + x])
+                send(rt[int(x)], T.relay[:, q], T.H[:, q], "hi" + x, rk)
+    spread("S", "a", 2); spread("V", "a", 3)
 
-    def row(tab, r, tile, reads, key, zero=()):
-        need("Y", zero)
-        dma("Y", tab[r::16, 0:M], tile, reads, [key])
-    row(T.TA, 0, T.CK[:, 0:256], ["CKl"], "TAr0", TAZ)
-    row(T.TA, 1, T.CK[:, 256:512], ["CKr"], "TAr1")
-    row(T.TA, 4, T.SZ[:], ["SZ"], "TAr4")
-    t1(T.I16[:], J[:, 0:128], c_p, A.is_equal, ["J", "c_p"], ["I16"])
-    ts(T.ISO[:], J[:, 0:128], c_p, float(SO), A.is_equal, A.mult, ["J", "c_p"], ["ISO"])
-    t1(T.WN[:], T.WM[:], -1.0, A.mult, num("WM", range(5)), ["WN"])
-    cp(T.UAB[:, 0:32], T.sai[:, 0:32], ["sa"], ["UA0"])
-    cp(T.UAB[:, 64:96], T.sai[:, 32:64], ["sb"], ["UB0"])
-    t1(ps[0][:, 64:96], T.sai[:, 0:32], -float(HALF), A.add, ["sa"], ["v0"], [0])
-    t1(ps[2][:, 448:480], T.sai[:, 32:64], -float(HALF), A.add, ["sb"], ["v1"], [2])
-    t1(col[:, 42:43], col[:, 12:13], -2 * PEN, A.mult, ["oh"], ["dd0"])
-    fill(T.H[:, M:SO], -262144.0, "Hd0")
-    fill(T.H[:, SO + M:2 * SO], -262144.0, "Hd1")
-    cp(T.TA[:, M:M + 1], col[:, 42:43], ["dd0", "TA3"], ["TAd"])
-    cp(T.TB[:, M:M + 1], col[:, 42:43], ["dd0", "TB3"], ["TBd"])
-    t1(T.FK[:, 0:512], T.FK16[:], -1.0, A.mult, ["FK16"], ["FK"])
-    row(T.TB, 2, T.FK[:, 0:256], ["FK"], "TBr2", TBZ)
-    row(T.TB, 3, T.FK[:, 256:512], ["FK"], "TBr3")
-    row(T.TB, 4, T.FSZ[:], ["FSZ"], "TBr4")
-    ts(T.FK[:, 512:768], T.FK16[:, 256:512], float(HALF), -PEN, A.is_equal, A.mult, ["FK16"], ["FKl"])
-    TAK = TAZ + ["TAr0", "TAr1", "TAr4", "TAd"]
-    TBK = TBZ + ["TBr2", "TBr3", "TBr4", "TBd"]
-    ts(T.WF[:], J[:, 0:144], c_g15, BIG, A.is_equal, A.mult, ["J", "c_g15"], ["WF"])
-    t1(T.IB[:], J[:, 0:128], c_p, A.is_equal, ["J", "c_p"], ["IB"])
-    ts(col[:, 32:36], col[:, 24:28], col[:, 7:8], -1.0, A.mult, A.add, ["oq", "c_g16"], ["cf"])
-    ts(col[:, 36:40], col[:, 24:28], col[:, 40:41], -1.0, A.mult, A.add, ["oq", "c_p13"], ["ck"])
-    t1(T.BM[:], T.JG[:], c_g, A.is_equal, ["JG", "c_4"], ["BM"])
-    t1(T.UGT[:], J[:, 0:128], c_p, A.is_gt, ["J", "c_p"], ["UGT"])
-    for j in range(4):
-        t1(T.WB[:, 144 * j:144 * (j + 1)], J[:, 0:144], col[:, 32 + j:33 + j], A.is_equal, ["J", "cf"], ["WB%d" % j])
-    tt(T.LT[:], T.UGT[:], T.BM[:], A.mult, ["UGT", "BM"], ["LT"])
-    for j in range(2):
-        tt(T.WB[:, 144 * j + 577:144 * j + 720], T.WB[:, 144 * j + 1:144 * j + 144],
-           T.WB[:, 144 * j + 288:144 * j + 431], A.add, num("WB", (j, j + 2)), ["WB%d" % (4 + j)])
-    tt(T.UGE[:], T.BM[:], T.LT[:], A.subtract, ["BM", "LT"], ["UGE"])
+    def counting():
+        ts(T.LT[:], J[:, 0:128], c_p, SC, A.is_gt, A.mult, ["J", "c_p"], ["LT"])
+        fill(T.ON[:], SC, "ON")
+        t1(T.IP[:], T.I16[:], SC, A.mult, ["I16"], ["IP"])
+        t1(T.IN[:], T.I16[:], -SC, A.mult, ["I16"], ["IN"])
+        fill(T.C25[:], -HALF * SC, "C25")
+        t1(T.CDS[:], T.CD[:], SC, A.mult, ["CD"], ["CDS"])
+        for c in (1.0, 0.0):
+            for t, st in ((T.M4, 4), (T.M16, 16)):
+                fill(t[:] if c else t[:, 0:128:st], c, t.name)
+        fill(T.ZQ[:, 3::8, :], 0.0, "ZQz")
+        fill(T.ZP[:], 0.0, "ZPz")
+        fill(T.ONE[:], 1.0, "ONE")
+        op("G", lambda: g.affine_select(T.S2[:], T.ONE[:], [[128, 2], [-1, 2], [1, 128]], A.is_equal, 0.0, 0, -2),
+           ["ONE"], ["S2"])
 
-    def consts_a():
-        tt(x0, T.FSZ[:], T.FK[:, 512:768], A.subtract, ["FSZ", "FKl"], ["t0"])
+    EDGE = (15, 14, 13, -1, -2, -3)
 
-    def consts_b():
-        t1(T.E[:, 0:160], J[:], c2[:, 3:4], A.is_equal, ["J", "c2b"], ["E0"])
-        t1(c2[:, 8:16], J[:, 0:8], c2[:, 0:1], A.is_equal, ["J", "c2a"], ["o8"])
-        ts(c2[:, 6:7], c2[:, 2:3], -1.0, 1.0, A.mult, A.add, ["c2a"], ["sg"])
-        tt(T.E[:, 162:320], T.E[:, 2:160], T.E[:, 0:158], A.subtract, ["E0"], ["E1"])
+    def bk(v, w):
+        if w in EDGE:
+            o = 908 * v + 140 + 128 * EDGE.index(w)
+            return T.BK[:, o:o + 128]
+        return T.BK[:, 908 * v + 12 - w:908 * v + 140 - w]
 
-    def consts_c():
-        for u in range(8):
-            t1(T.WU[:, 160 * u + 2:160 * u + 160], T.E[:, 162:320], c2[:, 8 + u:9 + u], A.mult, ["E1", "o8"],
-               ["WU%d" % u])
+    def aims():
+        ts(c_g15, c_g, 16.0, 17.0, A.mult, A.add, ["c_p"], ["c_g15"])
+        t1(col[:, 28:30], J[:, 0:2], c_v, A.is_equal, ["J", "c_p"], ["ov"])
+        t1(col[:, 32:35], J[:, 0:3], c_r, A.is_ge, ["J", "c_p"], ["mle"])
+        t1(col[:, 35:38], J[:, 1:4], c_r, A.is_le, ["J", "c_p"], ["mge"])
+        tt(col[:, 26:27], c_g15, c_r, A.add, ["c_g15", "c_p"], ["tg0"])
+        ts(col[:, 30:32], col[:, 28:30], col[:, 26:27], -1.0, A.mult, A.add, ["ov", "tg0"], ["tg"])
 
-    def consts_d():
-        t1(T.WC[:, 0:576], T.WB[:, 0:576], c2[:, 6:7], A.mult, ["sg"] + num("WB", range(4)), ["WC0"])
-        for j in (4, 5):
-            t1(T.WC[:, 144 * j + 1:144 * j + 144], T.WB[:, 144 * j + 1:144 * j + 144], c2[:, 6:7], A.mult,
-               ["sg", "WB%d" % j], ["WC%d" % j])
+    def shifting(v):
+        t1(T.BK[:, 908 * v:908 * v + 140], J[:, 4:144], col[:, 30 + v:31 + v], A.is_equal, ["J", "tg"],
+           ["BK%d" % (7 * v)])
+        for j, w in enumerate(EDGE):
+            ts(bk(v, w), J[:, 16 - w:144 - w], col[:, 30 + v:31 + v], col[:, 32 + j:33 + j], A.is_equal, A.mult,
+               ["J", "tg", "mle", "mge"], ["BK%d" % (7 * v + 1 + j)])
+    aims()
 
-    def consts_e():
-        t1(c2[:, 4:6], J[:, 0:2], c2[:, 1:2], A.is_equal, ["J", "c2a"], ["o2"])
-        ts(T.TT[:], T.CD[:], c_g15, 15.0 - M, A.subtract, A.add, ["CD", "c_g15"], ["TT"])
-        tt(T.UGT[:], T.UGE[:], T.IB[:], A.subtract, ["UGE", "IB"], ["UGT"])
-        fill(T.S[:, 0:16], 0.0, "S0")
-    for j in range(4):
-        t1(T.WT[:, 160 * j:160 * (j + 1)], J[:], col[:, 36 + j:37 + j], A.is_equal, ["J", "ck"], ["WT%d" % j])
+    def closing():
+        c = [col[:, 40 + j:41 + j] for j in range(8)]
+        tt(c[0], oh[0], oh[5], A.add, ["oh"], ["z0"])
+        tt(c[1], oh[3], oh[4], A.add, ["oh"], ["z1"])
+        tt(c[2], c[1], oh[6], A.subtract, ["z1"], ["z2"])
+        tt(c[3], c[1], oh[6], A.add, ["z1"], ["z3"])
+        ts(c[4], c[2], 256.0, c[0], A.mult, A.add, ["z2", "z0"], ["z4"])
+        ts(c[5], c[3], 2.0, c_g15, A.mult, A.add, ["z3", "c_g15"], ["z5"])
+        tt(c[6], c[5], c[0], A.add, ["z5", "z0"], ["z6"])
+        ts(T.OA[:], J[:, 17:145], c[5], c[4], A.is_equal, A.mult, ["J", "z5", "z4"], ["OA"])
+        ts(T.OB[:], J[:, 17:145], c[6], c[4], A.is_equal, A.mult, ["J", "z6", "z4"], ["OB"])
 
-    def zero_w(j):
-        for k in range(2):
-            dma("G", (T.W2, T.W)[j][:, 1032 * k:1032 * (k + 1)], T.Z[:], ["Z"], ["Wz%d_%d" % (j, k)])
-
-    def gb(ch, lo, hi, scale=-1.0):
-        o = 1024 * ch
-        act(T.MB[:, o + 16 * lo:o + 16 * hi], T.TB[:, :].indirect(T.UAB[:, 128 * ch + 64 + lo:128 * ch + 64 + hi]),
-            scale, TBK + ["UB%d" % ch], keys("MB%d" % ch, lo, hi))
-
-    def ga(ch, lo, hi, out=T.MD, key="MD"):
-        o = 1024 * ch
-        tt(out[:, o + 16 * lo:o + 16 * hi], T.TA[:, :].indirect(T.UAB[:, 128 * ch + lo:128 * ch + hi]),
-           T.MB[:, o + 16 * lo:o + 16 * hi], A.add, TAK + ["UA%d" % ch] + keys("MB%d" % ch, lo, hi),
-           keys("%s%d" % (key, ch), lo, hi))
-
-    MP = ((0, 0), (4, 0), (4, 64), (6, 0), (6, 64))
-
-    def meta(ch, nc, js, w=T.WM, wk=None):
-        o = 1024 * ch
-        for jj in js:
-            mm([[(ps[MP[j][0] + ch][:, MP[j][1]:MP[j][1] + nc], w[:, 144 * j + 15 - i:144 * j + 143 - i],
-                  T.MD[:, o + i:o + 16 * nc:16]) for i in range(16)] for j in jj],
-               keys("MD%d" % ch, 0, nc) + (wk or num("WM", jj)), MP[jj[0]][0] + ch)
-
-    def pt(ch, nc, j):
-        return T.P[:, 512 * ch + nc * j:512 * ch + nc * (j + 1)]
-
-    def dec(ch, nc, part):
-        k = "P%d_" % ch
-        if part == 0:
-            t1(pt(ch, nc, 6), ps[ch][:, 0:nc], 0.0, A.is_ge, [], [k + "6"], [ch])
-            t1(pt(ch, nc, 7), ps[ch][:, 0:nc], 0.0, A.is_lt, [], [k + "7"], [ch])
-        for j, b, c, m in (((5, 2, 448, 6), (4, 0, 64, 7)), ((0, 4, 0, 6), (1, 4, 64, 6)),
-                           ((2, 6, 0, 7), (3, 6, 64, 7)))[part]:
-            tt(pt(ch, nc, j), ps[b + ch][:, c:c + nc], pt(ch, nc, m), A.mult, [k + str(m), "v0", "v1"],
-               [k + str(j)], [b + ch])
-
-    def lists(ch, nc):
-        mm([[(ps[2 + ch][:, x * nc:(x + 1) * nc], w, pt(ch, nc, j))
-             for w, j in ((T.ISO[:], 7), (T.I16[:], x), (T.I16[:], 2 + x))] for x in range(2)],
-           num("P%d_" % ch, (0, 1, 2, 3, 7)) + ["I16", "ISO"], 2 + ch)
-
-    def decide(ch, nc, slot, fx, w=T.WM, wk=None, a=None, b=None, c=None, begun=False):
-        if not begun:
-            meta(ch, nc, ((0,), (1, 2)), w, wk)
-        if a:
-            a()
-        dec(ch, nc, 0)
-        out = ps[ch][:, 128:128 + nc]
-        mm([[(out, T.I16[:], pt(ch, nc, 4)), (out, T.I16[:], pt(ch, nc, 5)), (out, T.ISO[:], pt(ch, nc, 6))]],
-           num("P%d_" % ch, (4, 5, 6)) + ["I16", "ISO"], ch)
-        meta(ch, nc, ((3, 4),), w, wk)
-        if b:
-            b()
-        dec(ch, nc, 1)
-        t1(T.UL[:, 192 * slot + 2 * nc:192 * slot + 3 * nc], out, COL, A.add, [], ["UF%d" % slot], [ch])
-        for lo, hi in fx:
-            fixed(slot, nc, lo, hi)
-        if c:
-            c()
-        dec(ch, nc, 2)
-
-    CAND = ((0, 4), (2, 5), (1, 4), (3, 5))
-
-    def cands(ch):
-        mm([[(ps[2 + ch][:, 64 * (3 + j):64 * (4 + j)], T.I16[:], pt(ch, 64, x)) for x in CAND[j]] for j in range(4)],
-           num("P%d_" % ch, range(6)) + ["I16"], 2 + ch)
-
-    def grow(nc, lo, to):
-        for b, c, js in ((2, 448, (1, 3)), (0, 64, (0, 2))):
-            mm([[(ps[b + to][:, c + par:c + 64:2], T.I16[:], T.P[:, nc * x + lo:nc * x + lo + 32]) for x in CAND[j]]
-                for par, j in enumerate(js)], num("P0_", range(6)) + ["I16"], b + to)
-
-    def ua(ch):
-        t1(T.UAB[:, 128 * ch:128 * ch + 64], ps[ch][:, 64:128], COL, A.add, [], ["UA%d" % ch], [ch])
-
-    def ub(ch):
-        t1(T.UAB[:, 128 * ch + 64:128 * ch + 128], ps[2 + ch][:, 448:512], COL, A.add, [], ["UB%d" % ch], [2 + ch])
-
-    def ul(ch, nc, slot):
-        t1(T.UL[:, 192 * slot:192 * slot + 2 * nc], ps[2 + ch][:, 0:2 * nc], COL, A.add, [], ["UL%d" % slot], [2 + ch])
-
-    NFO, FLO = (0, 1024, 2048, 2560), (0, 2048, 4096, 5120)
-
-    def fixed(slot, nc, lo, hi):
-        o, u = NFO[slot], 192 * slot + 2 * nc
-        act(T.NF[:, o + 16 * lo:o + 16 * hi], T.H[:, :].indirect(T.UL[:, u + lo:u + hi]), -1.0,
-            HALL + ["UF%d" % slot], keys("NF%d" % slot, lo, hi))
-
-    def kids(slot, side, lo, nc=64):
-        o, u, f = NFO[slot] + 16 * lo, 192 * slot + side * nc + lo, FLO[slot] + 16 * (side * nc + lo)
-        tt(T.FL[:, f:f + 512], T.H[:, :].indirect(T.UL[:, u:u + 32]), T.NF[:, o:o + 512], A.is_lt,
-           HALL + ["UL%d" % slot] + keys("NF%d" % slot, lo, lo + 32), keys("FL%d_%d" % (slot, side), lo, lo + 32))
-
-    def kids_s(j, slot, side, lo):
-        o, u, f = NFO[slot] + 16 * lo, 192 * slot + side * 64 + lo, FLO[slot] + 16 * (side * 64 + lo)
-        kb, out = T.KB[:, 512 * j:512 * (j + 1)], ps[j][:, 0:512]
-        act(kb, T.H[:, :].indirect(T.UL[:, u:u + 32]), -1.0, HALL + ["UL%d" % slot], ["KB%d" % j])
-        mm([[(out, T.IB[:], kb), (out, T.IB[:], T.NF[:, o:o + 512])]],
-           ["KB%d" % j, "IB"] + keys("NF%d" % slot, lo, lo + 32), j)
-        op("S", lambda: S.activation(T.FL[:, f:f + 512], out, AF.Relu), [],
-           keys("FL%d_%d" % (slot, side), lo, lo + 32), [j])
-
-    def fails(slot, nc, outs, b, carry, ckey, sides=(0, 1)):
-        grp = []
-        for side in sides:
-            f = FLO[slot] + side * 16 * nc
-            x = [(outs[side], T.WF[:, 15 - i:143 - i], T.FL[:, f + i:f + 16 * nc:16]) for i in range(16)]
-            grp.append(x + ([(outs[side], T.IB[:], carry)] if ckey else []))
-        mm(grp, [k for x in sides for k in keys("FL%d_%d" % (slot, x), 0, nc)] + ["WF", "IB"] + ckey, b)
-
-    def fails_full(ch, rnd, sides):
-        b = ps[4 + ch]
-        fails(ch, 64, [b[:, 0:64], b[:, 64:128]], 4 + ch, T.F12[:, 64 + 64 * ch:128 + 64 * ch],
-              ["F2"] if rnd == 3 else [], sides)
-
-    def post_a(ch, rnd):
-        f, c = ps[4 + ch], ps[2 + ch]
-        k0, z0, s0, kk = 256 * ch, 192 * ch, 16 + 64 * ch, "K%d_" % ch
-        kL, kR, nL, both = (T.K[:, k0 + 64 * j:k0 + 64 * (j + 1)] for j in range(4))
-        t1(T.K[:, k0:k0 + 128], f[:, 0:128], 0.0, A.is_equal, [], [kk + "0"], [4 + ch])
-        t1(nL, f[:, 0:64], 0.0, A.is_gt, [], [kk + "2"], [4 + ch])
-        tt(T.ZZ[:, z0:z0 + 64], f[:, 0:64], T.CD[:, 64 * ch:64 * ch + 64], A.min, ["CD"], ["Z%d_0" % ch], [4 + ch])
-        op("V", lambda: V.tensor_tensor_scan(T.S[:, s0:s0 + 64], kL, kR, T.S[:, s0 - 1:s0], A.add, A.add),
-           [kk + "0", "S%d" % ch], ["S%d" % (ch + 1)])
-        tt(both, f[:, 64:128], kL, A.is_lt, [kk + "0"], [kk + "3"], [4 + ch])
-        tt(T.ZZ[:, z0 + 64:z0 + 128], f[:, 64:128], T.ZZ[:, z0:z0 + 64], A.min, ["Z%d_0" % ch], ["Z%d_1" % ch],
-           [4 + ch])
-        if rnd == 3:
-            grp = [[(f[:, 128 + u:192:4], T.LT[:], T.S[:, s0 + 3:s0 + 64:4]),
-                    (f[:, 128 + u:192:4], T.UGT[:], T.S[:, s0 - 1:s0 + 63:4]),
-                    (f[:, 128 + u:192:4], T.IB[:], T.S[:, s0 - 1 + u:s0 + 63:4])] for u in range(4)]
-        else:
-            grp = [[(f[:, 128:192], T.LT[:], T.S[:, s0:s0 + 64]), (f[:, 128:192], T.UGE[:], T.S[:, s0 - 1:s0 + 63])]]
-        if ch == 1:
-            grp.append([(f[:, 192:193], T.BM[:], T.S[:, 143:144])])
-        mm(grp, num("S", (ch, ch + 1)) + ["LT", "UGT", "UGE", "IB", "BM"], 4 + ch)
-        for j, (s, m, mk) in enumerate(((3, kL, "0"), (4, kL, "0"), (5, nL, "2"), (6, nL, "2"), (5, both, "3"),
-                                        (6, both, "3"))):
-            tt(T.Q[:, 384 * ch + 64 * j:384 * ch + 64 * (j + 1)], c[:, 64 * s:64 * (s + 1)], m, A.mult, [kk + mk],
-               ["Q%d_%d" % (ch, j)], [2 + ch])
-        nu, w, wk, o0 = ((8, T.WU, "WU", 14), (4, T.WT, "WT", 12))[ch]
-        st = 160 + 16 // nu
-        mm([[(ps[6 + ch][:, u:64 * nu:nu], w[:, st * u + o0 - 4 * q:st * u + 128 + o0 - 4 * q],
-              T.Q[:, 384 * ch + 64 * j:384 * ch + 64 * (j + 1)]) for j, q in enumerate((0, 1, 0, 1, 2, 3))]
-            for u in range(nu)], num("Q%d_" % ch, range(6)) + num(wk, range(nu)), 6 + ch)
-
-    def post_b(ch):
-        f, z0 = ps[4 + ch], 192 * ch
-        tt(T.ZZ[:, z0 + 128:z0 + 192], f[:, 128:192], T.ZZ[:, z0 + 64:z0 + 128], A.max, ["Z%d_1" % ch],
-           ["Z%d_2" % ch], [4 + ch])
-        if ch == 1:
-            ts(T.INV[:], T.TT[:], f[:, 192:193], float(HALF), A.is_ge, A.mult, ["TT"], ["INV"], [5])
-        t1(T.UP[:, 64 * ch:64 * ch + 64], T.ZZ[:, z0 + 128:z0 + 192], 16.0, A.add, ["Z%d_2" % ch], ["UP%d" % ch])
-
-    def lay(ch):
-        if ch == 0:
-            for r in range(2):
-                act(T.D[:, r:1024:2], ps[6][:, 0:512], c2[:, 4 + r:5 + r], ["o2"], ["D0_%d" % r], [6])
-        else:
-            for r in range(4):
-                t1(T.D[:, 1024 + r:2048:4], ps[7][:, 0:256], col[:, 28 + r:29 + r], A.mult, ["or"], ["D1_%d" % r], [7])
-
-    def scatter(ch):
-        rk = ["UP%d" % ch] + num("D%d_" % ch, range(4)) + num("Wz%d_" % ch, range(2))
-        if ch == 0:
-            op("S", lambda: S.activation(T.W2[:, :].indirect(T.UP[:, 0:64]), T.D[:, 0:1024], AF.Silu), rk, ["W2"])
-        else:
-            cp(T.W[:, :].indirect(T.UP[:, 64:128]), T.D[:, 1024:2048], rk, ["W"])
-
-    def conv(k):
-        lo, hi = (16 + 512 * k if k else 0), 528 + 512 * k
-        if k % 2:
-            act(T.W16[:, lo:hi], T.W[:, lo:hi], 1.0, ["W", "Wz1_0", "Wz1_1"], ["W16_%d" % k])
-        else:
-            cp(T.W16[:, lo:hi], T.W[:, lo:hi], ["W", "Wz1_0", "Wz1_1"], ["W16_%d" % k])
-
-    def back(ch, first):
-        o = 16 + 1024 * ch
-        win, wt = (T.X16, T.WC) if first else (T.W16, T.WB)
-        if first:
-            lo = o if ch else 0
-            act(T.X16[:, lo:o + 1024], T.W2[:, lo:o + 1024], 1.0, ["W2", "Wz0_0", "Wz0_1"], ["X16_%d" % ch])
-            rk = num("X16_", range(ch + 1)) + ["WC0", "WC4", "WC5", "INV", "I16"]
-        else:
-            rk = num("W16_", range(max(2 * ch - 1, 0), 2 * ch + 2)) + num("WB", range(6))
-        for j, b, c in ((1, 2, 448), (0, 0, 64)):
-            out = ps[b + ch][:, c:c + 64]
-            x = [(out, wt[:, 144 * (4 + j) + 15 - i:144 * (4 + j) + 143 - i], win[:, o + i:o + 1024:16])
-                 for i in range(15)]
-            x.append((out, wt[:, 144 * j:144 * j + 128], win[:, o + 15:o + 1024:16]))
-            x.append((out, wt[:, 144 * (j + 2) + 15:144 * (j + 2) + 143], win[:, o - 1:o + 1023:16]))
-            if first:
-                x.append((out, T.I16[:], T.INV[:, 64 * ch:64 * ch + 64]))
-            mm([x], rk, b + ch, first, not first)
-
-    F0 = OPT["first"]
-
-    def gather0(scale, out, key, both=True):
-        gb(0, 0, F0, scale); gb(0, F0, 32, scale); gb(0, 32, 64, scale)
-        ua(0)
-        ga(0, 0, F0, out, key)
-        if both:
-            ub(1)
-            gb(1, 0, 32, scale); gb(1, 32, 64, scale)
-        ga(0, F0, 32, out, key); ga(0, 32, 64, out, key)
-        if both:
-            ua(1)
-
-    def reopen(rnd, scale, out, key):
+    def refill():
         for k in range(4):
-            conv(k)
-        if rnd < 5:
-            zero_w(0); zero_w(1)
-        back(0, False); back(1, False)
-        ub(0)
-        gather0(scale, out, key)
+            dma("Y", T.W[:, 516 * k:516 * (k + 1)], T.ZC[:], ["ZC"], ["Wz%d" % k])
 
-    def both_chunks(rnd, ks):
-        decide(0, 64, 0, ((0, 32), (32, 64)), a=lambda: ga(1, 0, 32), c=lambda: ga(1, 32, 64))
-        lists(0, 64)
-        meta(1, 64, ((0,), (1, 2)))
-        if rnd == 3:
-            kids(3, 0, 0)
-            kids_s(0, 3, 1, 32)
-        ul(0, 64, 0)
-        kids(*ks[0])
-        decide(1, 64, 1, ((0, 32), (32, 64)), c=lambda: kids(*ks[1]), begun=True)
-        lists(1, 64); cands(0); cands(1)
-        if rnd == 3:
-            fails(3, 64, [ps[7][:, 256:384:2], ps[7][:, 257:384:2]], 7, T.F12[:, 0:64], ["F1"])
-            act(T.F12[:, 64:192], ps[7][:, 256:384], 1.0, [], ["F2"], [7])
-        kids(*ks[2])
-        ul(1, 64, 1)
-        for x in ks[3:]:
-            kids(*x)
-        fails_full(0, rnd, (0, 1))
-        if OPT["spath"]:
-            kids_s(0, 1, 0, 0)
+    table("a", (0, 1, 2, 3, 4, 0, 1, 2), "VSVSSVSV", range(5))
+    kids("b")
+    table("a", (0, 1, 2, 3, 4, 0, 1, 2), "VSVSSVSV", range(5, 8))
+
+    NB, CH = (8, 8, 4, 8), (0, 1, 0, 0)
+    PT = (T.PC0, T.PC1, T.PQ, T.PC0)
+    NFO, FLO = (0, 1024, 2048, 2560), (0, 2048, 4096, 5120)
+    MX, UO = {"a": T.MA, "b": T.MB}, {"a": 0, "b": 128}
+    LB = {"b": (6, 2), "a": (7, 3)}
+
+    def ulist(e, x, ch):
+        add(e, T.UAB[:, UO[x] + 64 * ch:UO[x] + 64 * ch + 64], ps[LB[x][ch]][:, 448:512], COL, [], ["U%s%d" % (x, ch)],
+            [LB[x][ch]])
+
+    def rows(e, x, ch, lo, hi):
+        o, u = 1024 * ch, UO[x] + 64 * ch
+        move(e, MX[x][:, o + 16 * lo:o + 16 * hi], TAB[x][:, 0:M + 1].indirect(T.UAB[:, u + lo:u + hi]),
+             TK[x] + ["U%s%d" % (x, ch)], keys("M%s%d" % (x, ch), lo, hi))
+
+    def turn(s, x, closes):
+        B, ch = NB[s], CH[s]
+        o, c = 1024 * ch, (24 * B if x == "b" else 0)
+        mm([[(ps[ch][:, c + b:c + 32 * B:B], MX[x][:, o + b:o + 128 * B:B], (T.SB if x == "b" else T.SA)[:])
+             for b in range(B)]], keys("M%s%d" % (x, ch), 0, 8 * B) + ["SA", "SB"], ch, False, closes)
+
+    def pk(s, k, side):
+        return "%s_%d_%d" % (PT[s].name, k, side)
+
+    def pw(s, k, side):
+        U = 16 // NB[s]
+        return PT[s][:, 8 * U * k + U - 1:8 * U * (k + 1):U, side::2]
+
+    MASK, KA, KB, XA, XB = range(5)
+
+    def val(s, v):
+        return ps[CH[s]][:, 8 * NB[s] * v:8 * NB[s] * (v + 1)]
+
+    def masks(s):
+        z = [PT[s].name + "z"]
+        t1(pw(s, MASK, 0), val(s, 3), 0.0, A.is_ge, z, [pk(s, MASK, 0)], [CH[s]])
+        t1(pw(s, MASK, 1), val(s, 3), 0.0, A.is_lt, z, [pk(s, MASK, 1)], [CH[s]])
+
+    def prods(s, which, next_lists=False):
+        for k, side in which:
+            v, m = {KA: (1 + side, 0), KB: (5 - side, 1), XA: (0, 1), XB: (6, 0)}[k]
+            out, key = pw(s, k, side), pk(s, k, side)
+            if next_lists:
+                out = T.GQ[:, 16 * k - 15:16 * k:2, side::2] if s == 2 else T.GC[:, 128 * k - 128 + side:128 * k:2]
+                key = "G%d_%d_%d" % (s, k, side)
+            tt(out, val(s, v), pw(s, MASK, m), A.mult, [pk(s, MASK, m), "GQz"], [key], [CH[s]])
+
+    def tlist(s, j, b):
+        B = NB[s]
+        U, N = 16 // B, 8 * B
+        r1, rs = ((T.R2, T.R2S) if U == 2 else (T.R4, T.R4S))
+        terms = ((MASK, 0, rs), (XB, 0, r1), (XA, 0, r1)) if j == 2 else ((MASK, 1, rs), (KA, j, r1), (KB, j, r1))
+        mm([[(ps[b][:, 64 * j:64 * j + N], PT[s][:, 8 * U * k + U - 1 - i:8 * U * (k + 1) + U - 1 - i, side::2],
+              r[:, N * i:N * (i + 1)]) for k, side, r in terms for i in range(U)]],
+           [pk(s, k, side) for k, side, r in terms] + [r1.name, rs.name], b)
+
+    def ut(e, s, j, b):
+        N = 8 * NB[s]
+        add(e, T.UL[:, 192 * s + 64 * j:192 * s + 64 * j + N], ps[b][:, 64 * j:64 * j + N], COL, [],
+            ["UL%d_%d" % (s, j)], [b])
+
+    def grow(s, x, to):
+        ks = (KA, XA) if x == "a" else (KB, XB)
+        if s == 2:
+            terms = [(T.GQ[:, 16 * k - 15 - i:16 * k + 1 - i, :], T.R2[:, 64 * i:64 * i + 64]) for k in ks for i in range(2)]
         else:
-            kids(1, 0, 0)
-        kids(1, 0, 32)
-        post_a(0, rnd); lay(0)
-        kids(1, 1, 0)
-        post_b(0)
-        scatter(0)
-        fails_full(1, rnd, (0,))
-        kids(1, 1, 32)
-        fails_full(1, rnd, (1,))
-        post_a(1, rnd); post_b(1); lay(1)
-        scatter(1)
-        back(0, True); back(1, True)
+            terms = [(T.GC[:, 128 * k - 128:128 * k], T.I16[:, 64 * to:64 * to + 64]) for k in ks]
+        mm([[(ps[LB[x][to]][:, 448:512], l, r) for l, r in terms]],
+           ["G%d_%d_%d" % (s, k, side) for k in ks for side in range(2)] + ["R2", "I16"], LB[x][to])
 
-    act(T.MB[:, 0:512], T.TA[:, :].indirect(T.UAB[:, 0:32]), -1.0, TAK + ["UA0"], keys("MB0", 0, 32))
-    tt(T.MD[:, 0:512], T.TB[:, :].indirect(T.UAB[:, 64:96]), T.MB[:, 0:512], A.add,
-       TBK + ["UB0"] + keys("MB0", 0, 32), keys("MD0", 0, 32))
-    decide(0, 32, 2, (), T.WN, ["WN"], consts_a, consts_b, consts_c)
-    grow(32, 0, 0)
-    consts_d()
-    ub(0); lists(0, 32)
-    gather0(-1.0, T.MD, "MD", False)
-    ul(0, 32, 2)
-    fixed(2, 32, 0, 32)
-    decide(0, 64, 3, (), a=consts_e, b=lambda: kids(2, 0, 0, 32), c=lambda: kids(2, 1, 0, 32))
-    grow(64, 0, 0)
-    ub(0); grow(64, 32, 1); lists(0, 64)
-    fails(2, 32, [ps[7][:, 256:320:2], ps[7][:, 257:320:2]], 7, None, [])
-    gather0(-1.0, T.MD, "MD")
-    ul(0, 64, 3)
-    need("G", ["UL3"])
-    zero_w(0); zero_w(1)
-    fixed(3, 64, 0, 32); fixed(3, 64, 32, 64)
-    act(T.F12[:, 0:64], ps[7][:, 256:320], 1.0, [], ["F1"], [7])
-    K0 = [(0, 0, 0), (0, 1, 0), (0, 0, 32), (0, 1, 32)]
-    both_chunks(3, [(3, 1, 0), (3, 0, 32)] + K0)
-    act(T.FSZU[:], x0, 256.0, ["t0"], ["FSZU"])
+    def cands(s):
+        js = [((KA, 0), (XA, 0)), ((KA, 1), (XA, 0)), ((KB, 0), (XB, 0)), ((KB, 1), (XB, 0))]
+        mm([[(ps[2 + s][:, 64 * j:64 * j + 64], T.I16[:], pw(s, k, side)) for k, side in x] for j, x in enumerate(js)],
+           [pk(s, k, side) for x in js for k, side in x] + ["I16"], 2 + s)
+
+    def fixed(s, lo, hi):
+        o, u = NFO[s], 192 * s + 128
+        act(T.NF[:, o + 16 * lo:o + 16 * hi], T.H[:, :].indirect(T.UL[:, u + lo:u + hi]), -1.0,
+            HALL + ["UL%d_2" % s], keys("NF%d" % s, lo, hi))
+
+    def test(s, side, lo, hi):
+        o, u, f = NFO[s], 192 * s + 64 * side, FLO[s] + 128 * NB[s] * side
+        tt(T.FL[:, f + 16 * lo:f + 16 * hi], T.H[:, :].indirect(T.UL[:, u + lo:u + hi]), T.NF[:, o + 16 * lo:o + 16 * hi],
+           A.is_lt, HALL + ["UL%d_%d" % (s, side)] + keys("NF%d" % s, lo, hi), keys("FL%d_%d" % (s, side), lo, hi))
+
+    def carry(s, b, terms, reads):
+        N = 16 * NB[s]
+        mm([[(ps[b][:, 0:N], T.IB[:], T.Z[:, 0:N])]
+            + [(ps[b][:, side:N:2], l, r) for side in range(2) for l, r in terms]], ["IB", "Z"] + reads, b, True, False)
+
+    def fails(s, side, b, alone):
+        B = NB[s]
+        f = FLO[s] + 128 * B * side
+        x = [(ps[b][:, 2 * j + side:16 * B:2 * B], T.FL[:, f + j:f + 128 * B:B], T.SF[:]) for j in range(B)]
+        rk = keys("FL%d_%d" % (s, side), 0, 8 * B) + ["SF"]
+        if alone:
+            mm([[y] for y in x], rk, b)
+        else:
+            mm([x], rk, b, False, side == 1)
+
+    def scan(out, m, key):
+        op("V", lambda: V.tensor_tensor_scan(out, m[:], T.K[:], 0.0, A.mult, A.add), ["K", m.name], [key])
+
+    def post(s, gaps=()):
+        f, c, p = ps[4 + s][:, 0:128], ps[2 + s], ps[6 + s]
+        gaps = list(gaps)
+
+        def gap():
+            if gaps:
+                gaps.pop(0)()
+        t1(T.K[:], f, 0.0, A.is_equal, [], ["K"], [4 + s])
+        gap()
+        scan(T.C4[:], T.M4, "C4")
+        scan(T.C16[:, 128 * s:128 * (s + 1)], T.M16, "C16_%d" % s)
+        gap()
+        tt(T.CODE[:], f, T.C4[:], A.add, ["C4"], ["CODE"], [4 + s])
+        tt(T.E[:], T.CDS[:], T.C4[:, 3:128:4], A.subtract, ["CDS", "C4"], ["E"])
+        x = [(p[:, 0:32], T.I16[:], T.C25[:]), (p[:, 0:32], T.IP[:], T.C16[:, 128 * s + 3:128 * s + 128:4]),
+             (p[:, 0:32], T.IN[:], T.C4[:, 3:128:4])]
+        for t in range(s + 1):
+            x += [(p[:, j:32:4], (T.LT if t == s else T.ON)[:], T.C16[:, 128 * t + 15:128 * t + 128:16]) for j in range(4)]
+        mm([x], ["I16", "C25", "IP", "IN", "LT", "ON", "C4"] + num("C16_", range(s + 1)), 6 + s)
+        gap()
+        for r in range(4):
+            t1(T.MR[:, 128 * r:128 * (r + 1)], T.CODE[:], r + 1.0, A.is_equal, ["CODE"], ["MR%d" % r])
+        zk = []
+        for r in range(4):
+            for side in range(2):
+                for v in range(2 if r < 3 or side else 0):
+                    zk.append("ZQ%d" % (8 * v + 4 * side + r))
+                    tt(T.ZQ[:, 8 * v + 4 * side + r::16, :], c[:, 128 * v + 64 * side:128 * v + 64 * side + 64],
+                       T.MR[:, 128 * r + side:128 * (r + 1):2], A.mult, ["MR%d" % r, "ZQz"], zk[-1:], [2 + s])
+            if r == 0:
+                tt(T.ZP[:, 3::4, :], p[:, 0:32], T.E[:], A.max, ["E", "ZPz"], ["ZP"], [6 + s])
+                mm([[(p[:, 64:96], T.ZP[:, 3 - i:35 - i, :], T.R4W[:, 32 * i:32 * (i + 1)]) for i in range(4)]],
+                   ["ZP", "R4W"], 6 + s)
+                add("S", T.UP[:, 32 * s:32 * (s + 1)], p[:, 64:96], COL + 16, [], ["UP%d" % s], [6 + s])
+        for lo, hi, b, lay, e in (((0, 128, 0, "S", "S"),), ((0, 64, 1, "V", "V"), (64, 128, 5, "S", "V")))[s]:
+            mm([[(ps[b][:, 4 * lo + j:4 * hi:4], T.ZQ[:, :, 2 * j + u], T.I16[:, lo:hi]) for u in range(2)]
+                for j in range(4)], zk + ["I16"], b)
+            d, dk = T.D[:, 512 * s + 4 * lo:512 * s + 4 * hi], "D%d_%d" % (s, lo)
+            add(lay, d, ps[b][:, 4 * lo:4 * hi], LIFT, [], [dk], [b])
+            win = T.W[:, :].indirect(T.UP[:, 32 * s + lo // 4:32 * s + hi // 4])
+            rk = ["UP%d" % s, dk] + num("Wz", range(4))
+            if e == "S":
+                op("S", lambda: S.activation(win, d, AF.Silu), rk, ["W"])
+            else:
+                cp(win, d, rk, ["W"])
+
+    def back(x, ch):
+        v, o = "ab".index(x), 16 + 1024 * ch
+        mm([[(ps[LB[x][ch]][:, 448:512], bk(v, w), T.W16[:, o + w:o + w + 1009:16]) for w in range(-3, 16)]],
+           num("W16_", range(max(2 * ch - 1, 0), 2 * ch + 2)) + num("BK", range(7 * v, 7 * v + 7)), LB[x][ch])
+
+    def reopen(more):
+        if more:
+            clear(0)
+        for k, e in enumerate("VSVS"):
+            lo, hi = (16 + 512 * k if k else 0), 528 + 512 * k
+            add(e, T.W16[:, lo:hi], T.W[:, lo:hi], -LIFT, ["W"] + num("Wz", range(4)), ["W16_%d" % k])
+        if more:
+            refill()
+        back("b", 0); back("a", 0); back("b", 1)
+
+    STAY, LEFT, RIGHT = ((XB, 0), (XA, 0)), ((KA, 0), (KB, 0)), ((KA, 1), (KB, 1))
+
+    def decide(s):
+        masks(s); prods(s, STAY); tlist(s, 2, 6)
+        prods(s, LEFT); prods(s, RIGHT)
+        tlist(s, 0, 7); tlist(s, 1, 7)
+
+    def full():
+        ulist("S", "b", 0); rows("S", "b", 0, 0, 48); rows("V", "b", 0, 48, 64)
+        ulist("V", "a", 0); rows("V", "a", 0, 0, 48); rows("S", "a", 0, 48, 64)
+        turn(0, "b", False); turn(0, "a", True)
+        back("a", 1)
+        ulist("S", "b", 1)
+        rows("V", "b", 1, 0, 16); rows("S", "b", 1, 16, 64)
+        decide(0)
+        ut("S", 0, 2, 6)
+        ulist("V", "a", 1)
+        ut("V", 0, 0, 7); ut("V", 0, 1, 7)
+        fixed(0, 0, 16); fixed(0, 16, 32); fixed(0, 32, 64)
+        cands(0); clear(1)
+        turn(1, "b", False)
+        test(0, 0, 0, 16); test(0, 1, 0, 16)
+        rows("S", "a", 1, 0, 64)
+        test(0, 0, 16, 32); test(0, 1, 16, 32)
+        turn(1, "a", True)
+        finish(True)
+
+    def finish(alone):
+        test(0, 0, 32, 64)
+        fails(0, 0, 4, alone)
+        test(0, 1, 32, 64)
+        fails(0, 1, 4, alone)
+        decide(1)
+        ut("S", 1, 2, 6)
+        fixed(1, 0, 16)
+        ut("S", 1, 0, 7); ut("S", 1, 1, 7)
+        cands(1)
+        fixed(1, 16, 32); fixed(1, 32, 64)
+        post(0, (lambda: None, lambda: None, lambda: test(1, 0, 0, 16)))
+        test(1, 1, 0, 16); test(1, 0, 16, 64)
+        fails(1, 0, 5, alone)
+        test(1, 1, 16, 64)
+        fails(1, 1, 5, alone)
+        post(1)
+
+    def doubled(s, tos):
+        masks(s)
+        prods(s, ((KB, 0), (KB, 1), (XB, 0), (XB, 1)), True)
+        grow(s, "b", 0)
+        prods(s, ((KA, 0), (KA, 1), (XA, 0), (XA, 1)), True)
+        grow(s, "a", 0)
+        for to in tos:
+            grow(s, "b", to); grow(s, "a", to)
+        prods(s, STAY + LEFT + RIGHT)
+        clear(0)
+        for j in (2, 0, 1):
+            tlist(s, j, 4 + (j == 2))
+
+    spread("S", "b", 0); spread("V", "b", 1)
+    pen("b")
+    clear(0)
+    rows("S", "a", 0, 0, 32); turn(2, "a", False)
+    counting()
+    spread("S", "b", 2); spread("V", "b", 3)
+    table("b", (1, 2, 3, 4, 5, 6, 7, 1), "VSVSVSVS")
+    rows("V", "b", 0, 16, 32); rows("S", "b", 0, 0, 16); turn(2, "b", True)
+    shifting(0)
+    doubled(2, ())
+    ulist("S", "b", 0); rows("S", "b", 0, 0, 64)
+    ulist("V", "a", 0); rows("V", "a", 0, 0, 64)
+    turn(3, "b", False); turn(3, "a", True)
+    ut("S", 2, 2, 5); ut("S", 2, 0, 4); ut("S", 2, 1, 4)
+    fixed(2, 0, 32)
+    shifting(1)
+    doubled(3, (1,))
+    need("Y", ["UL2_0"])
+    refill()
+    ulist("S", "b", 0); rows("S", "b", 0, 0, 64)
+    ulist("V", "a", 0); rows("V", "a", 0, 0, 64)
+    turn(0, "b", False); turn(0, "a", True)
+    ut("S", 3, 2, 5); ut("S", 3, 0, 4); ut("S", 3, 1, 4)
+    test(2, 0, 0, 32)
+    fixed(3, 0, 32)
+    decide(0)
+    test(2, 1, 0, 32)
+    ut("S", 0, 2, 6); ut("S", 0, 0, 7); ut("S", 0, 1, 7)
+    fails(2, 0, 4, True); fails(2, 1, 4, True)
+    cands(0); clear(1)
+    fixed(0, 0, 32)
+    act(T.F1[:], ps[4][:, 0:64], 1.0, [], ["F1"], [4])
+    test(3, 0, 0, 32); test(3, 1, 0, 32)
+    fixed(3, 32, 64); fixed(0, 32, 64)
+    ulist("S", "b", 1); ulist("S", "a", 1)
+    test(0, 0, 0, 32); test(0, 1, 0, 32)
+    rows("S", "b", 1, 0, 64)
+    turn(1, "b", False)
+    test(3, 0, 32, 64); test(3, 1, 32, 64)
+    carry(3, 4, [(T.IB[:], T.F1[:])], ["F1"])
+    fails(3, 0, 4, False); fails(3, 1, 4, False)
+    rows("S", "a", 1, 0, 64)
+    act(T.F2[:], ps[4][:, 0:128], 1.0, [], ["F2"], [4])
+    turn(1, "a", True)
+    for s in range(2):
+        carry(s, 4 + s, [(T.S2[:, 256 * s + 128 * i:256 * s + 128 * (i + 1)], T.F2[:, i::2, :]) for i in range(2)],
+              ["S2", "F2"])
+    finish(False)
     for rnd in (4, 5):
-        reopen(rnd - 1, -1.0, T.MD, "MD")
-        both_chunks(rnd, K0)
-    row(T.TA, 4, T.SZU[:], ["SZU"], "TAr4")
-    row(T.TB, 4, T.FSZU[:], ["FSZU"], "TBr4")
-    row(T.TA, 6, T.IDN[:], ["IDN"], "TAr0")
-    row(T.TB, 7, T.IDN[:], ["IDN"], "TBr2")
-    t1(T.TA[:, M:M + 1], col[:, 14:15], -1.0, A.mult, ["oh"], ["TAd"])
-    t1(T.TB[:, M:M + 1], col[:, 15:16], -1.0, A.mult, ["oh"], ["TBd"])
-
-    def put(ch, qs):
-        for e, y, r in zip(qs, (T.ya, T.yb, T.ys), (6, 7, 4)):
-            dma(e, y[:, 1024 * ch:1024 * (ch + 1)], T.OUT[r::16, 1024 * ch:1024 * (ch + 1)],
-                keys("OUT%d" % ch, 0, 64), [])
-    reopen(5, 1.0, T.OUT, "OUT")
-    put(0, "YYY")
-    ga(1, 0, 32, T.OUT, "OUT"); ga(1, 32, 64, T.OUT, "OUT")
-    put(1, "YSG")
+        reopen(True)
+        if rnd == 4:
+            closing()
+        full()
+    reopen(False)
+    back("a", 1)
+    pieces = ((0, 0, 32), (0, 32, 64), (1, 0, 32), (1, 32, 48), (1, 48, 64))
+    for j, (ch, lo, hi) in enumerate(pieces):
+        if lo == 0:
+            ulist("S", "b", ch); ulist("V", "a", ch)
+        rows("S", "b", ch, lo, hi); rows("V", "a", ch, lo, hi)
+        for i in [j - 1] * (j > 0) + [j] * (j == 4):
+            c, l, h = pieces[i]
+            move("SV"[i % 2], T.OUT[:, 1024 * c + 16 * l:1024 * c + 16 * h], ps[(0, 1, 4, 5, 0)[i]][:, 0:16 * (h - l)],
+                 [], keys("OUT%d" % c, l, h), [(0, 1, 4, 5, 0)[i]]) if i < j else None
+        o, w, b = 1024 * ch + 16 * lo, 16 * (hi - lo), (0, 1, 4, 5, 0)[j]
+        mm([[(ps[b][:, 0:w], T.OB[:], T.MB[:, o:o + w])]], keys("Mb%d" % ch, lo, hi) + ["OB"], b, True, False)
+        mm([[(ps[b][:, 0:w], T.OA[:], T.MA[:, o:o + w])]], keys("Ma%d" % ch, lo, hi) + ["OA"], b, False, True)
+        if j == 2:
+            for r, y in enumerate((T.ya, T.yb, T.ys)):
+                dma("Y", y[:, 0:1024], T.OUT[r::16, 0:1024], keys("OUT0", 0, 64), [])
+    move("V", T.OUT[:, 1792:2048], ps[0][:, 0:256], [], keys("OUT1", 48, 64), [0])
+    for r, y in enumerate((T.ya, T.yb, T.ys)):
+        dma("YSY"[r], y[:, 1024:2048], T.OUT[r::16, 1024:2048], keys("OUT1", 0, 64), [])
     ends["sent"] = sent[0]
     for s, v in ends.items():
         g.wait_ge(T.sem[s], v)

@@ -9,7 +9,7 @@ BIG = 16.0
 LIFT = 4096.0
 MAGIC = 1.5 * 2.0 ** 27
 SC = 2.0 ** -13
-OPT = {"route": "axbd", "order": "k01s23"}
+OPT = {"route": "addd", "order": "k0s123", "split": 1}
 NDMA = 48
 
 
@@ -20,12 +20,12 @@ def _sb(n, dt):
 SCRATCH = {}
 for _dt, _list in (
         ("bfloat16", dict(H=2 * SO, relay=SO, Z=1312, IB=128, SF=8, SZ=8, NF=3584, FL=7168, F1=64, F2=[16, 8],
-                          S2=512, ONE=512, CODE=128, J=160, J2=128, J4=128, JT=64)),
+                          S2=512, KB=1024, ONE=512, CODE=128, J=160, J2=128, J4=128, JT=64)),
         ("float16", dict(W16=2064, MA=2048, MB=2048, I16=128, I8=128, R2=128, R2S=128, R4=128, R4S=128, R4W=128,
                          LT=128, ON=128, IP=128, IN=128, SA=32, SB=32, OA=128, OB=128, BK=2 * 908, M4=128, M16=128,
-                         CDS=32, C25=32, ZERO=512, PQ=[163, 8], PC0=[81, 16], PC1=[81, 16], ZQ=[128, 8], ZP=[35, 4],
+                         CDS=32, C25=32, ZERO=512, PQ=[163, 8], PC0=[81, 16], PC1=[81, 16], ZQ=[256, 8], ZP=[35, 4],
                          GQ=[65, 8], GC=512,
-                         K=128, C4=128, C16=256, MR=512, E=32, Ua=512, Ub=512, La=512, Lb=512, Na=512, Nb=512,
+                         K=128, C4=128, C16=256, MR=1024, E=32, Ua=512, Ub=512, La=512, Lb=512, Na=512, Nb=512,
                          Sa=256, Sb=256, Ca=1024, Cb=1024, Za=[136, 16], Zb=[136, 16])),
         ("float32", dict(TA=4104, TB=4104, W=5152, IDR=256, IDT=256, CD=32, col=64, ZC=516, D=1024, OUT=2048,
                          st=64)),
@@ -55,6 +55,10 @@ def bits(m):
     return bin(m).count("1")
 
 
+def near_mask(src, helper, dst, topo):
+    return topo.mask(src, helper) & ~topo.mask(src, dst) if OPT["split"] else topo.mask(src, helper)
+
+
 def helper_program(g, core, T, topo):
     n = len(T.cores)
     out = 0
@@ -63,7 +67,7 @@ def helper_program(g, core, T, topo):
         for k, h in enumerate(routes(src, dst, T, topo)):
             if h == core:
                 q = quarter(k)
-                g.wait_ge(T.sem["hi%d" % k], bits(topo.mask(src, core)))
+                g.wait_ge(T.sem["hi%d" % k], bits(near_mask(src, core, dst, topo)))
                 rid, pid, _ = topo.addr(dst)
                 m = topo.mask(core, dst)
                 g.remote_dma(T.H[:, SO + q.start:SO + q.stop], T.relay[:, q], T.sem["rh%d" % k], T.sem.hout, pid, rid, m)
@@ -135,11 +139,12 @@ def rank_program(g, core, T, topo):
         eng[e].dma_start(out, in_).then_inc(T.sem[s], 16)
         done(e, (s, 16), reads, writes, [])
 
-    def send(to, out, in_, sem, reads):
+    def send(to, out, in_, sem, reads, m=None):
         need("G", reads)
         rid, pid, _ = topo.addr(to)
-        g.remote_dma(out, in_, T.sem[sem], T.sem.sent, pid, rid, topo.mask(core, to))
-        sent[0] += bits(topo.mask(core, to))
+        m = m or topo.mask(core, to)
+        g.remote_dma(out, in_, T.sem[sem], T.sem.sent, pid, rid, m)
+        sent[0] += bits(m)
 
     def arrives(key, sem, frm):
         wr[key] = [(sem, bits(topo.mask(frm, core)))]
@@ -245,16 +250,17 @@ def rank_program(g, core, T, topo):
         fill(z[:, 134:135, :], 0.0, z.name + "q")
     tt(ps[5][:, 0:1], ps[5][:, 0:1], oh[8], A.add, ["own", "oh"], ["own"], [5])
 
-    def kids(x):
+    def kids(x, between=lambda: None):
         U, L, N, Sf = T["U" + x], T["L" + x], T["N" + x], T["S" + x]
 
         def over(t, key, sides, closes):
             mm([[(ps[6][:, 256 * s + 128 * h:256 * s + 128 * h + 128], t[:, 256 * s + 128 * h:256 * s + 128 * h + 128],
                   T.I16[:]) for s in sides for h in range(2)]], [key, "I16"], 6, False, closes)
-        over(U, "U" + x, (0, 1), False)
         ts(L[:], U[:], -float(HALF), float(HALF), A.is_equal, A.mult, ["U" + x], ["L" + x])
         ts(N[:], U[:], 0.0, float(HALF), A.is_equal, A.mult, ["U" + x], ["N" + x])
         tt(Sf[:], ps[5][:, 0:256], L[:, 0:256], A.mult, ["own", "L" + x], ["S" + x], [5])
+        between()
+        over(U, "U" + x, (0, 1), False)
         over(L, "L" + x, (0, 1), False); over(N, "N" + x, (0, 1), False); over(Sf, "S" + x, (0,), True)
         act(T["C" + x][:, 0:512], ps[6][:, 0:512], 1.0, [], ["C%s0" % x, "C%s1" % x], [6])
 
@@ -279,11 +285,13 @@ def rank_program(g, core, T, topo):
         for q in qs:
             mm([[(ps[banks[q]][:, 128 * j:128 * (j + 1)], z[:, 8 * (j % 2):8 * (j % 2) + 128, 2 * q + j // 2], T.I16[:])]
                 for j in range(4)], rk, banks[q])
-            move(es[q], t[:, 512 * q:512 * (q + 1)], ps[banks[q]][:, 0:512], [], ["T%s%d" % (x, q)], [banks[q]])
-            if q == 5:
-                t1(t[:, M:M + 1], t[:, HALF:HALF + 1], col[:, 25:26], A.add, ["T%s4" % x, "fix"], ["T%sd" % x])
-                t1(t[:, HALF:HALF + 1], oh[5], -1.0, A.mult, ["oh"], ["T%s4" % x])
-    TK = {x: num("T" + x, range(8)) + ["T%sd" % x] for x in "ab"}
+            lo = int(q == 4)
+            move(es[q], t[:, 512 * q + lo:512 * (q + 1)], ps[banks[q]][:, lo:512], [], ["T%s%d" % (x, q)], [banks[q]])
+            if lo:
+                t1(t[:, M:M + 1], ps[banks[q]][:, 0:1], col[:, 25:26], A.add, ["fix"], ["T%sd" % x], [banks[q]])
+    TK = {x: num("T" + x, range(8)) + ["T%sd" % x, "T%se" % x] for x in "ab"}
+    for x in "ab":
+        t1(TAB[x][:, HALF:HALF + 1], oh[5], -1.0, A.mult, ["oh"], ["T%se" % x])
 
     def sizes(k):
         mm([[(ps[7][:, 128 * h + i:128 * h + 128:16], T.H[:, 256 * i + 128 * h:256 * i + 128 * h + 128], T.SZ[:])
@@ -310,49 +318,20 @@ def rank_program(g, core, T, topo):
     cp(T.UAB[:, 0:32], T.st[:, 0:32], ["st"], ["Ua0"])
     cp(T.UAB[:, 128:160], T.st[:, 32:64], ["st"], ["Ub0"])
     ts(T.SB[:], T.JT[:, 32:64], c_pp, col[:, 24:25], A.is_equal, A.mult, ["JB", "c_pp", "sg"], ["SB"])
-    spread("S", "a", 0); spread("S", "a", 1)
-    op("S", lambda: S.activation(T.ZC[:], T.Z[:, 0:516], AF.Silu, bias=bias[LIFT]), ["Z", "bias"], ["ZC"])
-    pen("a")
-    sizes(2)
-    cp(T.H[:, M:M + 1], T.H[:, HALF:HALF + 1], ["Ho2", "Hpad"], ["Hd"])
-    for t, j, w in ((T.R2, T.J2, 1.0), (T.R2S, T.J2, SO), (T.R4, T.J4, 1.0), (T.R4S, T.J4, SO), (T.R4W, T.J4, 1 / SC)):
-        ts(t[:], j[:], c_p, float(w), A.is_equal, A.mult, [j.name, "c_p"], [t.name])
-    fill(T.H[:, HALF:HALF + 1], -262144.0, "Ho2")
-    sizes(3)
-    ts(T.Ca[:, 512:768], ps[7][:, 0:256], MAGIC, -MAGIC, A.add, A.add, [], ["Ca2"], [7])
-    ts(T.SF[:], J[:, 0:8], c_g, BIG, A.is_equal, A.mult, ["J", "c_p"], ["SF"])
-    t1(T.IB[:], J[:, 0:128], c_p, A.is_equal, ["J", "c_p"], ["IB"])
-    tt(T.Ca[:, 768:1024], ps[7][:, 0:256], T.Ca[:, 512:768], A.subtract, ["Ca2"], ["Ca3"], [7])
-    rt = routes(core, dst, T, topo)
-    for x in OPT["order"]:
-        if x == "k":
-            send(dst, T.Ub[:], T.Ua[:], "rk", ["Ua"])
-        elif x == "s":
-            send(dst, T.Cb[:, 512:1024], T.Ca[:, 512:1024], "rs", ["Ca2", "Ca3"])
-        else:
-            q = quarter(int(x))
-            rk = ["Ho" + x] + (["Hd"] if x == "3" else [])
-            if rt[int(x)] is None:
-                send(dst, T.H[:, SO + q.start:SO + q.stop], T.H[:, q], "rh" + x, rk)
-            else:
-                send(rt[int(x)], T.relay[:, q], T.H[:, q], "hi" + x, rk)
-    spread("S", "a", 2); spread("V", "a", 3)
 
-    def counting():
+    def counting(step):
+        if step:
+            fill(T.M4[:], 1.0, "M4"); fill(T.M16[:], 1.0, "M16")
+            fill(T.ZQ[:, 3::8, :], 0.0, "ZQz")
+            fill(T.ZP[:], 0.0, "ZPz")
+            fill(T.M4[:, 0:128:4], 0.0, "M4"); fill(T.M16[:, 0:128:16], 0.0, "M16")
+            return
         ts(T.LT[:], J[:, 0:128], c_p, SC, A.is_gt, A.mult, ["J", "c_p"], ["LT"])
         fill(T.ON[:], SC, "ON")
         t1(T.IP[:], T.I16[:], SC, A.mult, ["I16"], ["IP"])
         t1(T.IN[:], T.I16[:], -SC, A.mult, ["I16"], ["IN"])
         fill(T.C25[:], -HALF * SC, "C25")
         t1(T.CDS[:], T.CD[:], SC, A.mult, ["CD"], ["CDS"])
-        for c in (1.0, 0.0):
-            for t, st in ((T.M4, 4), (T.M16, 16)):
-                fill(t[:] if c else t[:, 0:128:st], c, t.name)
-        fill(T.ZQ[:, 3::8, :], 0.0, "ZQz")
-        fill(T.ZP[:], 0.0, "ZPz")
-        fill(T.ONE[:], 1.0, "ONE")
-        op("G", lambda: g.affine_select(T.S2[:], T.ONE[:], [[128, 2], [-1, 2], [1, 128]], A.is_equal, 0.0, 0, -2),
-           ["ONE"], ["S2"])
 
     EDGE = (15, 14, 13, -1, -2, -3)
 
@@ -367,7 +346,11 @@ def rank_program(g, core, T, topo):
         t1(col[:, 28:30], J[:, 0:2], c_v, A.is_equal, ["J", "c_p"], ["ov"])
         t1(col[:, 32:35], J[:, 0:3], c_r, A.is_ge, ["J", "c_p"], ["mle"])
         t1(col[:, 35:38], J[:, 1:4], c_r, A.is_le, ["J", "c_p"], ["mge"])
+        closing(0)
         tt(col[:, 26:27], c_g15, c_r, A.add, ["c_g15", "c_p"], ["tg0"])
+        for t, j, w in ((T.R2, T.J2, 1.0), (T.R2S, T.J2, SO), (T.R4, T.J4, 1.0), (T.R4S, T.J4, SO),
+                        (T.R4W, T.J4, 1 / SC)):
+            ts(t[:], j[:], c_p, float(w), A.is_equal, A.mult, [j.name, "c_p"], [t.name])
         ts(col[:, 30:32], col[:, 28:30], col[:, 26:27], -1.0, A.mult, A.add, ["ov", "tg0"], ["tg"])
 
     def shifting(v):
@@ -376,27 +359,63 @@ def rank_program(g, core, T, topo):
         for j, w in enumerate(EDGE):
             ts(bk(v, w), J[:, 16 - w:144 - w], col[:, 30 + v:31 + v], col[:, 32 + j:33 + j], A.is_equal, A.mult,
                ["J", "tg", "mle", "mge"], ["BK%d" % (7 * v + 1 + j)])
-    aims()
 
-    def closing():
+    def closing(step):
         c = [col[:, 40 + j:41 + j] for j in range(8)]
-        tt(c[0], oh[0], oh[5], A.add, ["oh"], ["z0"])
-        tt(c[1], oh[3], oh[4], A.add, ["oh"], ["z1"])
-        tt(c[2], c[1], oh[6], A.subtract, ["z1"], ["z2"])
-        tt(c[3], c[1], oh[6], A.add, ["z1"], ["z3"])
-        ts(c[4], c[2], 256.0, c[0], A.mult, A.add, ["z2", "z0"], ["z4"])
-        ts(c[5], c[3], 2.0, c_g15, A.mult, A.add, ["z3", "c_g15"], ["z5"])
-        tt(c[6], c[5], c[0], A.add, ["z5", "z0"], ["z6"])
-        ts(T.OA[:], J[:, 17:145], c[5], c[4], A.is_equal, A.mult, ["J", "z5", "z4"], ["OA"])
-        ts(T.OB[:], J[:, 17:145], c[6], c[4], A.is_equal, A.mult, ["J", "z6", "z4"], ["OB"])
+        if step == 0:
+            tt(c[0], oh[0], oh[5], A.add, ["oh"], ["z0"])
+            ts(c[2], oh[3], oh[4], oh[6], A.add, A.subtract, ["oh"], ["z2"])
+            ts(c[3], oh[3], oh[4], oh[6], A.add, A.add, ["oh"], ["z3"])
+        elif step == 1:
+            ts(c[4], c[2], 256.0, c[0], A.mult, A.add, ["z2", "z0"], ["z4"])
+            ts(c[5], c[3], 2.0, c_g15, A.mult, A.add, ["z3", "c_g15"], ["z5"])
+        elif step == 2:
+            tt(c[6], c[5], c[0], A.add, ["z5", "z0"], ["z6"])
+            ts(T.OA[:], J[:, 17:145], c[5], c[4], A.is_equal, A.mult, ["J", "z5", "z4"], ["OA"])
+        else:
+            ts(T.OB[:], J[:, 17:145], c[6], c[4], A.is_equal, A.mult, ["J", "z6", "z4"], ["OB"])
 
     def refill():
         for k in range(4):
             dma("Y", T.W[:, 516 * k:516 * (k + 1)], T.ZC[:], ["ZC"], ["Wz%d" % k])
 
-    table("a", (0, 1, 2, 3, 4, 0, 1, 2), "VSVSSVSV", range(5))
-    kids("b")
-    table("a", (0, 1, 2, 3, 4, 0, 1, 2), "VSVSSVSV", range(5, 8))
+    spread("S", "a", 0); spread("S", "a", 1)
+    op("S", lambda: S.activation(T.ZC[:], T.Z[:, 0:516], AF.Silu, bias=bias[LIFT]), ["Z", "bias"], ["ZC"])
+    aims()
+    closing(1)
+    pen("a")
+    sizes(2)
+    cp(T.H[:, M:M + 1], T.H[:, HALF:HALF + 1], ["Ho2", "Hpad"], ["Hd"])
+    shifting(0)
+    closing(2)
+    fill(T.H[:, HALF:HALF + 1], -262144.0, "Ho2")
+    shifting(1)
+    closing(3)
+    sizes(3)
+    ts(T.Ca[:, 512:768], ps[7][:, 0:256], MAGIC, -MAGIC, A.add, A.add, [], ["Ca2"], [7])
+    ts(T.SF[:], J[:, 0:8], c_g, BIG, A.is_equal, A.mult, ["J", "c_p"], ["SF"])
+    t1(T.IB[:], J[:, 0:128], c_p, A.is_equal, ["J", "c_p"], ["IB"])
+    fill(T.ONE[:], 1.0, "ONE")
+    tt(T.Ca[:, 768:1024], ps[7][:, 0:256], T.Ca[:, 512:768], A.subtract, ["Ca2"], ["Ca3"], [7])
+    rt = routes(core, dst, T, topo)
+    for x in OPT["order"]:
+        if x == "k":
+            send(dst, T.Ub[:], T.Ua[:], "rk", ["Ua"])
+        elif x == "s":
+            send(dst, T.Cb[:, 512:1024], T.Ca[:, 512:1024], "rs", ["Ca2", "Ca3"])
+        else:
+            q = quarter(int(x))
+            rk = ["Ho" + x] + (["Hd"] if x == "3" else [])
+            if rt[int(x)] is None:
+                send(dst, T.H[:, SO + q.start:SO + q.stop], T.H[:, q], "rh" + x, rk)
+            else:
+                send(rt[int(x)], T.relay[:, q], T.H[:, q], "hi" + x, rk, near_mask(core, rt[int(x)], dst, topo))
+    op("G", lambda: g.affine_select(T.S2[:], T.ONE[:], [[128, 2], [-1, 2], [1, 128]], A.is_equal, 0.0, 0, -2),
+       ["ONE"], ["S2"])
+    spread("S", "a", 2); spread("V", "a", 3)
+    table("a", (0, 1, 2, 3, 4, 7, 0, 1), "SSSSVVVV", range(4))
+    kids("b", lambda: table("a", (0, 1, 2, 3, 4, 7, 0, 1), "SSSSVVVV", range(4, 6)))
+    table("a", (0, 1, 2, 3, 4, 7, 0, 1), "SSSSVVVV", range(6, 8))
 
     NB, CH = (8, 8, 4, 8), (0, 1, 0, 0)
     PT = (T.PC0, T.PC1, T.PQ, T.PC0)
@@ -488,7 +507,7 @@ def rank_program(g, core, T, topo):
         mm([[(ps[b][:, 0:N], T.IB[:], T.Z[:, 0:N])]
             + [(ps[b][:, side:N:2], l, r) for side in range(2) for l, r in terms]], ["IB", "Z"] + reads, b, True, False)
 
-    def fails(s, side, b, alone):
+    def fails(s, side, b, alone, closes=None):
         B = NB[s]
         f = FLO[s] + 128 * B * side
         x = [(ps[b][:, 2 * j + side:16 * B:2 * B], T.FL[:, f + j:f + 128 * B:B], T.SF[:]) for j in range(B)]
@@ -496,56 +515,70 @@ def rank_program(g, core, T, topo):
         if alone:
             mm([[y] for y in x], rk, b)
         else:
-            mm([x], rk, b, False, side == 1)
+            mm([x], rk, b, False, side == 1 if closes is None else closes)
 
     def scan(out, m, key):
         op("V", lambda: V.tensor_tensor_scan(out, m[:], T.K[:], 0.0, A.mult, A.add), ["K", m.name], [key])
 
-    def post(s, gaps=()):
-        f, c, p = ps[4 + s][:, 0:128], ps[2 + s], ps[6 + s]
-        gaps = list(gaps)
+    def test_s(s, side, lo, j, b):
+        o, u, f = NFO[s] + 16 * lo, 192 * s + 64 * side + lo, FLO[s] + 128 * NB[s] * side + 16 * lo
+        kb, out = T.KB[:, 512 * j:512 * (j + 1)], ps[b][:, 0:512]
+        act(kb, T.H[:, :].indirect(T.UL[:, u:u + 32]), -1.0, HALL + ["UL%d_%d" % (s, side)], ["KB%d" % j])
+        mm([[(out, T.IB[:], T.NF[:, o:o + 512]), (out, T.IB[:], kb)]],
+           ["KB%d" % j, "IB"] + keys("NF%d" % s, lo, lo + 32), b)
+        return lambda: op("S", lambda: S.activation(T.FL[:, f:f + 512], out, AF.Relu), [],
+                          keys("FL%d_%d" % (s, side), lo, lo + 32), [b])
 
-        def gap():
-            if gaps:
-                gaps.pop(0)()
-        t1(T.K[:], f, 0.0, A.is_equal, [], ["K"], [4 + s])
-        gap()
+    def kept(s):
+        t1(T.K[:], ps[4 + s][:, 0:128], 0.0, A.is_equal, [], ["K"], [4 + s])
+
+    def counts(s):
         scan(T.C4[:], T.M4, "C4")
         scan(T.C16[:, 128 * s:128 * (s + 1)], T.M16, "C16_%d" % s)
-        gap()
-        tt(T.CODE[:], f, T.C4[:], A.add, ["C4"], ["CODE"], [4 + s])
+
+    def codes(s):
+        p = ps[6 + s]
+        tt(T.CODE[:], ps[4 + s][:, 0:128], T.C4[:], A.add, ["C4"], ["CODE"], [4 + s])
         tt(T.E[:], T.CDS[:], T.C4[:, 3:128:4], A.subtract, ["CDS", "C4"], ["E"])
         x = [(p[:, 0:32], T.I16[:], T.C25[:]), (p[:, 0:32], T.IP[:], T.C16[:, 128 * s + 3:128 * s + 128:4]),
              (p[:, 0:32], T.IN[:], T.C4[:, 3:128:4])]
         for t in range(s + 1):
             x += [(p[:, j:32:4], (T.LT if t == s else T.ON)[:], T.C16[:, 128 * t + 15:128 * t + 128:16]) for j in range(4)]
         mm([x], ["I16", "C25", "IP", "IN", "LT", "ON", "C4"] + num("C16_", range(s + 1)), 6 + s)
-        gap()
+
+    def ranks(s):
         for r in range(4):
-            t1(T.MR[:, 128 * r:128 * (r + 1)], T.CODE[:], r + 1.0, A.is_equal, ["CODE"], ["MR%d" % r])
-        zk = []
-        for r in range(4):
-            for side in range(2):
-                for v in range(2 if r < 3 or side else 0):
-                    zk.append("ZQ%d" % (8 * v + 4 * side + r))
-                    tt(T.ZQ[:, 8 * v + 4 * side + r::16, :], c[:, 128 * v + 64 * side:128 * v + 64 * side + 64],
-                       T.MR[:, 128 * r + side:128 * (r + 1):2], A.mult, ["MR%d" % r, "ZQz"], zk[-1:], [2 + s])
-            if r == 0:
-                tt(T.ZP[:, 3::4, :], p[:, 0:32], T.E[:], A.max, ["E", "ZPz"], ["ZP"], [6 + s])
-                mm([[(p[:, 64:96], T.ZP[:, 3 - i:35 - i, :], T.R4W[:, 32 * i:32 * (i + 1)]) for i in range(4)]],
-                   ["ZP", "R4W"], 6 + s)
-                add("S", T.UP[:, 32 * s:32 * (s + 1)], p[:, 64:96], COL + 16, [], ["UP%d" % s], [6 + s])
-        for lo, hi, b, lay, e in (((0, 128, 0, "S", "S"),), ((0, 64, 1, "V", "V"), (64, 128, 5, "S", "V")))[s]:
-            mm([[(ps[b][:, 4 * lo + j:4 * hi:4], T.ZQ[:, :, 2 * j + u], T.I16[:, lo:hi]) for u in range(2)]
-                for j in range(4)], zk + ["I16"], b)
-            d, dk = T.D[:, 512 * s + 4 * lo:512 * s + 4 * hi], "D%d_%d" % (s, lo)
-            add(lay, d, ps[b][:, 4 * lo:4 * hi], LIFT, [], [dk], [b])
-            win = T.W[:, :].indirect(T.UP[:, 32 * s + lo // 4:32 * s + hi // 4])
-            rk = ["UP%d" % s, dk] + num("Wz", range(4))
-            if e == "S":
-                op("S", lambda: S.activation(win, d, AF.Silu), rk, ["W"])
-            else:
-                cp(win, d, rk, ["W"])
+            o = 512 * s + 128 * r
+            t1(T.MR[:, o:o + 128], T.CODE[:], r + 1.0, A.is_equal, ["CODE"], ["MR%d_%d" % (s, r)])
+
+    ROWS = [(r, side, v) for r in range(4) for side in range(2) for v in range(2) if r < 3 or side]
+
+    def pack(s, lo, hi):
+        for r, side, v in ROWS[lo:hi]:
+            row, o, c = 8 * v + 4 * side + r, 512 * s + 128 * r, 128 * v + 64 * side
+            tt(T.ZQ[:, 128 * s + row:128 * (s + 1):16, :], ps[2 + s][:, c:c + 64], T.MR[:, o + side:o + 128:2], A.mult,
+               ["MR%d_%d" % (s, r), "ZQz"], ["ZQ%d_%d" % (s, row)], [2 + s])
+
+    def places(s):
+        p = ps[6 + s]
+        tt(T.ZP[:, 3::4, :], p[:, 0:32], T.E[:], A.max, ["E", "ZPz"], ["ZP"], [6 + s])
+        mm([[(p[:, 64:96], T.ZP[:, 3 - i:35 - i, :], T.R4W[:, 32 * i:32 * (i + 1)]) for i in range(4)]],
+           ["ZP", "R4W"], 6 + s)
+        add("S", T.UP[:, 32 * s:32 * (s + 1)], p[:, 64:96], COL + 16, [], ["UP%d" % s], [6 + s])
+
+    def scatter(s):
+        zk = ["ZQ%d_%d" % (s, 8 * v + 4 * side + r) for r, side, v in ROWS]
+        rk = ["UP%d" % s] + num("Wz", range(4))
+        for lo, hi, b, lay in (((0, 128, 0, "S"),), ((0, 64, 1, "S"), (64, 128, 5, "V")))[s]:
+            mm([[(ps[b][:, 4 * lo + j:4 * hi:4], T.ZQ[:, 128 * s:128 * (s + 1), 2 * j + u], T.I16[:, lo:hi])
+                 for u in range(2)] for j in range(4)], zk + ["I16"], b)
+            rk.append("D%d_%d" % (s, lo))
+            add(lay, T.D[:, 512 * s + 4 * lo:512 * s + 4 * hi], ps[b][:, 4 * lo:4 * hi], LIFT, [], rk[-1:], [b])
+        win, d = T.W[:, :].indirect(T.UP[:, 32 * s:32 * (s + 1)]), T.D[:, 512 * s:512 * (s + 1)]
+        if s == 0:
+            op("S", lambda: S.activation(win, d, AF.Silu), rk, ["W"])
+        else:
+            cp(win, d, rk, ["W"])
 
     def back(x, ch):
         v, o = "ab".index(x), 16 + 1024 * ch
@@ -575,37 +608,55 @@ def rank_program(g, core, T, topo):
         turn(0, "b", False); turn(0, "a", True)
         back("a", 1)
         ulist("S", "b", 1)
-        rows("V", "b", 1, 0, 16); rows("S", "b", 1, 16, 64)
-        decide(0)
+        rows("V", "b", 1, 0, 24); rows("S", "b", 1, 24, 64)
+        masks(0)
+        ulist("S", "a", 1)
+        prods(0, STAY); tlist(0, 2, 6)
+        prods(0, LEFT); prods(0, RIGHT)
+        tlist(0, 0, 7); tlist(0, 1, 7)
+        rows("S", "a", 1, 48, 64); rows("V", "a", 1, 0, 24)
         ut("S", 0, 2, 6)
-        ulist("V", "a", 1)
         ut("V", 0, 0, 7); ut("V", 0, 1, 7)
+        rows("V", "a", 1, 24, 48)
         fixed(0, 0, 16); fixed(0, 16, 32); fixed(0, 32, 64)
-        cands(0); clear(1)
-        turn(1, "b", False)
+        clear(1); turn(1, "b", False); turn(1, "a", True)
+        cands(0)
         test(0, 0, 0, 16); test(0, 1, 0, 16)
-        rows("S", "a", 1, 0, 64)
-        test(0, 0, 16, 32); test(0, 1, 16, 32)
-        turn(1, "a", True)
-        finish(True)
+        finish(True, ((1, 16, 24), (0, 16, 32), (1, 24, 32), (0, 32, 64)))
 
-    def finish(alone):
-        test(0, 0, 32, 64)
+    def finish(alone, rest, x=None):
+        if not x:
+            masks(1)
+            test(0, *rest[0])
+            prods(1, STAY); tlist(1, 2, 6)
+            prods(1, LEFT); prods(1, RIGHT)
+            x = test_s(0, 1, 32, 0, 0)
+            ut("S", 1, 2, 6)
+            tlist(1, 0, 7); tlist(1, 1, 7)
+            cands(1)
+            fixed(1, 32, 64)
+        for r in rest[1:]:
+            test(0, *r)
+        ut("V", 1, 0, 7); ut("V", 1, 1, 7)
         fails(0, 0, 4, alone)
-        test(0, 1, 32, 64)
+        x()
         fails(0, 1, 4, alone)
-        decide(1)
-        ut("S", 1, 2, 6)
-        fixed(1, 0, 16)
-        ut("S", 1, 0, 7); ut("S", 1, 1, 7)
-        cands(1)
-        fixed(1, 16, 32); fixed(1, 32, 64)
-        post(0, (lambda: None, lambda: None, lambda: test(1, 0, 0, 16)))
-        test(1, 1, 0, 16); test(1, 0, 16, 64)
-        fails(1, 0, 5, alone)
-        test(1, 1, 16, 64)
-        fails(1, 1, 5, alone)
-        post(1)
+        fixed(1, 0, 32)
+        test(1, 0, 32, 64); test(1, 1, 32, 48)
+        kept(0); test(1, 1, 48, 56)
+        y = test_s(1, 1, 0, 1, 1)
+        counts(0); test(1, 1, 56, 64)
+        codes(0); test(1, 0, 0, 8)
+        y()
+        ranks(0); test(1, 0, 8, 16)
+        places(0); pack(0, 0, 4)
+        test(1, 0, 16, 32)
+        fails(1, 1, 5, alone, False); fails(1, 0, 5, alone, True)
+        pack(0, 4, 14)
+        scatter(0)
+        kept(1); counts(1); codes(1); ranks(1)
+        pack(1, 0, 4); places(1); pack(1, 4, 14)
+        scatter(1)
 
     def doubled(s, tos):
         masks(s)
@@ -623,19 +674,19 @@ def rank_program(g, core, T, topo):
     spread("S", "b", 0); spread("V", "b", 1)
     pen("b")
     clear(0)
-    rows("S", "a", 0, 0, 32); turn(2, "a", False)
-    counting()
     spread("S", "b", 2); spread("V", "b", 3)
-    table("b", (1, 2, 3, 4, 5, 6, 7, 1), "VSVSVSVS")
+    rows("S", "a", 0, 0, 32)
+    table("b", (1, 2, 3, 4, 5, 6, 7, 1), "VSVSVVSS")
+    turn(2, "a", False)
     rows("V", "b", 0, 16, 32); rows("S", "b", 0, 0, 16); turn(2, "b", True)
-    shifting(0)
+    counting(0)
     doubled(2, ())
     ulist("S", "b", 0); rows("S", "b", 0, 0, 64)
     ulist("V", "a", 0); rows("V", "a", 0, 0, 64)
     turn(3, "b", False); turn(3, "a", True)
     ut("S", 2, 2, 5); ut("S", 2, 0, 4); ut("S", 2, 1, 4)
     fixed(2, 0, 32)
-    shifting(1)
+    counting(1)
     doubled(3, (1,))
     need("Y", ["UL2_0"])
     refill()
@@ -645,54 +696,73 @@ def rank_program(g, core, T, topo):
     ut("S", 3, 2, 5); ut("S", 3, 0, 4); ut("S", 3, 1, 4)
     test(2, 0, 0, 32)
     fixed(3, 0, 32)
+    ulist("S", "b", 1); rows("S", "b", 1, 0, 64)
     decide(0)
     test(2, 1, 0, 32)
     ut("S", 0, 2, 6); ut("S", 0, 0, 7); ut("S", 0, 1, 7)
     fails(2, 0, 4, True); fails(2, 1, 4, True)
     cands(0); clear(1)
+    turn(1, "b", False)
     fixed(0, 0, 32)
     act(T.F1[:], ps[4][:, 0:64], 1.0, [], ["F1"], [4])
+    ulist("S", "a", 1)
+    fixed(3, 32, 64)
+    rows("S", "a", 1, 0, 64)
     test(3, 0, 0, 32); test(3, 1, 0, 32)
-    fixed(3, 32, 64); fixed(0, 32, 64)
-    ulist("S", "b", 1); ulist("S", "a", 1)
-    test(0, 0, 0, 32); test(0, 1, 0, 32)
-    rows("S", "b", 1, 0, 64)
-    turn(1, "b", False)
+    fixed(0, 32, 64)
+    test(0, 0, 0, 32); test(0, 1, 0, 24)
     test(3, 0, 32, 64); test(3, 1, 32, 64)
     carry(3, 4, [(T.IB[:], T.F1[:])], ["F1"])
-    fails(3, 0, 4, False); fails(3, 1, 4, False)
-    rows("S", "a", 1, 0, 64)
-    act(T.F2[:], ps[4][:, 0:128], 1.0, [], ["F2"], [4])
+    fails(3, 0, 4, False)
     turn(1, "a", True)
+    fails(3, 1, 4, False)
+    masks(1)
+    test(0, 1, 24, 32)
+    prods(1, STAY); tlist(1, 2, 6)
+    prods(1, LEFT); prods(1, RIGHT)
+    x = test_s(0, 1, 32, 0, 0)
+    act(T.F2[:], ps[4][:, 0:128], 1.0, [], ["F2"], [4])
+    ut("S", 1, 2, 6)
+    tlist(1, 0, 7); tlist(1, 1, 7)
+    cands(1)
+    fixed(1, 32, 64)
     for s in range(2):
         carry(s, 4 + s, [(T.S2[:, 256 * s + 128 * i:256 * s + 128 * (i + 1)], T.F2[:, i::2, :]) for i in range(2)],
               ["S2", "F2"])
-    finish(False)
+    finish(False, (None, (0, 32, 64)), x)
     for rnd in (4, 5):
         reopen(True)
-        if rnd == 4:
-            closing()
         full()
     reopen(False)
     back("a", 1)
     pieces = ((0, 0, 32), (0, 32, 64), (1, 0, 32), (1, 32, 48), (1, 48, 64))
-    for j, (ch, lo, hi) in enumerate(pieces):
-        if lo == 0:
-            ulist("S", "b", ch); ulist("V", "a", ch)
+    PB = (0, 1, 4, 5, 6)
+
+    def get(j):
+        ch, lo, hi = pieces[j]
+        o, w, b = 1024 * ch + 16 * lo, 16 * (hi - lo), PB[j]
         rows("S", "b", ch, lo, hi); rows("V", "a", ch, lo, hi)
-        for i in [j - 1] * (j > 0) + [j] * (j == 4):
-            c, l, h = pieces[i]
-            move("SV"[i % 2], T.OUT[:, 1024 * c + 16 * l:1024 * c + 16 * h], ps[(0, 1, 4, 5, 0)[i]][:, 0:16 * (h - l)],
-                 [], keys("OUT%d" % c, l, h), [(0, 1, 4, 5, 0)[i]]) if i < j else None
-        o, w, b = 1024 * ch + 16 * lo, 16 * (hi - lo), (0, 1, 4, 5, 0)[j]
         mm([[(ps[b][:, 0:w], T.OB[:], T.MB[:, o:o + w])]], keys("Mb%d" % ch, lo, hi) + ["OB"], b, True, False)
         mm([[(ps[b][:, 0:w], T.OA[:], T.MA[:, o:o + w])]], keys("Ma%d" % ch, lo, hi) + ["OA"], b, False, True)
-        if j == 2:
-            for r, y in enumerate((T.ya, T.yb, T.ys)):
-                dma("Y", y[:, 0:1024], T.OUT[r::16, 0:1024], keys("OUT0", 0, 64), [])
-    move("V", T.OUT[:, 1792:2048], ps[0][:, 0:256], [], keys("OUT1", 48, 64), [0])
-    for r, y in enumerate((T.ya, T.yb, T.ys)):
-        dma("YSY"[r], y[:, 1024:2048], T.OUT[r::16, 1024:2048], keys("OUT1", 0, 64), [])
+
+    def out(e, j):
+        ch, lo, hi = pieces[j]
+        move(e, T.OUT[:, 1024 * ch + 16 * lo:1024 * ch + 16 * hi], ps[PB[j]][:, 0:16 * (hi - lo)], [],
+             keys("OUT%d" % ch, lo, hi), [PB[j]])
+
+    def put(ch, qs):
+        for r, y in enumerate((T.ya, T.yb, T.ys)):
+            dma(qs[r], y[:, 1024 * ch:1024 * (ch + 1)], T.OUT[r::16, 1024 * ch:1024 * (ch + 1)],
+                keys("OUT%d" % ch, 0, 64), [])
+    ulist("S", "b", 0); ulist("V", "a", 0)
+    get(0)
+    ulist("S", "b", 1); ulist("V", "a", 1)
+    get(1); get(2); get(3)
+    out("S", 0); out("S", 1)
+    put(0, "YYY")
+    get(4)
+    out("S", 2); out("V", 3); out("V", 4)
+    put(1, "YSY")
     ends["sent"] = sent[0]
     for s, v in ends.items():
         g.wait_ge(T.sem[s], v)

@@ -9,8 +9,11 @@ BIG = 16.0
 LIFT = 4096.0
 MAGIC = 1.5 * 2.0 ** 27
 SC = 2.0 ** -13
-OPT = {"route": "addd", "order": "k0s123", "split": 1}
-NDMA = 48
+OPT = {"route": "abdd", "order": "k0s123"}
+CYC, HOP, GATHER, SCATTER = 0.92e-3, 0.26, 1.45, 3.8
+LANDS = {"rk": 8.2, "rs": 10.4, "rh": 16.0}
+GATHERED = ("Ma", "Mb", "NF", "FL", "KB", "OB", "OUT")
+NDMA = 40
 
 
 def _sb(n, dt):
@@ -19,16 +22,15 @@ def _sb(n, dt):
 
 SCRATCH = {}
 for _dt, _list in (
-        ("bfloat16", dict(H=2 * SO, relay=SO, Z=1312, IB=128, SF=8, SZ=8, NF=3584, FL=7168, F1=64, F2=[16, 8],
-                          S2=512, KB=1024, ONE=512, CODE=128, J=160, J2=128, J4=128, JT=64)),
+        ("bfloat16", dict(H=2 * SO, Z=1312, IB=128, SF=8, SZ=8, NF=3584, FL=7168, F1=64, F2=[16, 8], S2=512, KB=1024,
+                          ONE=512, CODE=128, J=160, J2=128, J4=128, JT=64)),
         ("float16", dict(W16=2064, MA=2048, MB=2048, I16=128, I8=128, R2=128, R2S=128, R4=128, R4S=128, R4W=128,
-                         LT=128, ON=128, IP=128, IN=128, SA=32, SB=32, OA=128, OB=128, BK=2 * 908, M4=128, M16=128,
+                         LT=128, ON=128, IP=128, IN=128, SA=32, SB=32, I256=128, I2K=128, BK=2 * 908, M4=128, M16=128,
                          CDS=32, C25=32, ZERO=512, PQ=[163, 8], PC0=[81, 16], PC1=[81, 16], ZQ=[256, 8], ZP=[35, 4],
-                         GQ=[65, 8], GC=512,
-                         K=128, C4=128, C16=256, MR=1024, E=32, Ua=512, Ub=512, La=512, Lb=512, Na=512, Nb=512,
-                         Sa=256, Sb=256, Ca=1024, Cb=1024, Za=[136, 16], Zb=[136, 16])),
-        ("float32", dict(TA=4104, TB=4104, W=5152, IDR=256, IDT=256, CD=32, col=64, ZC=516, D=1024, OUT=2048,
-                         st=64)),
+                         GQ=[65, 8], GC=512, K=128, C4=128, C16=256, MR=1024, E=32, Ua=512, Ub=512, La=512, Lb=512,
+                         Na=512, Nb=512, Sa=256, Sb=256, Ca=1024, Cb=1024, Za=[136, 16], Zb=[136, 16])),
+        ("float32", dict(TA=4104, TB=4104, W=5152, IDR=256, IDT=256, CD=32, col=64, ZC=516, D=1024, OUT=2048, OB=2048,
+                         IDN=256, SZU=512, st=64)),
         ("int32", dict(ki=512, sai=64, pci=8)),
         ("uint16", dict(UAB=256, UL=768, UP=64))):
     for _k, _n in _list.items():
@@ -56,7 +58,7 @@ def bits(m):
 
 
 def near_mask(src, helper, dst, topo):
-    return topo.mask(src, helper) & ~topo.mask(src, dst) if OPT["split"] else topo.mask(src, helper)
+    return topo.mask(src, helper) & ~topo.mask(src, dst)
 
 
 def helper_program(g, core, T, topo):
@@ -70,10 +72,58 @@ def helper_program(g, core, T, topo):
                 g.wait_ge(T.sem["hi%d" % k], bits(near_mask(src, core, dst, topo)))
                 rid, pid, _ = topo.addr(dst)
                 m = topo.mask(core, dst)
-                g.remote_dma(T.H[:, SO + q.start:SO + q.stop], T.relay[:, q], T.sem["rh%d" % k], T.sem.hout, pid, rid, m)
+                g.remote_dma(T.H[:, SO + q.start:SO + q.stop], T.H[:, q], T.sem["rh%d" % k], T.sem.hout, pid, rid, m)
                 out += bits(m)
     if out:
         g.wait_ge(T.sem.hout, out)
+
+
+def order(calls, landing):
+    n = len(calls)
+    pre, wr, rd, last = [], {}, {}, {}
+    ready = [0.0] * n
+    for j, (e, _, reads, writes, banks, dur, lat) in enumerate(calls):
+        p = {}
+        for k in reads:
+            if k in wr:
+                p[wr[k]] = HOP
+            ready[j] = max(ready[j], landing.get(k, 0.0))
+        for k in writes:
+            for i in ([wr[k]] if k in wr else []) + rd.get(k, []):
+                p[i] = HOP
+        for b in banks + ([e] if e in "GY" else []):
+            if b in last:
+                p.setdefault(last[b], HOP if calls[last[b]][0] != e else None)
+            last[b] = j
+        for k in reads:
+            rd.setdefault(k, []).append(j)
+        for k in writes:
+            wr[k], rd[k] = j, []
+        p.pop(j, None)
+        pre.append(p)
+    post = [{} for _ in range(n)]
+    for j in range(n):
+        for i, h in pre[j].items():
+            post[i][j] = h
+
+    def place(turns, before, start, back):
+        at, busy = [0.0] * n, {e: [] for e in "VSPGY"}
+        for j in turns:
+            e, dur = calls[j][0], calls[j][5]
+            t = start[j]
+            for i, h in before[j].items():
+                t = max(t, at[i] + calls[i][5] + (0.0 if h is None else h + calls[j if back else i][6]))
+            for k, (a, b) in enumerate(busy[e] + [(1e9, 1e9)]):
+                if t + dur <= a + 1e-9:
+                    break
+                t = max(t, b)
+            busy[e].insert(k, (t, t + dur))
+            at[j] = t
+        return at
+    at = place(range(n), pre, ready, False)
+    back = place(sorted(range(n), key=lambda j: (-at[j] - calls[j][5], -j)), post, [x[6] for x in calls], True)
+    at = place(sorted(range(n), key=lambda j: (-back[j] - calls[j][5], j)), pre, ready, False)
+    return sorted(range(n), key=lambda j: (at[j], j))
 
 
 def rank_program(g, core, T, topo):
@@ -117,59 +167,88 @@ def rank_program(g, core, T, topo):
             bank.setdefault(b, {})[e] = ev
         ends[ev[0]] = max(ends.get(ev[0], 0), ev[1])
 
-    def op(e, fn, reads, writes, banks=()):
+    def issue_op(e, fn, reads, writes, banks):
         need(e, reads, writes, banks)
         cnt[e] += 1
         fn().then_inc(T.sem["c" + e], 1)
         done(e, ("c" + e, cnt[e]), reads, writes, banks)
 
-    def mm(groups, reads, b, opens=True, closes=True):
+    def issue_mm(groups, reads, b, opens, closes):
         need("P", reads, [], [b])
-        for i, grp in enumerate(groups):
+        for grp in groups:
             for j, (o, l, r) in enumerate(grp):
                 last = g.tensor.matmul(o, l, r, opens and j == 0, closes and j == len(grp) - 1)
         cnt["P"] += 1
         last.then_inc(T.sem.cP, 1)
         done("P", ("cP", cnt["P"]), reads, [], [b])
 
-    def dma(e, out, in_, reads, writes):
+    def issue_dma(e, out, in_, reads, writes):
         need(e, reads, writes)
         s = "d%d" % ndma[0]
         ndma[0] += 1
         eng[e].dma_start(out, in_).then_inc(T.sem[s], 16)
         done(e, (s, 16), reads, writes, [])
 
-    def send(to, out, in_, sem, reads, m=None):
+    def issue_send(to, out, in_, sem, reads, m):
         need("G", reads)
         rid, pid, _ = topo.addr(to)
         m = m or topo.mask(core, to)
         g.remote_dma(out, in_, T.sem[sem], T.sem.sent, pid, rid, m)
         sent[0] += bits(m)
 
-    def arrives(key, sem, frm):
-        wr[key] = [(sem, bits(topo.mask(frm, core)))]
-        ends[sem] = wr[key][0][1]
+    calls, landing = [], {}
+
+    def width(ap):
+        w = 1
+        for x in ap.shape[1:]:
+            w *= x
+        return w
+
+    def op(e, fn, reads, writes, banks=(), n=64, per=1.0):
+        if writes[0].startswith(GATHERED) and not banks:
+            per = GATHER
+        calls.append((e, lambda: issue_op(e, fn, reads, writes, banks), reads, writes, list(banks),
+                      max(64, n * per) * CYC + (0.05 if per > 1 else 0.0), 0.0))
+
+    def mm(groups, reads, b, opens=True, closes=True):
+        calls.append(("P", lambda: issue_mm(groups, reads, b, opens, closes), reads, [], [b],
+                      sum(max(64, width(x[0])) for grp in groups for x in grp) * CYC / 2, 0.0))
+
+    def dma(e, out, in_, reads, writes, lat=2.5):
+        calls.append((e, lambda: issue_dma(e, out, in_, reads, writes), reads, writes, [], 0.08, lat))
+
+    def send(to, out, in_, sem, reads, m=None):
+        calls.append(("G", lambda: issue_send(to, out, in_, sem, reads, m), reads, [], [], 0.6, 60.0))
+
+    def arrives(names, sem, frm):
+        for key in names:
+            wr[key] = [(sem, bits(topo.mask(frm, core)))]
+            landing[key] = LANDS[sem[:2]]
+        ends[sem] = bits(topo.mask(frm, core))
 
     def ts(out, in0, s1, s2, o0, o1, reads, writes, banks=()):
-        op("V", lambda: V.tensor_scalar(out, in0, s1, s2, o0, o1), reads, writes, banks)
+        op("V", lambda: V.tensor_scalar(out, in0, s1, s2, o0, o1), reads, writes, banks, width(out),
+           1.0 if banks else 0.5)
 
     def t1(out, in0, s1, o0, reads, writes, banks=()):
-        op("V", lambda: V.tensor_scalar(out, in0, s1, None, o0), reads, writes, banks)
+        op("V", lambda: V.tensor_scalar(out, in0, s1, None, o0), reads, writes, banks, width(out),
+           0.5 if writes[0].startswith("MR") else 1.0)
 
     def tt(out, in0, in1, o, reads, writes, banks=()):
-        op("V", lambda: V.tensor_tensor(out, in0, in1, o), reads, writes, banks)
+        op("V", lambda: V.tensor_tensor(out, in0, in1, o), reads, writes, banks, width(out))
 
     def cp(out, in_, reads, writes, banks=()):
-        op("V", lambda: V.tensor_copy(out, in_), reads, writes, banks)
+        op("V", lambda: V.tensor_copy(out, in_), reads, writes, banks, width(out))
 
     def act(out, in_, scale, reads, writes, banks=()):
-        op("S", lambda: S.activation(out, in_, AF.Copy, scale=scale), reads, writes, banks)
+        op("S", lambda: S.activation(out, in_, AF.Copy, scale=scale), reads, writes, banks, width(out))
 
     def add(e, out, in_, c, reads, writes, banks=()):
         if e == "V":
             t1(out, in_, c, A.add, reads, writes, banks)
         else:
-            op("S", lambda: S.activation(out, in_, AF.Identity, bias=bias[c]), reads + ["bias"], writes, banks)
+            op("S", lambda: S.activation(out, in_, AF.Identity, bias=bias[c]), reads + ["bias"], writes, banks,
+               width(out))
 
     def move(e, out, in_, reads, writes, banks=()):
         if e == "V":
@@ -178,7 +257,7 @@ def rank_program(g, core, T, topo):
             act(out, in_, 1.0, reads, writes, banks)
 
     def fill(out, c, key):
-        op("V", lambda: V.memset(out, c), [], [key])
+        op("V", lambda: V.memset(out, c), [], [key], (), width(out), 0.5)
 
     def keys(name, lo, hi):
         return ["%s_%d" % (name, k) for k in range(lo // 8, (hi + 7) // 8)]
@@ -189,25 +268,26 @@ def rank_program(g, core, T, topo):
     def clear(b, w=448):
         mm([[(ps[b][:, 0:w], T.ZERO[:, 0:128], T.ZERO[:, 0:w])]], ["ZERO"], b, True, False)
 
-    arrives("Ub", "rk", src)
-    arrives("Cb2", "rs", src)
-    wr["Cb3"] = wr["Cb2"]
+    arrives(["Ub"], "rk", src)
+    arrives(["Cb2", "Cb3"], "rs", src)
     for k, h in enumerate(routes(src, core, T, topo)):
-        arrives("Hf%d" % k, "rh%d" % k, src if h is None else h)
-    HALL = num("Ho", range(4)) + num("Hf", range(4)) + ["Hd"]
+        arrives(["Hf%d" % k], "rh%d" % k, src if h is None else h)
 
-    dma("S", T.ki[:, 0:256], T.kl[:], [], ["kl"])
-    dma("Y", T.ki[:, 256:512], T.kr[:], [], ["kr"])
+    def ho(k):
+        return ["Ho%d" % k] + ["Hx%d" % k] * (rank % 2)
+    HALL = [x for k in range(4) for x in ho(k)] + num("Hf", range(4)) + ["Hd"]
+
+    dma("S", T.ki[:, 0:256], T.kl[:], [], ["kl"], 1.9)
+    dma("Y", T.ki[:, 256:512], T.kr[:], [], ["kr"], 1.9)
     for k in range(4):
         c = slice(1024 * k, 1024 * (k + 1))
         if rank % 2 == 0:
-            dma("Y", T.H[:, c], T.h[:, c], [], ["Ho%d" % k])
+            dma("Y", T.H[:, c], T.h[:, c], [], ["Ho%d" % k], 2.6 + 0.7 * k)
         else:
-            dma("Y", T.H[0::2, c], T.h[1::2, c], [], ["Hx"])
-            dma("Y", T.H[1::2, c], T.h[0::2, c], [], ["Ho%d" % k])
-            wr["Ho%d" % k] = wr["Ho%d" % k] + wr.pop("Hx")
-    dma("S", T.sai[:, 0:32], T.sa[:], [], ["sa"])
-    dma("S", T.sai[:, 32:64], T.sb[:], [], ["sb"])
+            dma("Y", T.H[0::2, c], T.h[1::2, c], [], ["Hx%d" % k], 2.6 + 0.7 * k)
+            dma("Y", T.H[1::2, c], T.h[0::2, c], [], ["Ho%d" % k], 2.6 + 0.7 * k)
+    dma("Y", T.sai[:, 0:32], T.sa[:], [], ["sa"], 6.0)
+    dma("Y", T.sai[:, 32:64], T.sb[:], [], ["sb"], 6.0)
 
     op("G", lambda: g.iota(T.pci[:, 0:1], [[1, 1]], 0, 1), [], ["pci0"])
     for t, pat, base, mult, key in (
@@ -216,7 +296,8 @@ def rank_program(g, core, T, topo):
             (T.JT[:, 0:32], [[1, 4], [16, 8]], 0, 0, "JA"), (T.JT[:, 32:64], [[-1, 4], [16, 8]], 3, 0, "JB"),
             (T.J2[:], [[1, 2], [2, 64]], 0, 0, "J2"), (T.J4[:], [[1, 4], [4, 32]], 0, 0, "J4"),
             (T.CD[:], [[0, 8], [2, 4]], HALF + 16, 8, "CD")):
-        op("G", lambda: g.iota(t, pat, base, mult, allow_small_or_imprecise_dtypes=True), [], [key])
+        op("G", lambda a=(t, pat, base, mult): g.iota(*a, allow_small_or_imprecise_dtypes=True), [], [key], (),
+           width(t) + 80, 2.0)
     fill(T.ZERO[:], 0.0, "ZERO")
     clear(6, 512); clear(7, 256)
     col, pci, J = T.col, T.pci, T.J
@@ -231,24 +312,16 @@ def rank_program(g, core, T, topo):
     ts(pci[:, 4:5], pci[:, 0:1], 3, 1, SH, AND, ["pci0"], ["pci4"])
     fill(T.Z[:], 0.0, "Z")
     cp(col[:, 0:5], pci[:, 0:5], num("pci", range(5)) + num("bias", range(4)), ["c_p", "bias"])
-    c_p, c_pm, c_g, c_r, c_v, c_g15, c_gm, c_pp = (col[:, j:j + 1] for j in range(8))
+    c_p, c_pm, c_g, c_r, c_v, c_g17, c_gm, c_pp = (col[:, j:j + 1] for j in range(8))
     oh = [col[:, 8 + j:9 + j] for j in range(16)]
-    fill(T.H[:, M:SO], -262144.0, "Hpad")
     t1(c_gm, c_g, -float(M), A.mult, ["c_p"], ["c_gm"])
     t1(col[:, 8:24], J[:, 0:16], c_pm, A.is_equal, ["J", "c_p"], ["oh"])
     t1(T.I16[:], J[:, 0:128], c_p, A.is_equal, ["J", "c_p"], ["I16"])
+    ts(ps[5][:, 0:256], T.IDR[:], c_gm, 1.0 / HALF, A.add, A.mult, ["IDR", "c_gm"], ["own"], [5])
+    tt(ps[5][:, 0:1], ps[5][:, 0:1], oh[8], A.add, ["own", "oh"], ["own"], [5])
+    t1(T.Ua[:], T.ki[:], -float(HALF), A.add, ["kl", "kr"], ["Ua"])
     ts(T.SZ[:], J[:, 0:8], c_g, 1.0 / 256, A.is_equal, A.mult, ["J", "c_p"], ["SZ"])
     ts(T.I8[:], J[:, 0:128], c_p, -PEN / HALF, A.is_equal, A.mult, ["J", "c_p"], ["I8"])
-    ts(ps[5][:, 0:256], T.IDR[:], c_gm, 1.0 / HALF, A.add, A.mult, ["IDR", "c_gm"], ["own"], [5])
-    for t, w in ((T.PQ, 1304), (T.PC0, 656), (T.PC1, 656)):
-        act(t[:] if t is T.PQ else t[:, 0::2, :], T.Z[:, 0:w], 1.0, ["Z"], [t.name + "z"])
-    act(T.GQ[:, 0::2, :], T.Z[:, 0:264], 1.0, ["Z"], ["GQz"])
-    for z in (T.Za, T.Zb):
-        fill(z[:, 5::8, :], float(HALF), z.name + "5")
-        fill(z[:, 7::8, :], 0.0, z.name + "7")
-        fill(z[:, 128:133, :], 0.0, z.name + "p")
-        fill(z[:, 134:135, :], 0.0, z.name + "q")
-    tt(ps[5][:, 0:1], ps[5][:, 0:1], oh[8], A.add, ["own", "oh"], ["own"], [5])
 
     def kids(x, between=lambda: None):
         U, L, N, Sf = T["U" + x], T["L" + x], T["N" + x], T["S" + x]
@@ -272,16 +345,11 @@ def rank_program(g, core, T, topo):
             move(e, zrow(x, j + 1, h), T["C" + x][:, 256 * j + 128 * h:256 * j + 128 * h + 128], ["C%s%d" % (x, j)],
                  ["Z%s%d_%d" % (x, j + 1, h)])
 
-    def pen(x):
-        for h in range(2):
-            ts(zrow(x, 6, h), T["C" + x][:, 256 + 128 * h:384 + 128 * h], 0.0, -PEN, A.is_equal, A.mult, ["C%s1" % x],
-               ["Z%s6_%d" % (x, h)])
-
     TAB = {"a": T.TA, "b": T.TB}
 
     def table(x, banks, es, qs=range(8)):
         z, t = T["Z" + x], TAB[x]
-        rk = ["Z%s%d_%d" % (x, r, h) for r in (0, 1, 2, 3, 4, 6) for h in range(2)] + num(z.name, "57pq") + ["I16"]
+        rk = ["Z%s%d_%d" % (x, r, h) for r in range(5) for h in range(2)] + num(z.name, "567p") + ["I16"]
         for q in qs:
             mm([[(ps[banks[q]][:, 128 * j:128 * (j + 1)], z[:, 8 * (j % 2):8 * (j % 2) + 128, 2 * q + j // 2], T.I16[:])]
                 for j in range(4)], rk, banks[q])
@@ -290,112 +358,22 @@ def rank_program(g, core, T, topo):
             if lo:
                 t1(t[:, M:M + 1], ps[banks[q]][:, 0:1], col[:, 25:26], A.add, ["fix"], ["T%sd" % x], [banks[q]])
     TK = {x: num("T" + x, range(8)) + ["T%sd" % x, "T%se" % x] for x in "ab"}
-    for x in "ab":
-        t1(TAB[x][:, HALF:HALF + 1], oh[5], -1.0, A.mult, ["oh"], ["T%se" % x])
 
     def sizes(k):
         mm([[(ps[7][:, 128 * h + i:128 * h + 128:16], T.H[:, 256 * i + 128 * h:256 * i + 128 * h + 128], T.SZ[:])
-             for i in range(4 * k, 4 * k + 4) for h in range(2)]], ["SZ", "Ho%d" % k], 7, False, k == 3)
+             for i in range(4 * k, 4 * k + 4) for h in range(2)]], ["SZ"] + ho(k), 7, False, k == 3)
 
-    t1(T.Ua[:], T.ki[:], -float(HALF), A.add, ["kl", "kr"], ["Ua"])
-    for x in "ab":
-        for h in range(2):
-            act(zrow(x, 0, h), T.IDT[:, 128 * h:128 * h + 128], 1.0, ["IDT"], ["Z%s0_%d" % (x, h)])
     kids("a")
     clear(6, 512)
     sizes(0)
     mm([[(ps[7][:, 128 * h:128 * h + 128], T.La[:, 128 * h:128 * h + 128], T.I8[:]) for h in range(2)]], ["La", "I8"], 7,
        False, False)
-    sizes(1)
-    ts(T.st[:], T.sai[:], float(HALF), float(HALF), A.is_equal, A.mult, ["sa", "sb"], ["st"])
-    tt(c_pp, c_p, oh[4], A.subtract, ["c_p", "oh"], ["c_pp"])
-    ts(col[:, 24:25], c_pm, 2.5, -2.0, A.is_gt, A.mult, ["c_p"], ["sg"])
-    tt(col[:, 25:26], oh[0], oh[5], A.subtract, ["oh"], ["fix"])
-    tt(T.st[:], T.st[:], T.sai[:], A.add, ["st"], ["st"])
-    t1(col[:, 24:25], col[:, 24:25], 1.0, A.add, ["sg"], ["sg"])
-    t1(col[:, 25:26], col[:, 25:26], float(HALF), A.mult, ["fix"], ["fix"])
-    t1(T.SA[:], T.JT[:, 0:32], c_pp, A.is_equal, ["JA", "c_pp"], ["SA"])
-    cp(T.UAB[:, 0:32], T.st[:, 0:32], ["st"], ["Ua0"])
-    cp(T.UAB[:, 128:160], T.st[:, 32:64], ["st"], ["Ub0"])
-    ts(T.SB[:], T.JT[:, 32:64], c_pp, col[:, 24:25], A.is_equal, A.mult, ["JB", "c_pp", "sg"], ["SB"])
-
-    def counting(step):
-        if step:
-            fill(T.M4[:], 1.0, "M4"); fill(T.M16[:], 1.0, "M16")
-            fill(T.ZQ[:, 3::8, :], 0.0, "ZQz")
-            fill(T.ZP[:], 0.0, "ZPz")
-            fill(T.M4[:, 0:128:4], 0.0, "M4"); fill(T.M16[:, 0:128:16], 0.0, "M16")
-            return
-        ts(T.LT[:], J[:, 0:128], c_p, SC, A.is_gt, A.mult, ["J", "c_p"], ["LT"])
-        fill(T.ON[:], SC, "ON")
-        t1(T.IP[:], T.I16[:], SC, A.mult, ["I16"], ["IP"])
-        t1(T.IN[:], T.I16[:], -SC, A.mult, ["I16"], ["IN"])
-        fill(T.C25[:], -HALF * SC, "C25")
-        t1(T.CDS[:], T.CD[:], SC, A.mult, ["CD"], ["CDS"])
-
-    EDGE = (15, 14, 13, -1, -2, -3)
-
-    def bk(v, w):
-        if w in EDGE:
-            o = 908 * v + 140 + 128 * EDGE.index(w)
-            return T.BK[:, o:o + 128]
-        return T.BK[:, 908 * v + 12 - w:908 * v + 140 - w]
-
-    def aims():
-        ts(c_g15, c_g, 16.0, 17.0, A.mult, A.add, ["c_p"], ["c_g15"])
-        t1(col[:, 28:30], J[:, 0:2], c_v, A.is_equal, ["J", "c_p"], ["ov"])
-        t1(col[:, 32:35], J[:, 0:3], c_r, A.is_ge, ["J", "c_p"], ["mle"])
-        t1(col[:, 35:38], J[:, 1:4], c_r, A.is_le, ["J", "c_p"], ["mge"])
-        closing(0)
-        tt(col[:, 26:27], c_g15, c_r, A.add, ["c_g15", "c_p"], ["tg0"])
-        for t, j, w in ((T.R2, T.J2, 1.0), (T.R2S, T.J2, SO), (T.R4, T.J4, 1.0), (T.R4S, T.J4, SO),
-                        (T.R4W, T.J4, 1 / SC)):
-            ts(t[:], j[:], c_p, float(w), A.is_equal, A.mult, [j.name, "c_p"], [t.name])
-        ts(col[:, 30:32], col[:, 28:30], col[:, 26:27], -1.0, A.mult, A.add, ["ov", "tg0"], ["tg"])
-
-    def shifting(v):
-        t1(T.BK[:, 908 * v:908 * v + 140], J[:, 4:144], col[:, 30 + v:31 + v], A.is_equal, ["J", "tg"],
-           ["BK%d" % (7 * v)])
-        for j, w in enumerate(EDGE):
-            ts(bk(v, w), J[:, 16 - w:144 - w], col[:, 30 + v:31 + v], col[:, 32 + j:33 + j], A.is_equal, A.mult,
-               ["J", "tg", "mle", "mge"], ["BK%d" % (7 * v + 1 + j)])
-
-    def closing(step):
-        c = [col[:, 40 + j:41 + j] for j in range(8)]
-        if step == 0:
-            tt(c[0], oh[0], oh[5], A.add, ["oh"], ["z0"])
-            ts(c[2], oh[3], oh[4], oh[6], A.add, A.subtract, ["oh"], ["z2"])
-            ts(c[3], oh[3], oh[4], oh[6], A.add, A.add, ["oh"], ["z3"])
-        elif step == 1:
-            ts(c[4], c[2], 256.0, c[0], A.mult, A.add, ["z2", "z0"], ["z4"])
-            ts(c[5], c[3], 2.0, c_g15, A.mult, A.add, ["z3", "c_g15"], ["z5"])
-        elif step == 2:
-            tt(c[6], c[5], c[0], A.add, ["z5", "z0"], ["z6"])
-            ts(T.OA[:], J[:, 17:145], c[5], c[4], A.is_equal, A.mult, ["J", "z5", "z4"], ["OA"])
-        else:
-            ts(T.OB[:], J[:, 17:145], c[6], c[4], A.is_equal, A.mult, ["J", "z6", "z4"], ["OB"])
-
-    def refill():
-        for k in range(4):
-            dma("Y", T.W[:, 516 * k:516 * (k + 1)], T.ZC[:], ["ZC"], ["Wz%d" % k])
-
-    spread("S", "a", 0); spread("S", "a", 1)
-    op("S", lambda: S.activation(T.ZC[:], T.Z[:, 0:516], AF.Silu, bias=bias[LIFT]), ["Z", "bias"], ["ZC"])
-    aims()
-    closing(1)
-    pen("a")
-    sizes(2)
-    cp(T.H[:, M:M + 1], T.H[:, HALF:HALF + 1], ["Ho2", "Hpad"], ["Hd"])
-    shifting(0)
-    closing(2)
+    sizes(1); sizes(2)
+    fill(T.H[:, M:SO], -262144.0, "Hpad")
+    cp(T.H[:, M:M + 1], T.H[:, HALF:HALF + 1], ho(2) + ["Hpad"], ["Hd"])
     fill(T.H[:, HALF:HALF + 1], -262144.0, "Ho2")
-    shifting(1)
-    closing(3)
     sizes(3)
     ts(T.Ca[:, 512:768], ps[7][:, 0:256], MAGIC, -MAGIC, A.add, A.add, [], ["Ca2"], [7])
-    ts(T.SF[:], J[:, 0:8], c_g, BIG, A.is_equal, A.mult, ["J", "c_p"], ["SF"])
-    t1(T.IB[:], J[:, 0:128], c_p, A.is_equal, ["J", "c_p"], ["IB"])
-    fill(T.ONE[:], 1.0, "ONE")
     tt(T.Ca[:, 768:1024], ps[7][:, 0:256], T.Ca[:, 512:768], A.subtract, ["Ca2"], ["Ca3"], [7])
     rt = routes(core, dst, T, topo)
     for x in OPT["order"]:
@@ -405,17 +383,77 @@ def rank_program(g, core, T, topo):
             send(dst, T.Cb[:, 512:1024], T.Ca[:, 512:1024], "rs", ["Ca2", "Ca3"])
         else:
             q = quarter(int(x))
-            rk = ["Ho" + x] + (["Hd"] if x == "3" else [])
+            rk = ho(int(x)) + (["Hd"] if x == "3" else [])
             if rt[int(x)] is None:
                 send(dst, T.H[:, SO + q.start:SO + q.stop], T.H[:, q], "rh" + x, rk)
             else:
-                send(rt[int(x)], T.relay[:, q], T.H[:, q], "hi" + x, rk, near_mask(core, rt[int(x)], dst, topo))
-    op("G", lambda: g.affine_select(T.S2[:], T.ONE[:], [[128, 2], [-1, 2], [1, 128]], A.is_equal, 0.0, 0, -2),
-       ["ONE"], ["S2"])
+                send(rt[int(x)], T.H[:, q], T.H[:, q], "hi" + x, rk, near_mask(core, rt[int(x)], dst, topo))
+    for x in "ab":
+        z = T["Z" + x]
+        for h in range(2):
+            act(zrow(x, 0, h), T.IDT[:, 128 * h:128 * h + 128], 1.0, ["IDT"], ["Z%s0_%d" % (x, h)])
+        for r in (5, 6, 7):
+            fill(z[:, r::8, :], 0.0, z.name + str(r))
+        fill(z[:, 128:133, :], 0.0, z.name + "p")
+        fill(TAB[x][:, HALF:HALF + 1], 0.0, "T%se" % x)
+    t1(col[:, 25:26], oh[0], float(HALF), A.mult, ["oh"], ["fix"])
+    for t, w in ((T.PQ, 1304), (T.PC0, 656), (T.PC1, 656)):
+        act(t[:] if t is T.PQ else t[:, 0::2, :], T.Z[:, 0:w], 1.0, ["Z"], [t.name + "z"])
+    act(T.GQ[:, 0::2, :], T.Z[:, 0:264], 1.0, ["Z"], ["GQz"])
+    spread("S", "a", 0); spread("S", "a", 1)
+    op("S", lambda: S.activation(T.ZC[:], T.Z[:, 0:516], AF.Silu, bias=bias[LIFT]), ["Z", "bias"], ["ZC"], (), 2000)
     spread("S", "a", 2); spread("V", "a", 3)
-    table("a", (0, 1, 2, 3, 4, 7, 0, 1), "SSSSVVVV", range(4))
-    kids("b", lambda: table("a", (0, 1, 2, 3, 4, 7, 0, 1), "SSSSVVVV", range(4, 6)))
-    table("a", (0, 1, 2, 3, 4, 7, 0, 1), "SSSSVVVV", range(6, 8))
+    kids("b", lambda: table("a", (0, 1, 2, 3, 4, 7, 0, 1), "SVSSVSVS", range(3)))
+    table("a", (0, 1, 2, 3, 4, 7, 0, 1), "SVSSVSVS", range(3, 8))
+    ts(T.st[:], T.sai[:], float(HALF), float(HALF), A.is_equal, A.mult, ["sa", "sb"], ["st"])
+    tt(T.st[:], T.st[:], T.sai[:], A.add, ["st"], ["st"])
+    cp(T.UAB[:, 0:32], T.st[:, 0:32], ["st"], ["Ua0"])
+    cp(T.UAB[:, 128:160], T.st[:, 32:64], ["st"], ["Ub0"])
+    tt(c_pp, c_p, oh[4], A.subtract, ["c_p", "oh"], ["c_pp"])
+    ts(col[:, 24:25], c_pm, 2.5, -2.0, A.is_gt, A.mult, ["c_p"], ["sg"])
+    t1(col[:, 24:25], col[:, 24:25], 1.0, A.add, ["sg"], ["sg"])
+    t1(T.SA[:], T.JT[:, 0:32], c_pp, A.is_equal, ["JA", "c_pp"], ["SA"])
+    ts(T.SB[:], T.JT[:, 32:64], c_pp, col[:, 24:25], A.is_equal, A.mult, ["JB", "c_pp", "sg"], ["SB"])
+    for t, j, w in ((T.R2, T.J2, 1.0), (T.R2S, T.J2, SO), (T.R4, T.J4, 1.0), (T.R4S, T.J4, SO), (T.R4W, T.J4, 1 / SC),
+                    (T.I256, J, 256.0), (T.I2K, J, PEN / 8), (T.IB, J, 1.0), (T.IP, J, SC), (T.IN, J, -SC)):
+        ts(t[:], j[:, 0:128], c_p, float(w), A.is_equal, A.mult, [j.name, "c_p"], [t.name])
+    ts(T.SF[:], J[:, 0:8], c_g, BIG, A.is_equal, A.mult, ["J", "c_p"], ["SF"])
+    ts(T.LT[:], J[:, 0:128], c_p, SC, A.is_gt, A.mult, ["J", "c_p"], ["LT"])
+    t1(T.CDS[:], T.CD[:], SC, A.mult, ["CD"], ["CDS"])
+    ts(T.IDN[:], T.IDR[:], c_gm, float(HALF), A.add, A.add, ["IDR", "c_gm"], ["IDN"])
+    for t, c, key in ((T.ON[:], SC, "ON"), (T.C25[:], -HALF * SC, "C25"), (T.ONE[:], 1.0, "ONE"), (T.M4[:], 1.0, "M4"),
+                      (T.M16[:], 1.0, "M16"), (T.ZQ[:, 3::8, :], 0.0, "ZQz"), (T.ZP[:], 0.0, "ZPz"),
+                      (T.M4[:, 0:128:4], 0.0, "M4"), (T.M16[:, 0:128:16], 0.0, "M16")):
+        fill(t, c, key)
+    op("G", lambda: g.affine_select(T.S2[:], T.ONE[:], [[128, 2], [-1, 2], [1, 128]], A.is_equal, 0.0, 0, -2),
+       ["ONE"], ["S2"], (), 600, 2.0)
+    EDGE = (15, 14, 13, -1, -2, -3)
+
+    def bk(v, w):
+        o = 908 * v + (140 + 128 * EDGE.index(w) if w in EDGE else 12 - w)
+        return T.BK[:, o:o + 128]
+    ts(c_g17, c_g, 16.0, 17.0, A.mult, A.add, ["c_p"], ["c_g17"])
+    t1(col[:, 28:30], J[:, 0:2], c_v, A.is_equal, ["J", "c_p"], ["ov"])
+    t1(col[:, 32:35], J[:, 0:3], c_r, A.is_ge, ["J", "c_p"], ["mle"])
+    t1(col[:, 35:38], J[:, 1:4], c_r, A.is_le, ["J", "c_p"], ["mge"])
+    tt(col[:, 26:27], c_g17, c_r, A.add, ["c_g17", "c_p"], ["tg0"])
+    ts(col[:, 30:32], col[:, 28:30], col[:, 26:27], -1.0, A.mult, A.add, ["ov", "tg0"], ["tg"])
+    for v in range(2):
+        t1(T.BK[:, 908 * v:908 * v + 140], J[:, 4:144], col[:, 30 + v:31 + v], A.is_equal, ["J", "tg"], ["BK%d" % (7 * v)])
+        for j, w in enumerate(EDGE):
+            ts(bk(v, w), J[:, 16 - w:144 - w], col[:, 30 + v:31 + v], col[:, 32 + j:33 + j], A.is_equal, A.mult,
+               ["J", "tg", "mle", "mge"], ["BK%d" % (7 * v + 1 + j)])
+
+    def true_sizes(j, x):
+        C, out = T["C" + x], ps[2 + j]
+        mm([[(out[:, 0:256], T.I2K[:], T["L" + x][:, 0:256])]
+            + [(out[:, 128 * h:128 * h + 128], C[:, o + 128 * h:o + 128 * h + 128], T.I256[:])
+               for o in (512, 768) for h in range(2)]], ["I2K", "I256", "L" + x, "C%s2" % x, "C%s3" % x], 2 + j)
+        act(T.SZU[:, 256 * j:256 * (j + 1)], out[:, 0:256], 1.0, [], ["SZU" + x], [2 + j])
+
+    def refill(after=()):
+        for k in range(4):
+            dma("Y", T.W[:, 516 * k:516 * (k + 1)], T.ZC[:], ["ZC"] + list(after), ["Wz%d" % k], 3.0 + k)
 
     NB, CH = (8, 8, 4, 8), (0, 1, 0, 0)
     PT = (T.PC0, T.PC1, T.PQ, T.PC0)
@@ -427,10 +465,14 @@ def rank_program(g, core, T, topo):
         add(e, T.UAB[:, UO[x] + 64 * ch:UO[x] + 64 * ch + 64], ps[LB[x][ch]][:, 448:512], COL, [], ["U%s%d" % (x, ch)],
             [LB[x][ch]])
 
+    def tab(x, ch, lo, hi):
+        u = UO[x] + 64 * ch
+        return TAB[x][:, 0:M + 1].indirect(T.UAB[:, u + lo:u + hi])
+
     def rows(e, x, ch, lo, hi):
-        o, u = 1024 * ch, UO[x] + 64 * ch
-        move(e, MX[x][:, o + 16 * lo:o + 16 * hi], TAB[x][:, 0:M + 1].indirect(T.UAB[:, u + lo:u + hi]),
-             TK[x] + ["U%s%d" % (x, ch)], keys("M%s%d" % (x, ch), lo, hi))
+        o = 1024 * ch
+        move(e, MX[x][:, o + 16 * lo:o + 16 * hi], tab(x, ch, lo, hi), TK[x] + ["U%s%d" % (x, ch)],
+             keys("M%s%d" % (x, ch), lo, hi))
 
     def turn(s, x, closes):
         B, ch = NB[s], CH[s]
@@ -446,6 +488,7 @@ def rank_program(g, core, T, topo):
         return PT[s][:, 8 * U * k + U - 1:8 * U * (k + 1):U, side::2]
 
     MASK, KA, KB, XA, XB = range(5)
+    STAY, LEFT, RIGHT = ((XB, 0), (XA, 0)), ((KA, 0), (KB, 0)), ((KA, 1), (KB, 1))
 
     def val(s, v):
         return ps[CH[s]][:, 8 * NB[s] * v:8 * NB[s] * (v + 1)]
@@ -502,12 +545,19 @@ def rank_program(g, core, T, topo):
         tt(T.FL[:, f + 16 * lo:f + 16 * hi], T.H[:, :].indirect(T.UL[:, u + lo:u + hi]), T.NF[:, o + 16 * lo:o + 16 * hi],
            A.is_lt, HALL + ["UL%d_%d" % (s, side)] + keys("NF%d" % s, lo, hi), keys("FL%d_%d" % (s, side), lo, hi))
 
-    def carry(s, b, terms, reads):
-        N = 16 * NB[s]
-        mm([[(ps[b][:, 0:N], T.IB[:], T.Z[:, 0:N])]
-            + [(ps[b][:, side:N:2], l, r) for side in range(2) for l, r in terms]], ["IB", "Z"] + reads, b, True, False)
+    def test_s(s, side, lo, hi, b):
+        o, u, f, w = NFO[s] + 16 * lo, 192 * s + 64 * side, FLO[s] + 128 * NB[s] * side + 16 * lo, 16 * (hi - lo)
+        kb, out = T.KB[:, 512 * b:512 * b + w], ps[b][:, 0:w]
+        act(kb, T.H[:, :].indirect(T.UL[:, u + lo:u + hi]), -1.0, HALL + ["UL%d_%d" % (s, side)], ["KB%d" % b])
+        mm([[(out, T.IB[:], T.NF[:, o:o + w]), (out, T.IB[:], kb)]], ["KB%d" % b, "IB"] + keys("NF%d" % s, lo, hi), b)
+        return lambda: op("S", lambda: S.activation(T.FL[:, f:f + w], out, AF.Relu), [],
+                          keys("FL%d_%d" % (s, side), lo, hi), [b], w)
 
-    def fails(s, side, b, alone, closes=None):
+    def carry(b, terms, reads):
+        mm([[(ps[b][:, 0:128], T.IB[:], T.Z[:, 0:128])]
+            + [(ps[b][:, side:128:2], l, r) for side in range(2) for l, r in terms]], ["IB", "Z"] + reads, b, True, False)
+
+    def fails(s, side, b, alone, closes):
         B = NB[s]
         f = FLO[s] + 128 * B * side
         x = [(ps[b][:, 2 * j + side:16 * B:2 * B], T.FL[:, f + j:f + 128 * B:B], T.SF[:]) for j in range(B)]
@@ -515,30 +565,23 @@ def rank_program(g, core, T, topo):
         if alone:
             mm([[y] for y in x], rk, b)
         else:
-            mm([x], rk, b, False, side == 1 if closes is None else closes)
-
-    def scan(out, m, key):
-        op("V", lambda: V.tensor_tensor_scan(out, m[:], T.K[:], 0.0, A.mult, A.add), ["K", m.name], [key])
-
-    def test_s(s, side, lo, j, b):
-        o, u, f = NFO[s] + 16 * lo, 192 * s + 64 * side + lo, FLO[s] + 128 * NB[s] * side + 16 * lo
-        kb, out = T.KB[:, 512 * j:512 * (j + 1)], ps[b][:, 0:512]
-        act(kb, T.H[:, :].indirect(T.UL[:, u:u + 32]), -1.0, HALL + ["UL%d_%d" % (s, side)], ["KB%d" % j])
-        mm([[(out, T.IB[:], T.NF[:, o:o + 512]), (out, T.IB[:], kb)]],
-           ["KB%d" % j, "IB"] + keys("NF%d" % s, lo, lo + 32), b)
-        return lambda: op("S", lambda: S.activation(T.FL[:, f:f + 512], out, AF.Relu), [],
-                          keys("FL%d_%d" % (s, side), lo, lo + 32), [b])
+            mm([x], rk, b, False, closes)
 
     def kept(s):
         t1(T.K[:], ps[4 + s][:, 0:128], 0.0, A.is_equal, [], ["K"], [4 + s])
 
     def counts(s):
-        scan(T.C4[:], T.M4, "C4")
-        scan(T.C16[:, 128 * s:128 * (s + 1)], T.M16, "C16_%d" % s)
+        for out, m, key in ((T.C4[:], T.M4, "C4"), (T.C16[:, 128 * s:128 * (s + 1)], T.M16, "C16_%d" % s)):
+            op("V", lambda out=out, m=m: V.tensor_tensor_scan(out, m[:], T.K[:], 0.0, A.mult, A.add), ["K", m.name], [key])
 
     def codes(s):
         p = ps[6 + s]
-        tt(T.CODE[:], ps[4 + s][:, 0:128], T.C4[:], A.add, ["C4"], ["CODE"], [4 + s])
+        if s == 0:
+            tt(T.CODE[:], ps[4][:, 0:128], T.C4[:], A.add, ["C4"], ["CODE"], [4])
+        else:
+            for j in range(4):
+                c = ps[3][:, 64 * j:64 * j + 64]
+                tt(c, c, T.K[:, j % 2:128:2], A.mult, ["K"], ["CV%d" % j], [3])
         tt(T.E[:], T.CDS[:], T.C4[:, 3:128:4], A.subtract, ["CDS", "C4"], ["E"])
         x = [(p[:, 0:32], T.I16[:], T.C25[:]), (p[:, 0:32], T.IP[:], T.C16[:, 128 * s + 3:128 * s + 128:4]),
              (p[:, 0:32], T.IN[:], T.C4[:, 3:128:4])]
@@ -549,7 +592,8 @@ def rank_program(g, core, T, topo):
     def ranks(s):
         for r in range(4):
             o = 512 * s + 128 * r
-            t1(T.MR[:, o:o + 128], T.CODE[:], r + 1.0, A.is_equal, ["CODE"], ["MR%d_%d" % (s, r)])
+            c = (T.CODE, T.C4)[s]
+            t1(T.MR[:, o:o + 128], c[:], r + 1.0, A.is_equal, [c.name], ["MR%d_%d" % (s, r)])
 
     ROWS = [(r, side, v) for r in range(4) for side in range(2) for v in range(2) if r < 3 or side]
 
@@ -557,28 +601,28 @@ def rank_program(g, core, T, topo):
         for r, side, v in ROWS[lo:hi]:
             row, o, c = 8 * v + 4 * side + r, 512 * s + 128 * r, 128 * v + 64 * side
             tt(T.ZQ[:, 128 * s + row:128 * (s + 1):16, :], ps[2 + s][:, c:c + 64], T.MR[:, o + side:o + 128:2], A.mult,
-               ["MR%d_%d" % (s, r), "ZQz"], ["ZQ%d_%d" % (s, row)], [2 + s])
+               ["MR%d_%d" % (s, r), "ZQz"] + ["CV%d" % (c // 64)] * s, ["ZQ%d_%d" % (s, row)], [2 + s])
 
     def places(s):
         p = ps[6 + s]
         tt(T.ZP[:, 3::4, :], p[:, 0:32], T.E[:], A.max, ["E", "ZPz"], ["ZP"], [6 + s])
         mm([[(p[:, 64:96], T.ZP[:, 3 - i:35 - i, :], T.R4W[:, 32 * i:32 * (i + 1)]) for i in range(4)]],
            ["ZP", "R4W"], 6 + s)
-        add("S", T.UP[:, 32 * s:32 * (s + 1)], p[:, 64:96], COL + 16, [], ["UP%d" % s], [6 + s])
+        add("SV"[s], T.UP[:, 32 * s:32 * (s + 1)], p[:, 64:96], COL + 16, [], ["UP%d" % s], [6 + s])
 
     def scatter(s):
         zk = ["ZQ%d_%d" % (s, 8 * v + 4 * side + r) for r, side, v in ROWS]
         rk = ["UP%d" % s] + num("Wz", range(4))
-        for lo, hi, b, lay in (((0, 128, 0, "S"),), ((0, 64, 1, "S"), (64, 128, 5, "V")))[s]:
+        for lo, hi, b in (((0, 128, 0),), ((0, 64, 1), (64, 128, 5)))[s]:
             mm([[(ps[b][:, 4 * lo + j:4 * hi:4], T.ZQ[:, 128 * s:128 * (s + 1), 2 * j + u], T.I16[:, lo:hi])
                  for u in range(2)] for j in range(4)], zk + ["I16"], b)
             rk.append("D%d_%d" % (s, lo))
-            add(lay, T.D[:, 512 * s + 4 * lo:512 * s + 4 * hi], ps[b][:, 4 * lo:4 * hi], LIFT, [], rk[-1:], [b])
+            add("SV"[s], T.D[:, 512 * s + 4 * lo:512 * s + 4 * hi], ps[b][:, 4 * lo:4 * hi], LIFT, [], rk[-1:], [b])
         win, d = T.W[:, :].indirect(T.UP[:, 32 * s:32 * (s + 1)]), T.D[:, 512 * s:512 * (s + 1)]
         if s == 0:
-            op("S", lambda: S.activation(win, d, AF.Silu), rk, ["W"])
+            op("S", lambda: S.activation(win, d, AF.Silu), rk, ["W"], (), 512, SCATTER)
         else:
-            cp(win, d, rk, ["W"])
+            op("V", lambda: V.tensor_copy(win, d), rk, ["W"], (), 512, SCATTER)
 
     def back(x, ch):
         v, o = "ab".index(x), 16 + 1024 * ch
@@ -595,16 +639,26 @@ def rank_program(g, core, T, topo):
             refill()
         back("b", 0); back("a", 0); back("b", 1)
 
-    STAY, LEFT, RIGHT = ((XB, 0), (XA, 0)), ((KA, 0), (KB, 0)), ((KA, 1), (KB, 1))
-
     def decide(s):
         masks(s); prods(s, STAY); tlist(s, 2, 6)
         prods(s, LEFT); prods(s, RIGHT)
         tlist(s, 0, 7); tlist(s, 1, 7)
 
-    def full():
-        ulist("S", "b", 0); rows("S", "b", 0, 0, 48); rows("V", "b", 0, 48, 64)
-        ulist("V", "a", 0); rows("V", "a", 0, 0, 48); rows("S", "a", 0, 48, 64)
+    def last_rows():
+        for j, x in enumerate("ab"):
+            t, rk = TAB[x], ["T%s0" % x, "T%s1" % x]
+            dma("Y", t[5 + j::16, 0:M], T.IDN[:], ["IDN"], rk[:1])
+            dma("Y", t[7::16, 0:M], T.SZU[:, 256 * j:256 * (j + 1)], ["SZU" + x], rk[1:])
+
+    def last_columns():
+        for j, x in enumerate("ab"):
+            t, rk = TAB[x], ["T%s0" % x, "T%s1" % x]
+            cp(t[:, M:M + 1], t[:, HALF:HALF + 1], rk, ["T%sd" % x])
+            t1(t[:, HALF:HALF + 1], oh[5 + j], -1.0, A.mult, rk + ["T%sd" % x], ["T%se" % x])
+
+    def full(last):
+        ulist("S", "b", 0); rows("S", "b", 0, 0, 40); rows("V", "b", 0, 40, 48)
+        ulist("V", "a", 0); rows("V", "b", 0, 48, 64); rows("V", "a", 0, 0, 40); rows("S", "a", 0, 40, 64)
         turn(0, "b", False); turn(0, "a", True)
         back("a", 1)
         ulist("S", "b", 1)
@@ -621,38 +675,42 @@ def rank_program(g, core, T, topo):
         fixed(0, 0, 16); fixed(0, 16, 32); fixed(0, 32, 64)
         clear(1); turn(1, "b", False); turn(1, "a", True)
         cands(0)
+        if last:
+            last_rows()
         test(0, 0, 0, 16); test(0, 1, 0, 16)
-        finish(True, ((1, 16, 24), (0, 16, 32), (1, 24, 32), (0, 32, 64)))
+        masks(1)
+        test(0, 1, 16, 24)
+        prods(1, STAY); tlist(1, 2, 6)
+        prods(1, LEFT); prods(1, RIGHT)
+        x = test_s(0, 1, 32, 64, 0)
+        ut("S", 1, 2, 6)
+        tlist(1, 0, 7); tlist(1, 1, 7)
+        cands(1)
+        fixed(1, 32, 64)
+        test(0, 0, 16, 32); test(0, 1, 24, 32)
+        finish(True, x)
+        if last:
+            last_columns()
 
-    def finish(alone, rest, x=None):
-        if not x:
-            masks(1)
-            test(0, *rest[0])
-            prods(1, STAY); tlist(1, 2, 6)
-            prods(1, LEFT); prods(1, RIGHT)
-            x = test_s(0, 1, 32, 0, 0)
-            ut("S", 1, 2, 6)
-            tlist(1, 0, 7); tlist(1, 1, 7)
-            cands(1)
-            fixed(1, 32, 64)
-        for r in rest[1:]:
-            test(0, *r)
+    def finish(alone, x):
+        test(0, 0, 32, 64)
         ut("V", 1, 0, 7); ut("V", 1, 1, 7)
-        fails(0, 0, 4, alone)
+        fails(0, 0, 4, alone, False)
         x()
-        fails(0, 1, 4, alone)
+        fails(0, 1, 4, alone, True)
         fixed(1, 0, 32)
         test(1, 0, 32, 64); test(1, 1, 32, 48)
         kept(0); test(1, 1, 48, 56)
-        y = test_s(1, 1, 0, 1, 1)
+        y = test_s(1, 1, 0, 32, 1)
         counts(0); test(1, 1, 56, 64)
-        codes(0); test(1, 0, 0, 8)
-        y()
-        ranks(0); test(1, 0, 8, 16)
-        places(0); pack(0, 0, 4)
+        z = test_s(1, 0, 0, 16, 0)
+        codes(0)
+        y(); z()
+        ranks(0)
+        places(0); pack(0, 0, 8)
         test(1, 0, 16, 32)
         fails(1, 1, 5, alone, False); fails(1, 0, 5, alone, True)
-        pack(0, 4, 14)
+        pack(0, 8, 14)
         scatter(0)
         kept(1); counts(1); codes(1); ranks(1)
         pack(1, 0, 4); places(1); pack(1, 4, 14)
@@ -672,24 +730,21 @@ def rank_program(g, core, T, topo):
             tlist(s, j, 4 + (j == 2))
 
     spread("S", "b", 0); spread("V", "b", 1)
-    pen("b")
     clear(0)
     spread("S", "b", 2); spread("V", "b", 3)
     rows("S", "a", 0, 0, 32)
-    table("b", (1, 2, 3, 4, 5, 6, 7, 1), "VSVSVVSS")
+    table("b", (2, 3, 4, 7, 5, 6, 1, 2), "VSVSVSVS")
     turn(2, "a", False)
     rows("V", "b", 0, 16, 32); rows("S", "b", 0, 0, 16); turn(2, "b", True)
-    counting(0)
+    true_sizes(0, "a"); true_sizes(1, "b")
     doubled(2, ())
     ulist("S", "b", 0); rows("S", "b", 0, 0, 64)
     ulist("V", "a", 0); rows("V", "a", 0, 0, 64)
     turn(3, "b", False); turn(3, "a", True)
     ut("S", 2, 2, 5); ut("S", 2, 0, 4); ut("S", 2, 1, 4)
     fixed(2, 0, 32)
-    counting(1)
     doubled(3, (1,))
-    need("Y", ["UL2_0"])
-    refill()
+    refill(["UL2_0"])
     ulist("S", "b", 0); rows("S", "b", 0, 0, 64)
     ulist("V", "a", 0); rows("V", "a", 0, 0, 64)
     turn(0, "b", False); turn(0, "a", True)
@@ -700,7 +755,7 @@ def rank_program(g, core, T, topo):
     decide(0)
     test(2, 1, 0, 32)
     ut("S", 0, 2, 6); ut("S", 0, 0, 7); ut("S", 0, 1, 7)
-    fails(2, 0, 4, True); fails(2, 1, 4, True)
+    fails(2, 0, 4, True, True); fails(2, 1, 4, True, True)
     cands(0); clear(1)
     turn(1, "b", False)
     fixed(0, 0, 32)
@@ -712,57 +767,50 @@ def rank_program(g, core, T, topo):
     fixed(0, 32, 64)
     test(0, 0, 0, 32); test(0, 1, 0, 24)
     test(3, 0, 32, 64); test(3, 1, 32, 64)
-    carry(3, 4, [(T.IB[:], T.F1[:])], ["F1"])
-    fails(3, 0, 4, False)
     turn(1, "a", True)
-    fails(3, 1, 4, False)
+    carry(4, [(T.IB[:], T.F1[:])], ["F1"])
+    fails(3, 0, 4, False, False); fails(3, 1, 4, False, True)
     masks(1)
     test(0, 1, 24, 32)
     prods(1, STAY); tlist(1, 2, 6)
     prods(1, LEFT); prods(1, RIGHT)
-    x = test_s(0, 1, 32, 0, 0)
+    x = test_s(0, 1, 32, 64, 0)
     act(T.F2[:], ps[4][:, 0:128], 1.0, [], ["F2"], [4])
     ut("S", 1, 2, 6)
     tlist(1, 0, 7); tlist(1, 1, 7)
     cands(1)
     fixed(1, 32, 64)
     for s in range(2):
-        carry(s, 4 + s, [(T.S2[:, 256 * s + 128 * i:256 * s + 128 * (i + 1)], T.F2[:, i::2, :]) for i in range(2)],
+        carry(4 + s, [(T.S2[:, 256 * s + 128 * i:256 * s + 128 * (i + 1)], T.F2[:, i::2, :]) for i in range(2)],
               ["S2", "F2"])
-    finish(False, (None, (0, 32, 64)), x)
+    finish(False, x)
     for rnd in (4, 5):
         reopen(True)
-        full()
+        full(rnd == 5)
     reopen(False)
     back("a", 1)
-    pieces = ((0, 0, 32), (0, 32, 64), (1, 0, 32), (1, 32, 48), (1, 48, 64))
-    PB = (0, 1, 4, 5, 6)
 
-    def get(j):
-        ch, lo, hi = pieces[j]
-        o, w, b = 1024 * ch + 16 * lo, 16 * (hi - lo), PB[j]
-        rows("S", "b", ch, lo, hi); rows("V", "a", ch, lo, hi)
-        mm([[(ps[b][:, 0:w], T.OB[:], T.MB[:, o:o + w])]], keys("Mb%d" % ch, lo, hi) + ["OB"], b, True, False)
-        mm([[(ps[b][:, 0:w], T.OA[:], T.MA[:, o:o + w])]], keys("Ma%d" % ch, lo, hi) + ["OA"], b, False, True)
-
-    def out(e, j):
-        ch, lo, hi = pieces[j]
-        move(e, T.OUT[:, 1024 * ch + 16 * lo:1024 * ch + 16 * hi], ps[PB[j]][:, 0:16 * (hi - lo)], [],
-             keys("OUT%d" % ch, lo, hi), [PB[j]])
+    def get(ch, lo, hi, e="S"):
+        o, w = 1024 * ch + 16 * lo, 16 * (hi - lo)
+        move(e, T.OB[:, o:o + w], tab("b", ch, lo, hi), TK["b"] + ["Ub%d" % ch], keys("OB%d" % ch, lo, hi))
+        tt(T.OUT[:, o:o + w], tab("a", ch, lo, hi), T.OB[:, o:o + w], A.add,
+           TK["a"] + ["Ua%d" % ch] + keys("OB%d" % ch, lo, hi), keys("OUT%d" % ch, lo, hi))
 
     def put(ch, qs):
         for r, y in enumerate((T.ya, T.yb, T.ys)):
-            dma(qs[r], y[:, 1024 * ch:1024 * (ch + 1)], T.OUT[r::16, 1024 * ch:1024 * (ch + 1)],
+            dma(qs[r], y[:, 1024 * ch:1024 * (ch + 1)], T.OUT[5 + r::16, 1024 * ch:1024 * (ch + 1)],
                 keys("OUT%d" % ch, 0, 64), [])
     ulist("S", "b", 0); ulist("V", "a", 0)
-    get(0)
-    ulist("S", "b", 1); ulist("V", "a", 1)
-    get(1); get(2); get(3)
-    out("S", 0); out("S", 1)
+    get(0, 0, 8, "V"); get(0, 8, 40)
+    ulist("S", "b", 1)
+    get(0, 40, 64)
+    ulist("S", "a", 1)
     put(0, "YYY")
-    get(4)
-    out("S", 2); out("V", 3); out("V", 4)
+    get(1, 0, 32); get(1, 32, 64)
     put(1, "YSY")
+    for j in order(calls, landing):
+        calls[j][1]()
     ends["sent"] = sent[0]
     for s, v in ends.items():
-        g.wait_ge(T.sem[s], v)
+        if max(x.get(s, 0) for x in seen.values()) < v:
+            g.wait_ge(T.sem[s], v)

@@ -1,3 +1,4 @@
+import numpy as np
 from concourse.mybir import AluOpType as A, ActivationFunctionType as AF
 
 M = 4096
@@ -9,9 +10,10 @@ BIG = 16.0
 LIFT = 4096.0
 MAGIC = 1.5 * 2.0 ** 27
 SC = 2.0 ** -13
-OPT = {"route": "abdd", "order": "k0s123"}
-CYC, HOP, GATHER, SCATTER = 0.92e-3, 0.26, 1.45, 3.8
-LANDS = {"rk": 8.2, "rs": 10.4, "rh": 16.0}
+OPT = {"route": "abdd", "order": "0kst123"}
+CYC, HOP, TRIES = 0.83e-3, 0.25, 20000
+PACES = ((1.0, 1.25, 2.6, 0.3 / 76, 0.25, 1.0), (1.3, 1.8, 2.8, 0.25 / 103, 0.2, 1.25),
+         (1.25, 1.5, 5.3, 0.25 / 100, 0.28, 1.0), (1.1, 1.4, 3.6, 0.2 / 86, 0.22, 1.35))
 GATHERED = ("Ma", "Mb", "NF", "FL", "KB", "OB", "OUT")
 NDMA = 40
 
@@ -24,11 +26,11 @@ SCRATCH = {}
 for _dt, _list in (
         ("bfloat16", dict(H=2 * SO, Z=1312, IB=128, SF=8, SZ=8, NF=3584, FL=7168, F1=64, F2=[16, 8], S2=512, KB=1024,
                           ONE=512, CODE=128, J=160, J2=128, J4=128, JT=64)),
-        ("float16", dict(W16=2064, MA=2048, MB=2048, I16=128, I8=128, R2=128, R2S=128, R4=128, R4S=128, R4W=128,
-                         LT=128, ON=128, IP=128, IN=128, SA=32, SB=32, I256=128, I2K=128, BK=2 * 908, M4=128, M16=128,
+        ("float16", dict(W16=2064, MA=2048, MB=2048, I16=128, I8=[16, 8], R2=128, R2S=128, R4=128, R4S=128, R4W=128,
+                         LT=128, ON=128, IP=128, IN=128, SA=32, SB=32, I256=128, BK=2 * 908, M4=128, M16=128,
                          CDS=32, C25=32, ZERO=512, PQ=[163, 8], PC0=[81, 16], PC1=[81, 16], ZQ=[256, 8], ZP=[35, 4],
-                         GQ=[65, 8], GC=512, K=128, C4=128, C16=256, MR=1024, E=32, Ua=512, Ub=512, La=512, Lb=512,
-                         Na=512, Nb=512, Sa=256, Sb=256, Ca=1024, Cb=1024, Za=[136, 16], Zb=[136, 16])),
+                         GQ=[65, 8], GC=512, K=128, C4=128, C16=256, MR=1024, E=32, U=512, L=512, N=512, SL=256,
+                         LF=512, KC=1024, Ca=1024, Cb=1024, Za=[136, 16], Zb=[136, 16])),
         ("float32", dict(TA=4104, TB=4104, W=5152, IDR=256, IDT=256, CD=32, col=64, ZC=516, D=1024, OUT=2048, OB=2048,
                          IDN=256, SZU=512, st=64)),
         ("int32", dict(ki=512, sai=64, pci=8)),
@@ -37,7 +39,7 @@ for _dt, _list in (
         SCRATCH[_k] = _sb(_n, _dt)
 for _b in range(8):
     SCRATCH["ps%d" % _b] = ("psum", [128, 512], "float32")
-SEMAPHORES = (["cV", "cS", "cP", "cG", "sent", "rk", "rs", "hout"] + ["rh%d" % k for k in range(4)]
+SEMAPHORES = (["cV", "cS", "cP", "cG", "sent", "rk", "rs", "rt", "hout"] + ["rh%d" % k for k in range(4)]
               + ["hi%d" % k for k in range(4)] + ["d%d" % i for i in range(NDMA)])
 
 
@@ -78,22 +80,24 @@ def helper_program(g, core, T, topo):
         g.wait_ge(T.sem.hout, out)
 
 
-def order(calls, landing):
+ORDER = []
+
+
+def order(calls):
     n = len(calls)
     pre, wr, rd, last = [], {}, {}, {}
     ready = [0.0] * n
-    for j, (e, _, reads, writes, banks, dur, lat) in enumerate(calls):
+    for j, (e, _, reads, writes, banks, dur, lat, either) in enumerate(calls):
         p = {}
         for k in reads:
             if k in wr:
-                p[wr[k]] = HOP
-            ready[j] = max(ready[j], landing.get(k, 0.0))
+                p[wr[k]] = 1
         for k in writes:
             for i in ([wr[k]] if k in wr else []) + rd.get(k, []):
-                p[i] = HOP
+                p[i] = 1
         for b in banks + ([e] if e in "GY" else []):
             if b in last:
-                p.setdefault(last[b], HOP if calls[last[b]][0] != e else None)
+                p.setdefault(last[b], int(calls[last[b]][0] != e or either or calls[last[b]][7]))
             last[b] = j
         for k in reads:
             rd.setdefault(k, []).append(j)
@@ -101,29 +105,79 @@ def order(calls, landing):
             wr[k], rd[k] = j, []
         p.pop(j, None)
         pre.append(p)
-    post = [{} for _ in range(n)]
+    on, lag = [c[0] for c in calls], [c[6] for c in calls]
+    mean = [sum(c[5]) / len(PACES) for c in calls]
+    ahead, behind = [[] for _ in range(n)], [[] for _ in range(n)]
     for j in range(n):
-        for i, h in pre[j].items():
-            post[i][j] = h
+        for i, waits in pre[j].items():
+            ahead[i].append((j, mean[i] + waits * (HOP + lag[i])))
+            behind[j].append((i, mean[j] + waits * (HOP + lag[i])))
+    links = [[[(i, calls[i][5][k] + waits * (PACES[k][4] + PACES[k][5] * lag[i])) for i, waits in p.items()] for p in pre]
+             for k in range(len(PACES))]
 
-    def place(turns, before, start, back):
-        at, busy = [0.0] * n, {e: [] for e in "VSPGY"}
-        for j in turns:
-            e, dur = calls[j][0], calls[j][5]
-            t = start[j]
-            for i, h in before[j].items():
-                t = max(t, at[i] + calls[i][5] + (0.0 if h is None else h + calls[j if back else i][6]))
-            for k, (a, b) in enumerate(busy[e] + [(1e9, 1e9)]):
-                if t + dur <= a + 1e-9:
-                    break
-                t = max(t, b)
-            busy[e].insert(k, (t, t + dur))
+    def place(turn, after, before, start):
+        left, at = [len(x) for x in before], list(start)
+        free, busy = [(turn[j], j) for j in range(n) if not left[j]], {e: [] for e in "VSPGY"}
+        while free:
+            x = min(free)
+            free.remove(x)
+            j = x[1]
+            t, q = at[j], busy[on[j]]
+            k = len(q)
+            while k and q[k - 1][1] > t:
+                k -= 1
+            while k < len(q) and t + mean[j] > q[k][0] + 1e-9:
+                t = max(t, q[k][1])
+                k += 1
+            q.insert(k, (t, t + mean[j]))
             at[j] = t
+            for i, w in after[j]:
+                at[i] = max(at[i], t + w)
+                left[i] -= 1
+                if not left[i]:
+                    free.append((turn[i], i))
         return at
-    at = place(range(n), pre, ready, False)
-    back = place(sorted(range(n), key=lambda j: (-at[j] - calls[j][5], -j)), post, [x[6] for x in calls], True)
-    at = place(sorted(range(n), key=lambda j: (-back[j] - calls[j][5], j)), pre, ready, False)
-    return sorted(range(n), key=lambda j: (at[j], j))
+
+    def tighten(at):
+        back = place([-at[j] - mean[j] for j in range(n)], behind, ahead, lag)
+        return place([-back[j] - mean[j] for j in range(n)], ahead, behind, ready)
+
+    def length(at):
+        turns, total = sorted(range(n), key=lambda j: (at[j], j)), 0.0
+        for k, pace in enumerate(PACES):
+            begin, free = list(ready), dict.fromkeys("VSPGY", 0.0)
+            for j in turns:
+                t = max(begin[j], free[on[j]])
+                for i, w in links[k][j]:
+                    if begin[i] + w > t:
+                        t = begin[i] + w
+                begin[j], free[on[j]] = t, t + calls[j][5][k]
+            total += free["Y"] * pace[3]
+        return total
+    at = tighten(place(range(n), ahead, behind, ready))
+    now = least = length(at)
+    best, either = (at, list(on)), [j for j in range(n) if calls[j][7]]
+    rng = np.random.RandomState(n)
+    for it in range(TRIES):
+        turn, was = list(at), list(on)
+        if it % 4 == 0:
+            for j in rng.choice(either, 1 + it % 8 // 4):
+                on[j] = "V" if on[j] == "S" else "S"
+        else:
+            lo, shift = int(rng.randint(n)), float(rng.uniform(-1, 1) * rng.choice((0.4, 1.0, 3.0)))
+            for j in range(lo, min(n, lo + int(rng.choice((1, 2, 4, 8, 20, 60))))):
+                turn[j] += shift
+        x = place(turn, ahead, behind, ready)
+        if it % 15 == 0:
+            x = tighten(x)
+        v = length(x)
+        if v <= now + 0.0006 * (1 - it / TRIES) * rng.random_sample():
+            at, now = x, v
+            if v < least:
+                best, least = (x, list(on)), v
+        else:
+            on[:] = was
+    return [(j, best[1][j]) for j in sorted(range(n), key=lambda j: (best[0][j], j))]
 
 
 def rank_program(g, core, T, topo):
@@ -196,7 +250,7 @@ def rank_program(g, core, T, topo):
         g.remote_dma(out, in_, T.sem[sem], T.sem.sent, pid, rid, m)
         sent[0] += bits(m)
 
-    calls, landing = [], {}
+    calls = []
 
     def width(ap):
         w = 1
@@ -205,25 +259,29 @@ def rank_program(g, core, T, topo):
         return w
 
     def op(e, fn, reads, writes, banks=(), n=64, per=1.0):
-        if writes[0].startswith(GATHERED) and not banks:
-            per = GATHER
-        calls.append((e, lambda: issue_op(e, fn, reads, writes, banks), reads, writes, list(banks),
-                      max(64, n * per) * CYC + (0.05 if per > 1 else 0.0), 0.0))
+        kind = 1 if writes[0].startswith(GATHERED) and not banks else 2 if writes[0] == "W" else 0
+        either = isinstance(fn, dict)
+        calls.append((e, lambda on: issue_op(on, fn[on] if either else fn, reads, writes, banks), reads, writes,
+                      list(banks), [(70 + n * x[kind] if kind else max(64, n * per)) * CYC * x[0] for x in PACES], 0.0,
+                      either))
 
     def mm(groups, reads, b, opens=True, closes=True):
-        calls.append(("P", lambda: issue_mm(groups, reads, b, opens, closes), reads, [], [b],
-                      sum(max(64, width(x[0])) for grp in groups for x in grp) * CYC / 2, 0.0))
+        cycles = sum(max(64, width(x[0])) for grp in groups for x in grp) / 2
+        calls.append(("P", lambda on: issue_mm(groups, reads, b, opens, closes), reads, [], [b],
+                      [cycles * CYC * x[0] for x in PACES], 0.0, False))
 
     def dma(e, out, in_, reads, writes, lat=2.5):
-        calls.append((e, lambda: issue_dma(e, out, in_, reads, writes), reads, writes, [], 0.08, lat))
+        calls.append((e, lambda on: issue_dma(e, out, in_, reads, writes), reads, writes, [], [0.08] * len(PACES), lat,
+                      False))
 
-    def send(to, out, in_, sem, reads, m=None):
-        calls.append(("G", lambda: issue_send(to, out, in_, sem, reads, m), reads, [], [], 0.6, 60.0))
+    def send(to, out, in_, sem, reads, lands, lag, m=None):
+        first = not any(c[6] for c in calls if c[0] == "G")
+        calls.append(("G", lambda on: issue_send(to, out, in_, sem, reads, m), reads, lands, [],
+                      [(1.8 if first else 0.6) * x[5] for x in PACES], lag, False))
 
     def arrives(names, sem, frm):
         for key in names:
             wr[key] = [(sem, bits(topo.mask(frm, core)))]
-            landing[key] = LANDS[sem[:2]]
         ends[sem] = bits(topo.mask(frm, core))
 
     def ts(out, in0, s1, s2, o0, o1, reads, writes, banks=()):
@@ -244,17 +302,13 @@ def rank_program(g, core, T, topo):
         op("S", lambda: S.activation(out, in_, AF.Copy, scale=scale), reads, writes, banks, width(out))
 
     def add(e, out, in_, c, reads, writes, banks=()):
-        if e == "V":
-            t1(out, in_, c, A.add, reads, writes, banks)
-        else:
-            op("S", lambda: S.activation(out, in_, AF.Identity, bias=bias[c]), reads + ["bias"], writes, banks,
-               width(out))
+        op(e, {"V": lambda: V.tensor_scalar(out, in_, c, None, A.add),
+               "S": lambda: S.activation(out, in_, AF.Identity, bias=bias[c])}, reads + ["bias"], writes, banks,
+           width(out))
 
-    def move(e, out, in_, reads, writes, banks=()):
-        if e == "V":
-            cp(out, in_, reads, writes, banks)
-        else:
-            act(out, in_, 1.0, reads, writes, banks)
+    def move(e, out, in_, reads, writes, banks=(), c=1.0):
+        op(e, {"V": lambda: V.tensor_scalar(out, in_, c, None, A.mult),
+               "S": lambda: S.activation(out, in_, AF.Copy, scale=c)}, reads, writes, banks, width(out))
 
     def fill(out, c, key):
         op("V", lambda: V.memset(out, c), [], [key], (), width(out), 0.5)
@@ -268,24 +322,22 @@ def rank_program(g, core, T, topo):
     def clear(b, w=448):
         mm([[(ps[b][:, 0:w], T.ZERO[:, 0:128], T.ZERO[:, 0:w])]], ["ZERO"], b, True, False)
 
-    arrives(["Ub"], "rk", src)
+    arrives(["Cb0", "Cb1"], "rk", src)
     arrives(["Cb2", "Cb3"], "rs", src)
+    arrives(["Cb4", "Cb5"], "rt", src)
     for k, h in enumerate(routes(src, core, T, topo)):
         arrives(["Hf%d" % k], "rh%d" % k, src if h is None else h)
 
     def ho(k):
-        return ["Ho%d" % k] + ["Hx%d" % k] * (rank % 2)
+        return ["Hx%d" % k, "Ho%d" % k]
     HALL = [x for k in range(4) for x in ho(k)] + num("Hf", range(4)) + ["Hd"]
 
     dma("S", T.ki[:, 0:256], T.kl[:], [], ["kl"], 1.9)
     dma("Y", T.ki[:, 256:512], T.kr[:], [], ["kr"], 1.9)
     for k in range(4):
         c = slice(1024 * k, 1024 * (k + 1))
-        if rank % 2 == 0:
-            dma("Y", T.H[:, c], T.h[:, c], [], ["Ho%d" % k], 2.6 + 0.7 * k)
-        else:
-            dma("Y", T.H[0::2, c], T.h[1::2, c], [], ["Hx%d" % k], 2.6 + 0.7 * k)
-            dma("Y", T.H[1::2, c], T.h[0::2, c], [], ["Ho%d" % k], 2.6 + 0.7 * k)
+        for j, key in enumerate(ho(k)):
+            dma("Y", T.H[j::2, c], T.h[(j + rank) % 2::2, c], [], [key], 3.1 + 0.78 * k)
     dma("Y", T.sai[:, 0:32], T.sa[:], [], ["sa"], 6.0)
     dma("Y", T.sai[:, 32:64], T.sb[:], [], ["sb"], 6.0)
 
@@ -299,11 +351,11 @@ def rank_program(g, core, T, topo):
         op("G", lambda a=(t, pat, base, mult): g.iota(*a, allow_small_or_imprecise_dtypes=True), [], [key], (),
            width(t) + 80, 2.0)
     fill(T.ZERO[:], 0.0, "ZERO")
-    clear(6, 512); clear(7, 256)
+    clear(6, 512); clear(7, 128); clear(4, 128)
     col, pci, J = T.col, T.pci, T.J
     SH, AND = A.arith_shift_right, A.bitwise_and
     bias = {}
-    for j, c in enumerate((COL, COL + 16, LIFT, -LIFT)):
+    for j, c in enumerate((COL, COL + 16, LIFT, -LIFT, 1.0)):
         bias[c] = col[:, 56 + j:57 + j]
         fill(bias[c], c, "bias%d" % j)
     t1(pci[:, 1:2], pci[:, 0:1], 15, AND, ["pci0"], ["pci1"])
@@ -311,7 +363,7 @@ def rank_program(g, core, T, topo):
     t1(pci[:, 3:4], pci[:, 0:1], 3, AND, ["pci0"], ["pci3"])
     ts(pci[:, 4:5], pci[:, 0:1], 3, 1, SH, AND, ["pci0"], ["pci4"])
     fill(T.Z[:], 0.0, "Z")
-    cp(col[:, 0:5], pci[:, 0:5], num("pci", range(5)) + num("bias", range(4)), ["c_p", "bias"])
+    cp(col[:, 0:5], pci[:, 0:5], num("pci", range(5)) + num("bias", range(5)), ["c_p", "bias"])
     c_p, c_pm, c_g, c_r, c_v, c_g17, c_gm, c_pp = (col[:, j:j + 1] for j in range(8))
     oh = [col[:, 8 + j:9 + j] for j in range(16)]
     t1(c_gm, c_g, -float(M), A.mult, ["c_p"], ["c_gm"])
@@ -319,23 +371,17 @@ def rank_program(g, core, T, topo):
     t1(T.I16[:], J[:, 0:128], c_p, A.is_equal, ["J", "c_p"], ["I16"])
     ts(ps[5][:, 0:256], T.IDR[:], c_gm, 1.0 / HALF, A.add, A.mult, ["IDR", "c_gm"], ["own"], [5])
     tt(ps[5][:, 0:1], ps[5][:, 0:1], oh[8], A.add, ["own", "oh"], ["own"], [5])
-    t1(T.Ua[:], T.ki[:], -float(HALF), A.add, ["kl", "kr"], ["Ua"])
+    t1(T.U[:], T.ki[:], -float(HALF), A.add, ["kl", "kr"], ["U"])
     ts(T.SZ[:], J[:, 0:8], c_g, 1.0 / 256, A.is_equal, A.mult, ["J", "c_p"], ["SZ"])
     ts(T.I8[:], J[:, 0:128], c_p, -PEN / HALF, A.is_equal, A.mult, ["J", "c_p"], ["I8"])
 
-    def kids(x, between=lambda: None):
-        U, L, N, Sf = T["U" + x], T["L" + x], T["N" + x], T["S" + x]
-
-        def over(t, key, sides, closes):
-            mm([[(ps[6][:, 256 * s + 128 * h:256 * s + 128 * h + 128], t[:, 256 * s + 128 * h:256 * s + 128 * h + 128],
-                  T.I16[:]) for s in sides for h in range(2)]], [key, "I16"], 6, False, closes)
-        ts(L[:], U[:], -float(HALF), float(HALF), A.is_equal, A.mult, ["U" + x], ["L" + x])
-        ts(N[:], U[:], 0.0, float(HALF), A.is_equal, A.mult, ["U" + x], ["N" + x])
-        tt(Sf[:], ps[5][:, 0:256], L[:, 0:256], A.mult, ["own", "L" + x], ["S" + x], [5])
-        between()
-        over(U, "U" + x, (0, 1), False)
-        over(L, "L" + x, (0, 1), False); over(N, "N" + x, (0, 1), False); over(Sf, "S" + x, (0,), True)
-        act(T["C" + x][:, 0:512], ps[6][:, 0:512], 1.0, [], ["C%s0" % x, "C%s1" % x], [6])
+    ts(T.L[:], T.U[:], -float(HALF), float(HALF), A.is_equal, A.mult, ["U"], ["L"])
+    ts(T.N[:], T.U[:], 0.0, float(HALF), A.is_equal, A.mult, ["U"], ["N"])
+    tt(T.SL[:], ps[5][:, 0:256], T.L[:, 0:256], A.mult, ["own", "L"], ["SL"], [5])
+    for t, w in ((T.U, 4), (T.L, 4), (T.N, 4), (T.SL, 2)):
+        mm([[(ps[6][:, 128 * j:128 * j + 128], t[:, 128 * j:128 * j + 128], T.I16[:]) for j in range(w)]],
+           [t.name, "I16"], 6, False, w == 2)
+    act(T.Ca[:, 0:512], ps[6][:, 0:512], 1.0, [], ["Ca0", "Ca1"], [6])
 
     def zrow(x, r, h):
         return T["Z" + x][:, 8 * h + r:128:16, :]
@@ -345,12 +391,19 @@ def rank_program(g, core, T, topo):
             move(e, zrow(x, j + 1, h), T["C" + x][:, 256 * j + 128 * h:256 * j + 128 * h + 128], ["C%s%d" % (x, j)],
                  ["Z%s%d_%d" % (x, j + 1, h)])
 
+    def spread_keys(es, x, u):
+        for j in range(4):
+            o = 512 + 256 * u + 64 * j
+            move(es[j], T["Z" + x][:, 8 * (j % 2) + 3 + j // 2:128:16, 8 * u:8 * u + 8], T["C" + x][:, o:o + 64],
+                 ["C%s%d" % (x, 2 + 2 * u + j // 2)], ["Y%s%d_%d" % (x, u, j)])
+
     TAB = {"a": T.TA, "b": T.TB}
 
-    def table(x, banks, es, qs=range(8)):
+    def table(x, u, banks, es):
         z, t = T["Z" + x], TAB[x]
-        rk = ["Z%s%d_%d" % (x, r, h) for r in range(5) for h in range(2)] + num(z.name, "567p") + ["I16"]
-        for q in qs:
+        rk = (["Z%s%d_%d" % (x, r, h) for r in range(3) for h in range(2)] + num("Y%s%d_" % (x, u), range(4))
+              + num(z.name, "567p") + ["I16"])
+        for q in range(4 * u, 4 * u + 4):
             mm([[(ps[banks[q]][:, 128 * j:128 * (j + 1)], z[:, 8 * (j % 2):8 * (j % 2) + 128, 2 * q + j // 2], T.I16[:])]
                 for j in range(4)], rk, banks[q])
             lo = int(q == 4)
@@ -360,34 +413,43 @@ def rank_program(g, core, T, topo):
     TK = {x: num("T" + x, range(8)) + ["T%sd" % x, "T%se" % x] for x in "ab"}
 
     def sizes(k):
-        mm([[(ps[7][:, 128 * h + i:128 * h + 128:16], T.H[:, 256 * i + 128 * h:256 * i + 128 * h + 128], T.SZ[:])
-             for i in range(4 * k, 4 * k + 4) for h in range(2)]], ["SZ"] + ho(k), 7, False, k == 3)
+        b = (7, 4)[k // 2]
+        mm([[(ps[b][:, 64 * h + i % 8:64 * h + 64:8], T.H[:, 256 * i + 128 * h:256 * i + 128 * h + 128], T.SZ[:])
+             for i in range(4 * k, 4 * k + 4) for h in range(2)]], ["SZ"] + ho(k), b, False, False)
 
-    kids("a")
-    clear(6, 512)
-    sizes(0)
-    mm([[(ps[7][:, 128 * h:128 * h + 128], T.La[:, 128 * h:128 * h + 128], T.I8[:]) for h in range(2)]], ["La", "I8"], 7,
-       False, False)
-    sizes(1); sizes(2)
-    fill(T.H[:, M:SO], -262144.0, "Hpad")
-    cp(T.H[:, M:M + 1], T.H[:, HALF:HALF + 1], ho(2) + ["Hpad"], ["Hd"])
-    fill(T.H[:, HALF:HALF + 1], -262144.0, "Ho2")
-    sizes(3)
-    ts(T.Ca[:, 512:768], ps[7][:, 0:256], MAGIC, -MAGIC, A.add, A.add, [], ["Ca2"], [7])
-    tt(T.Ca[:, 768:1024], ps[7][:, 0:256], T.Ca[:, 512:768], A.subtract, ["Ca2"], ["Ca3"], [7])
+    def opening(u):
+        b, o = (7, 4)[u], 512 + 256 * u
+        mm([[(ps[b][:, 64 * h:64 * h + 64], T.L[:, 128 * h:128 * h + 128], T.I8[:, u::2, :]) for h in range(2)]],
+           ["L", "I8"], b, False, u == 0)
+        if u:
+            sizes(2)
+            fill(T.H[:, M:SO], -262144.0, "Hpad")
+            cp(T.H[:, M:M + 1], T.H[:, HALF:HALF + 1], ho(2) + ["Hpad"], ["Hd"])
+            fill(T.H[:, HALF:HALF + 1], -262144.0, "Ho2")
+            sizes(3)
+            mm([[(ps[b][:, 0:64], T.ZERO[:, 0:128], T.ZERO[:, 0:64])]], ["ZERO"], b, False, True)
+        ts(T.Ca[:, o:o + 128], ps[b][:, 0:128], MAGIC, -MAGIC, A.add, A.add, [], ["Ca%d" % (2 + 2 * u)], [b])
+        tt(T.Ca[:, o + 128:o + 256], ps[b][:, 0:128], T.Ca[:, o:o + 128], A.subtract, ["Ca%d" % (2 + 2 * u)],
+           ["Ca%d" % (3 + 2 * u)], [b])
+
+    sizes(0); sizes(1)
+    opening(0); opening(1)
     rt = routes(core, dst, T, topo)
     for x in OPT["order"]:
         if x == "k":
-            send(dst, T.Ub[:], T.Ua[:], "rk", ["Ua"])
-        elif x == "s":
-            send(dst, T.Cb[:, 512:1024], T.Ca[:, 512:1024], "rs", ["Ca2", "Ca3"])
+            send(dst, T.Cb[:, 0:512], T.Ca[:, 0:512], "rk", ["Ca0", "Ca1"], ["Cb0", "Cb1"], 2.2)
+        elif x in "st":
+            o = 512 + 256 * "st".index(x)
+            js = (o // 128 - 2, o // 128 - 1)
+            send(dst, T.Cb[:, o:o + 256], T.Ca[:, o:o + 256], "r" + x, num("Ca", js), num("Cb", js), 2.0)
         else:
             q = quarter(int(x))
             rk = ho(int(x)) + (["Hd"] if x == "3" else [])
             if rt[int(x)] is None:
-                send(dst, T.H[:, SO + q.start:SO + q.stop], T.H[:, q], "rh" + x, rk)
+                send(dst, T.H[:, SO + q.start:SO + q.stop], T.H[:, q], "rh" + x, rk, ["Hf" + x], 5.0)
             else:
-                send(rt[int(x)], T.H[:, q], T.H[:, q], "hi" + x, rk, near_mask(core, rt[int(x)], dst, topo))
+                send(rt[int(x)], T.H[:, q], T.H[:, q], "hi" + x, rk, ["Hf" + x], 7.5,
+                     near_mask(core, rt[int(x)], dst, topo))
     for x in "ab":
         z = T["Z" + x]
         for h in range(2):
@@ -400,11 +462,16 @@ def rank_program(g, core, T, topo):
     for t, w in ((T.PQ, 1304), (T.PC0, 656), (T.PC1, 656)):
         act(t[:] if t is T.PQ else t[:, 0::2, :], T.Z[:, 0:w], 1.0, ["Z"], [t.name + "z"])
     act(T.GQ[:, 0::2, :], T.Z[:, 0:264], 1.0, ["Z"], ["GQz"])
-    spread("S", "a", 0); spread("S", "a", 1)
+    spread("S", "a", 0); spread("V", "a", 1)
+    for u in range(2):
+        spread_keys("VSVS", "a", u)
+        table("a", u, (0, 1, 2, 3, 5, 6, 7, 4), "SVSVVSVS")
+    spread("S", "b", 0); spread("V", "b", 1)
+    clear(0)
+    for u in range(2):
+        spread_keys("VSVS", "b", u)
+        table("b", u, (1, 2, 3, 5, 6, 7, 4, 1), "SVSVVSVS")
     op("S", lambda: S.activation(T.ZC[:], T.Z[:, 0:516], AF.Silu, bias=bias[LIFT]), ["Z", "bias"], ["ZC"], (), 2000)
-    spread("S", "a", 2); spread("V", "a", 3)
-    kids("b", lambda: table("a", (0, 1, 2, 3, 4, 7, 0, 1), "SVSSVSVS", range(3)))
-    table("a", (0, 1, 2, 3, 4, 7, 0, 1), "SVSSVSVS", range(3, 8))
     ts(T.st[:], T.sai[:], float(HALF), float(HALF), A.is_equal, A.mult, ["sa", "sb"], ["st"])
     tt(T.st[:], T.st[:], T.sai[:], A.add, ["st"], ["st"])
     cp(T.UAB[:, 0:32], T.st[:, 0:32], ["st"], ["Ua0"])
@@ -415,7 +482,7 @@ def rank_program(g, core, T, topo):
     t1(T.SA[:], T.JT[:, 0:32], c_pp, A.is_equal, ["JA", "c_pp"], ["SA"])
     ts(T.SB[:], T.JT[:, 32:64], c_pp, col[:, 24:25], A.is_equal, A.mult, ["JB", "c_pp", "sg"], ["SB"])
     for t, j, w in ((T.R2, T.J2, 1.0), (T.R2S, T.J2, SO), (T.R4, T.J4, 1.0), (T.R4S, T.J4, SO), (T.R4W, T.J4, 1 / SC),
-                    (T.I256, J, 256.0), (T.I2K, J, PEN / 8), (T.IB, J, 1.0), (T.IP, J, SC), (T.IN, J, -SC)):
+                    (T.I256, J, 256.0), (T.IB, J, 1.0), (T.IP, J, SC), (T.IN, J, -SC)):
         ts(t[:], j[:, 0:128], c_p, float(w), A.is_equal, A.mult, [j.name, "c_p"], [t.name])
     ts(T.SF[:], J[:, 0:8], c_g, BIG, A.is_equal, A.mult, ["J", "c_p"], ["SF"])
     ts(T.LT[:], J[:, 0:128], c_p, SC, A.is_gt, A.mult, ["J", "c_p"], ["LT"])
@@ -446,14 +513,18 @@ def rank_program(g, core, T, topo):
 
     def true_sizes(j, x):
         C, out = T["C" + x], ps[2 + j]
-        mm([[(out[:, 0:256], T.I2K[:], T["L" + x][:, 0:256])]
-            + [(out[:, 128 * h:128 * h + 128], C[:, o + 128 * h:o + 128 * h + 128], T.I256[:])
-               for o in (512, 768) for h in range(2)]], ["I2K", "I256", "L" + x, "C%s2" % x, "C%s3" % x], 2 + j)
+        ts(T.LF[:, 256 * j:256 * j + 256], C[:, 256:512], 0.0, PEN, A.is_equal, A.mult, ["C%s1" % x], ["LF" + x])
+        for k in range(4):
+            cp(T.KC[:, 512 * j + 128 * k:512 * j + 128 * k + 128], zrow(x, 3 + k // 2, k % 2),
+               ["Y%s%d_%d" % (x, u, k) for u in range(2)], ["KC%s%d" % (x, k)])
+        mm([[(out[:, 128 * h:128 * h + 128], t[:, o + 128 * h:o + 128 * h + 128], T.I256[:])
+             for t, o in ((T.KC, 512 * j), (T.KC, 512 * j + 256), (T.LF, 256 * j))] for h in range(2)],
+           ["I256", "LF" + x] + num("KC" + x, range(4)), 2 + j)
         act(T.SZU[:, 256 * j:256 * (j + 1)], out[:, 0:256], 1.0, [], ["SZU" + x], [2 + j])
 
     def refill(after=()):
         for k in range(4):
-            dma("Y", T.W[:, 516 * k:516 * (k + 1)], T.ZC[:], ["ZC"] + list(after), ["Wz%d" % k], 3.0 + k)
+            dma("Y", T.W[:, 516 * k:516 * (k + 1)], T.ZC[:], ["ZC"] + list(after), ["Wz%d" % k], 2.2 + 0.9 * k)
 
     NB, CH = (8, 8, 4, 8), (0, 1, 0, 0)
     PT = (T.PC0, T.PC1, T.PQ, T.PC0)
@@ -537,8 +608,8 @@ def rank_program(g, core, T, topo):
 
     def fixed(s, lo, hi):
         o, u = NFO[s], 192 * s + 128
-        act(T.NF[:, o + 16 * lo:o + 16 * hi], T.H[:, :].indirect(T.UL[:, u + lo:u + hi]), -1.0,
-            HALL + ["UL%d_2" % s], keys("NF%d" % s, lo, hi))
+        move("S", T.NF[:, o + 16 * lo:o + 16 * hi], T.H[:, :].indirect(T.UL[:, u + lo:u + hi]),
+             HALL + ["UL%d_2" % s], keys("NF%d" % s, lo, hi), (), -1.0)
 
     def test(s, side, lo, hi):
         o, u, f = NFO[s], 192 * s + 64 * side, FLO[s] + 128 * NB[s] * side
@@ -568,7 +639,9 @@ def rank_program(g, core, T, topo):
             mm([x], rk, b, False, closes)
 
     def kept(s):
-        t1(T.K[:], ps[4 + s][:, 0:128], 0.0, A.is_equal, [], ["K"], [4 + s])
+        f = ps[4 + s][:, 0:128]
+        op("V", {"V": lambda: V.tensor_scalar(T.K[:], f, 0.0, None, A.is_equal),
+                 "S": lambda: S.activation(T.K[:], f, AF.Relu, bias=bias[1.0], scale=-1.0)}, ["bias"], ["K"], [4 + s], 128)
 
     def counts(s):
         for out, m, key in ((T.C4[:], T.M4, "C4"), (T.C16[:, 128 * s:128 * (s + 1)], T.M16, "C16_%d" % s)):
@@ -613,16 +686,16 @@ def rank_program(g, core, T, topo):
     def scatter(s):
         zk = ["ZQ%d_%d" % (s, 8 * v + 4 * side + r) for r, side, v in ROWS]
         rk = ["UP%d" % s] + num("Wz", range(4))
-        for lo, hi, b in (((0, 128, 0),), ((0, 64, 1), (64, 128, 5)))[s]:
+        for lo, hi, b in ((0, 64, s), (64, 128, 4 + s)):
             mm([[(ps[b][:, 4 * lo + j:4 * hi:4], T.ZQ[:, 128 * s:128 * (s + 1), 2 * j + u], T.I16[:, lo:hi])
                  for u in range(2)] for j in range(4)], zk + ["I16"], b)
             rk.append("D%d_%d" % (s, lo))
-            add("SV"[s], T.D[:, 512 * s + 4 * lo:512 * s + 4 * hi], ps[b][:, 4 * lo:4 * hi], LIFT, [], rk[-1:], [b])
+            add("S" if b == 4 else "V", T.D[:, 512 * s + 4 * lo:512 * s + 4 * hi], ps[b][:, 4 * lo:4 * hi], LIFT, [], rk[-1:], [b])
         win, d = T.W[:, :].indirect(T.UP[:, 32 * s:32 * (s + 1)]), T.D[:, 512 * s:512 * (s + 1)]
         if s == 0:
-            op("S", lambda: S.activation(win, d, AF.Silu), rk, ["W"], (), 512, SCATTER)
+            op("S", lambda: S.activation(win, d, AF.Silu), rk, ["W"], (), 512)
         else:
-            op("V", lambda: V.tensor_copy(win, d), rk, ["W"], (), 512, SCATTER)
+            op("V", lambda: V.tensor_copy(win, d), rk, ["W"], (), 512)
 
     def back(x, ch):
         v, o = "ab".index(x), 16 + 1024 * ch
@@ -729,11 +802,7 @@ def rank_program(g, core, T, topo):
         for j in (2, 0, 1):
             tlist(s, j, 4 + (j == 2))
 
-    spread("S", "b", 0); spread("V", "b", 1)
-    clear(0)
-    spread("S", "b", 2); spread("V", "b", 3)
     rows("S", "a", 0, 0, 32)
-    table("b", (2, 3, 4, 7, 5, 6, 1, 2), "VSVSVSVS")
     turn(2, "a", False)
     rows("V", "b", 0, 16, 32); rows("S", "b", 0, 0, 16); turn(2, "b", True)
     true_sizes(0, "a"); true_sizes(1, "b")
@@ -801,15 +870,16 @@ def rank_program(g, core, T, topo):
             dma(qs[r], y[:, 1024 * ch:1024 * (ch + 1)], T.OUT[5 + r::16, 1024 * ch:1024 * (ch + 1)],
                 keys("OUT%d" % ch, 0, 64), [])
     ulist("S", "b", 0); ulist("V", "a", 0)
-    get(0, 0, 8, "V"); get(0, 8, 40)
-    ulist("S", "b", 1)
-    get(0, 40, 64)
-    ulist("S", "a", 1)
+    get(0, 0, 8, "V"); get(0, 8, 32); get(0, 32, 48)
+    ulist("S", "b", 1); ulist("V", "a", 1)
+    get(0, 48, 64)
     put(0, "YYY")
     get(1, 0, 32); get(1, 32, 64)
     put(1, "YSY")
-    for j in order(calls, landing):
-        calls[j][1]()
+    if not ORDER:
+        ORDER.extend(order(calls))
+    for j, e in ORDER:
+        calls[j][1](e)
     ends["sent"] = sent[0]
     for s, v in ends.items():
         if max(x.get(s, 0) for x in seen.values()) < v:

import numpy as np
from concourse.mybir import AluOpType as A, ActivationFunctionType as AF

M = 4096
SO = 4112
HALF = 2048
COL = HALF + 0.25
PEN = 16384.0
BIG = 16.0
LIFT = 4096.0
MAGIC = 1.5 * 2.0 ** 27
SC = 2.0 ** -13
OPT = {"route": "abdd", "order": "0kst123"}
CYC, HOP, TRIES = 0.83e-3, 0.25, 20000
PACES = ((1.0, 1.25, 2.6, 0.3 / 76, 0.25, 1.0), (1.3, 1.8, 2.8, 0.25 / 103, 0.2, 1.25),
         (1.25, 1.5, 5.3, 0.25 / 100, 0.28, 1.0), (1.1, 1.4, 3.6, 0.2 / 86, 0.22, 1.35))
GATHERED = ("Ma", "Mb", "NF", "FL", "KB", "OB", "OUT")
NDMA = 40


def _sb(n, dt):
    return ("sbuf", [128] + (n if isinstance(n, list) else [n]), dt)


SCRATCH = {}
for _dt, _list in (
        ("bfloat16", dict(H=2 * SO, Z=1312, IB=128, SF=8, SZ=8, NF=3584, FL=7168, F1=64, F2=[16, 8], S2=512, KB=1024,
                          ONE=512, CODE=128, J=160, J2=128, J4=128, JT=64)),
        ("float16", dict(W16=2064, MA=2048, MB=2048, I16=128, I8=[16, 8], R2=128, R2S=128, R4=128, R4S=128, R4W=128,
                         LT=128, ON=128, IP=128, IN=128, SA=32, SB=32, I256=128, BK=2 * 908, M4=128, M16=128,
                         CDS=32, C25=32, ZERO=512, PQ=[163, 8], PC0=[81, 16], PC1=[81, 16], ZQ=[256, 8], ZP=[35, 4],
                         GQ=[65, 8], GC=512, K=128, C4=128, C16=256, MR=1024, E=32, U=512, L=512, N=512, SL=256,
                         LF=512, KC=1024, Ca=1024, Cb=1024, Za=[136, 16], Zb=[136, 16])),
        ("float32", dict(TA=4104, TB=4104, W=5152, IDR=256, IDT=256, CD=32, col=64, ZC=516, D=1024, OUT=2048, OB=2048,
                         IDN=256, SZU=512, st=64)),
        ("int32", dict(ki=512, sai=64, pci=8)),
        ("uint16", dict(UAB=256, UL=768, UP=64))):
    for _k, _n in _list.items():
        SCRATCH[_k] = _sb(_n, _dt)
for _b in range(8):
    SCRATCH["ps%d" % _b] = ("psum", [128, 512], "float32")
SEMAPHORES = (["cV", "cS", "cP", "cG", "sent", "rk", "rs", "rt", "hout"] + ["rh%d" % k for k in range(4)]
              + ["hi%d" % k for k in range(4)] + ["d%d" % i for i in range(NDMA)])


def quarter(k):
    return slice(1024 * k, 1024 * (k + 1) if k < 3 else SO)


def routes(src, dst, T, topo):
    ok = [c for c in topo.cores_of(src) if c != src and T.rank_of(c) is None and topo.may_write(c, dst)]
    other = [c for c in ok if topo.die(c) != topo.die(src)]
    same = [c for c in ok if topo.die(c) == topo.die(src)]
    pick = {"d": None, "a": other[0], "b": other[-1], "x": same[0] if same else None}
    return [pick[c] for c in OPT["route"]]


def bits(m):
    return bin(m).count("1")


def near_mask(src, helper, dst, topo):
    return topo.mask(src, helper) & ~topo.mask(src, dst)


def helper_program(g, core, T, topo):
    n = len(T.cores)
    out = 0
    for r in range(n):
        src, dst = T.cores[r], T.cores[(r - 1) % n]
        for k, h in enumerate(routes(src, dst, T, topo)):
            if h == core:
                q = quarter(k)
                g.wait_ge(T.sem["hi%d" % k], bits(near_mask(src, core, dst, topo)))
                rid, pid, _ = topo.addr(dst)
                m = topo.mask(core, dst)
                g.remote_dma(T.H[:, SO + q.start:SO + q.stop], T.H[:, q], T.sem["rh%d" % k], T.sem.hout, pid, rid, m)
                out += bits(m)
    if out:
        g.wait_ge(T.sem.hout, out)


ORDER = []


def order(calls):
    n = len(calls)
    pre, wr, rd, last = [], {}, {}, {}
    ready = [0.0] * n
    for j, (e, _, reads, writes, banks, dur, lat, either) in enumerate(calls):
        p = {}
        for k in reads:
            if k in wr:
                p[wr[k]] = 1
        for k in writes:
            for i in ([wr[k]] if k in wr else []) + rd.get(k, []):
                p[i] = 1
        for b in banks + ([e] if e in "GY" else []):
            if b in last:
                p.setdefault(last[b], int(calls[last[b]][0] != e or either or calls[last[b]][7]))
            last[b] = j
        for k in reads:
            rd.setdefault(k, []).append(j)
        for k in writes:
            wr[k], rd[k] = j, []
        p.pop(j, None)
        pre.append(p)
    on, lag = [c[0] for c in calls], [c[6] for c in calls]
    mean = [sum(c[5]) / len(PACES) for c in calls]
    ahead, behind = [[] for _ in range(n)], [[] for _ in range(n)]
    for j in range(n):
        for i, waits in pre[j].items():
            ahead[i].append((j, mean[i] + waits * (HOP + lag[i])))
            behind[j].append((i, mean[j] + waits * (HOP + lag[i])))
    links = [[[(i, calls[i][5][k] + waits * (PACES[k][4] + PACES[k][5] * lag[i])) for i, waits in p.items()] for p in pre]
             for k in range(len(PACES))]

    def place(turn, after, before, start):
        left, at = [len(x) for x in before], list(start)
        free, busy = [(turn[j], j) for j in range(n) if not left[j]], {e: [] for e in "VSPGY"}
        while free:
            x = min(free)
            free.remove(x)
            j = x[1]
            t, q = at[j], busy[on[j]]
            k = len(q)
            while k and q[k - 1][1] > t:
                k -= 1
            while k < len(q) and t + mean[j] > q[k][0] + 1e-9:
                t = max(t, q[k][1])
                k += 1
            q.insert(k, (t, t + mean[j]))
            at[j] = t
            for i, w in after[j]:
                at[i] = max(at[i], t + w)
                left[i] -= 1
                if not left[i]:
                    free.append((turn[i], i))
        return at

    def tighten(at):
        back = place([-at[j] - mean[j] for j in range(n)], behind, ahead, lag)
        return place([-back[j] - mean[j] for j in range(n)], ahead, behind, ready)

    def length(at):
        turns, total = sorted(range(n), key=lambda j: (at[j], j)), 0.0
        for k, pace in enumerate(PACES):
            begin, free = list(ready), dict.fromkeys("VSPGY", 0.0)
            for j in turns:
                t = max(begin[j], free[on[j]])
                for i, w in links[k][j]:
                    if begin[i] + w > t:
                        t = begin[i] + w
                begin[j], free[on[j]] = t, t + calls[j][5][k]
            total += free["Y"] * pace[3]
        return total
    at = tighten(place(range(n), ahead, behind, ready))
    now = least = length(at)
    best, either = (at, list(on)), [j for j in range(n) if calls[j][7]]
    rng = np.random.RandomState(n)
    for it in range(TRIES):
        turn, was = list(at), list(on)
        if it % 4 == 0:
            for j in rng.choice(either, 1 + it % 8 // 4):
                on[j] = "V" if on[j] == "S" else "S"
        else:
            lo, shift = int(rng.randint(n)), float(rng.uniform(-1, 1) * rng.choice((0.4, 1.0, 3.0)))
            for j in range(lo, min(n, lo + int(rng.choice((1, 2, 4, 8, 20, 60))))):
                turn[j] += shift
        x = place(turn, ahead, behind, ready)
        if it % 15 == 0:
            x = tighten(x)
        v = length(x)
        if v <= now + 0.0006 * (1 - it / TRIES) * rng.random_sample():
            at, now = x, v
            if v < least:
                best, least = (x, list(on)), v
        else:
            on[:] = was
    return [(j, best[1][j]) for j in sorted(range(n), key=lambda j: (best[0][j], j))]


def rank_program(g, core, T, topo):
    rank = T.rank_of(core)
    if rank is None:
        helper_program(g, core, T, topo)
        return
    n = len(T.cores)
    dst, src = T.cores[(rank - 1) % n], T.cores[(rank + 1) % n]
    V, S = g.vector, g.scalar
    eng = {"V": V, "S": S, "P": g.tensor, "G": g, "Y": g.sync}
    ps = [T["ps%d" % b] for b in range(8)]
    cnt = {"V": 0, "S": 0, "P": 0, "G": 0}
    seen = {e: {} for e in eng}
    wr, rd, bank, ends = {}, {}, {}, {}
    ndma, sent = [0], [0]

    def need(e, reads, writes=(), banks=()):
        ev = []
        for k in reads:
            ev += wr[k]
        for k in writes:
            ev += wr.get(k, []) + rd.get(k, [])
        for b in banks:
            ev += [x for o, x in bank.get(b, {}).items() if o != e]
        top = {}
        for s, v in ev:
            top[s] = max(top.get(s, 0), v)
        for s, v in top.items():
            if seen[e].get(s, 0) < v:
                eng[e].wait_ge(T.sem[s], v)
                seen[e][s] = v

    def done(e, ev, reads, writes, banks):
        for k in reads:
            rd.setdefault(k, []).append(ev)
        for k in writes:
            wr[k] = [ev]
            rd[k] = []
        for b in banks:
            bank.setdefault(b, {})[e] = ev
        ends[ev[0]] = max(ends.get(ev[0], 0), ev[1])

    def issue_op(e, fn, reads, writes, banks):
        need(e, reads, writes, banks)
        cnt[e] += 1
        fn().then_inc(T.sem["c" + e], 1)
        done(e, ("c" + e, cnt[e]), reads, writes, banks)

    def issue_mm(groups, reads, b, opens, closes):
        need("P", reads, [], [b])
        for grp in groups:
            for j, (o, l, r) in enumerate(grp):
                last = g.tensor.matmul(o, l, r, opens and j == 0, closes and j == len(grp) - 1)
        cnt["P"] += 1
        last.then_inc(T.sem.cP, 1)
        done("P", ("cP", cnt["P"]), reads, [], [b])

    def issue_dma(e, out, in_, reads, writes):
        need(e, reads, writes)
        s = "d%d" % ndma[0]
        ndma[0] += 1
        eng[e].dma_start(out, in_).then_inc(T.sem[s], 16)
        done(e, (s, 16), reads, writes, [])

    def issue_send(to, out, in_, sem, reads, m):
        need("G", reads)
        rid, pid, _ = topo.addr(to)
        m = m or topo.mask(core, to)
        g.remote_dma(out, in_, T.sem[sem], T.sem.sent, pid, rid, m)
        sent[0] += bits(m)

    calls = []

    def width(ap):
        w = 1
        for x in ap.shape[1:]:
            w *= x
        return w

    def op(e, fn, reads, writes, banks=(), n=64, per=1.0):
        kind = 1 if writes[0].startswith(GATHERED) and not banks else 2 if writes[0] == "W" else 0
        either = isinstance(fn, dict)
        calls.append((e, lambda on: issue_op(on, fn[on] if either else fn, reads, writes, banks), reads, writes,
                      list(banks), [(70 + n * x[kind] if kind else max(64, n * per)) * CYC * x[0] for x in PACES], 0.0,
                      either))

    def mm(groups, reads, b, opens=True, closes=True):
        cycles = sum(max(64, width(x[0])) for grp in groups for x in grp) / 2
        calls.append(("P", lambda on: issue_mm(groups, reads, b, opens, closes), reads, [], [b],
                      [cycles * CYC * x[0] for x in PACES], 0.0, False))

    def dma(e, out, in_, reads, writes, lat=2.5):
        calls.append((e, lambda on: issue_dma(e, out, in_, reads, writes), reads, writes, [], [0.08] * len(PACES), lat,
                      False))

    def send(to, out, in_, sem, reads, lands, lag, m=None):
        first = not any(c[6] for c in calls if c[0] == "G")
        calls.append(("G", lambda on: issue_send(to, out, in_, sem, reads, m), reads, lands, [],
                      [(1.8 if first else 0.6) * x[5] for x in PACES], lag, False))

    def arrives(names, sem, frm):
        for key in names:
            wr[key] = [(sem, bits(topo.mask(frm, core)))]
        ends[sem] = bits(topo.mask(frm, core))

    def ts(out, in0, s1, s2, o0, o1, reads, writes, banks=()):
        op("V", lambda: V.tensor_scalar(out, in0, s1, s2, o0, o1), reads, writes, banks, width(out),
           1.0 if banks else 0.5)

    def t1(out, in0, s1, o0, reads, writes, banks=()):
        op("V", lambda: V.tensor_scalar(out, in0, s1, None, o0), reads, writes, banks, width(out),
           0.5 if writes[0].startswith("MR") else 1.0)

    def tt(out, in0, in1, o, reads, writes, banks=()):
        op("V", lambda: V.tensor_tensor(out, in0, in1, o), reads, writes, banks, width(out))

    def cp(out, in_, reads, writes, banks=()):
        op("V", lambda: V.tensor_copy(out, in_), reads, writes, banks, width(out))

    def act(out, in_, scale, reads, writes, banks=()):
        op("S", lambda: S.activation(out, in_, AF.Copy, scale=scale), reads, writes, banks, width(out))

    def add(e, out, in_, c, reads, writes, banks=()):
        op(e, {"V": lambda: V.tensor_scalar(out, in_, c, None, A.add),
               "S": lambda: S.activation(out, in_, AF.Identity, bias=bias[c])}, reads + ["bias"], writes, banks,
           width(out))

    def move(e, out, in_, reads, writes, banks=(), c=1.0):
        op(e, {"V": lambda: V.tensor_scalar(out, in_, c, None, A.mult),
               "S": lambda: S.activation(out, in_, AF.Copy, scale=c)}, reads, writes, banks, width(out))

    def fill(out, c, key):
        op("V", lambda: V.memset(out, c), [], [key], (), width(out), 0.5)

    def keys(name, lo, hi):
        return ["%s_%d" % (name, k) for k in range(lo // 8, (hi + 7) // 8)]

    def num(name, js):
        return [name + str(j) for j in js]

    def clear(b, w=448):
        mm([[(ps[b][:, 0:w], T.ZERO[:, 0:128], T.ZERO[:, 0:w])]], ["ZERO"], b, True, False)

    arrives(["Cb0", "Cb1"], "rk", src)
    arrives(["Cb2", "Cb3"], "rs", src)
    arrives(["Cb4", "Cb5"], "rt", src)
    for k, h in enumerate(routes(src, core, T, topo)):
        arrives(["Hf%d" % k], "rh%d" % k, src if h is None else h)

    def ho(k):
        return ["Hx%d" % k, "Ho%d" % k]
    HALL = [x for k in range(4) for x in ho(k)] + num("Hf", range(4)) + ["Hd"]

    dma("S", T.ki[:, 0:256], T.kl[:], [], ["kl"], 1.9)
    dma("Y", T.ki[:, 256:512], T.kr[:], [], ["kr"], 1.9)
    for k in range(4):
        c = slice(1024 * k, 1024 * (k + 1))
        for j, key in enumerate(ho(k)):
            dma("Y", T.H[j::2, c], T.h[(j + rank) % 2::2, c], [], [key], 3.1 + 0.78 * k)
    dma("Y", T.sai[:, 0:32], T.sa[:], [], ["sa"], 6.0)
    dma("Y", T.sai[:, 32:64], T.sb[:], [], ["sb"], 6.0)

    op("G", lambda: g.iota(T.pci[:, 0:1], [[1, 1]], 0, 1), [], ["pci0"])
    for t, pat, base, mult, key in (
            (T.J[:], [[1, 160]], 0, 0, "J"), (T.IDR[:], [[1, 256]], -HALF, 256, "IDR"),
            (T.IDT[:], [[128, 2], [0, 8], [256, 16]], -HALF, 1, "IDT"),
            (T.JT[:, 0:32], [[1, 4], [16, 8]], 0, 0, "JA"), (T.JT[:, 32:64], [[-1, 4], [16, 8]], 3, 0, "JB"),
            (T.J2[:], [[1, 2], [2, 64]], 0, 0, "J2"), (T.J4[:], [[1, 4], [4, 32]], 0, 0, "J4"),
            (T.CD[:], [[0, 8], [2, 4]], HALF + 16, 8, "CD")):
        op("G", lambda a=(t, pat, base, mult): g.iota(*a, allow_small_or_imprecise_dtypes=True), [], [key], (),
           width(t) + 80, 2.0)
    fill(T.ZERO[:], 0.0, "ZERO")
    clear(6, 512); clear(7, 128); clear(4, 128)
    col, pci, J = T.col, T.pci, T.J
    SH, AND = A.arith_shift_right, A.bitwise_and
    bias = {}
    for j, c in enumerate((COL, COL + 16, LIFT, -LIFT, 1.0)):
        bias[c] = col[:, 56 + j:57 + j]
        fill(bias[c], c, "bias%d" % j)
    t1(pci[:, 1:2], pci[:, 0:1], 15, AND, ["pci0"], ["pci1"])
    t1(pci[:, 2:3], pci[:, 0:1], 4, SH, ["pci0"], ["pci2"])
    t1(pci[:, 3:4], pci[:, 0:1], 3, AND, ["pci0"], ["pci3"])
    ts(pci[:, 4:5], pci[:, 0:1], 3, 1, SH, AND, ["pci0"], ["pci4"])
    fill(T.Z[:], 0.0, "Z")
    cp(col[:, 0:5], pci[:, 0:5], num("pci", range(5)) + num("bias", range(5)), ["c_p", "bias"])
    c_p, c_pm, c_g, c_r, c_v, c_g17, c_gm, c_pp = (col[:, j:j + 1] for j in range(8))
    oh = [col[:, 8 + j:9 + j] for j in range(16)]
    t1(c_gm, c_g, -float(M), A.mult, ["c_p"], ["c_gm"])
    t1(col[:, 8:24], J[:, 0:16], c_pm, A.is_equal, ["J", "c_p"], ["oh"])
    t1(T.I16[:], J[:, 0:128], c_p, A.is_equal, ["J", "c_p"], ["I16"])
    ts(ps[5][:, 0:256], T.IDR[:], c_gm, 1.0 / HALF, A.add, A.mult, ["IDR", "c_gm"], ["own"], [5])
    tt(ps[5][:, 0:1], ps[5][:, 0:1], oh[8], A.add, ["own", "oh"], ["own"], [5])
    t1(T.U[:], T.ki[:], -float(HALF), A.add, ["kl", "kr"], ["U"])
    ts(T.SZ[:], J[:, 0:8], c_g, 1.0 / 256, A.is_equal, A.mult, ["J", "c_p"], ["SZ"])
    ts(T.I8[:], J[:, 0:128], c_p, -PEN / HALF, A.is_equal, A.mult, ["J", "c_p"], ["I8"])

    ts(T.L[:], T.U[:], -float(HALF), float(HALF), A.is_equal, A.mult, ["U"], ["L"])
    ts(T.N[:], T.U[:], 0.0, float(HALF), A.is_equal, A.mult, ["U"], ["N"])
    tt(T.SL[:], ps[5][:, 0:256], T.L[:, 0:256], A.mult, ["own", "L"], ["SL"], [5])
    for t, w in ((T.U, 4), (T.L, 4), (T.N, 4), (T.SL, 2)):
        mm([[(ps[6][:, 128 * j:128 * j + 128], t[:, 128 * j:128 * j + 128], T.I16[:]) for j in range(w)]],
           [t.name, "I16"], 6, False, w == 2)
    act(T.Ca[:, 0:512], ps[6][:, 0:512], 1.0, [], ["Ca0", "Ca1"], [6])

    def zrow(x, r, h):
        return T["Z" + x][:, 8 * h + r:128:16, :]

    def spread(e, x, j):
        for h in range(2):
            move(e, zrow(x, j + 1, h), T["C" + x][:, 256 * j + 128 * h:256 * j + 128 * h + 128], ["C%s%d" % (x, j)],
                 ["Z%s%d_%d" % (x, j + 1, h)])

    def spread_keys(es, x, u):
        for j in range(4):
            o = 512 + 256 * u + 64 * j
            move(es[j], T["Z" + x][:, 8 * (j % 2) + 3 + j // 2:128:16, 8 * u:8 * u + 8], T["C" + x][:, o:o + 64],
                 ["C%s%d" % (x, 2 + 2 * u + j // 2)], ["Y%s%d_%d" % (x, u, j)])

    TAB = {"a": T.TA, "b": T.TB}

    def table(x, u, banks, es):
        z, t = T["Z" + x], TAB[x]
        rk = (["Z%s%d_%d" % (x, r, h) for r in range(3) for h in range(2)] + num("Y%s%d_" % (x, u), range(4))
              + num(z.name, "567p") + ["I16"])
        for q in range(4 * u, 4 * u + 4):
            mm([[(ps[banks[q]][:, 128 * j:128 * (j + 1)], z[:, 8 * (j % 2):8 * (j % 2) + 128, 2 * q + j // 2], T.I16[:])]
                for j in range(4)], rk, banks[q])
            lo = int(q == 4)
            move(es[q], t[:, 512 * q + lo:512 * (q + 1)], ps[banks[q]][:, lo:512], [], ["T%s%d" % (x, q)], [banks[q]])
            if lo:
                t1(t[:, M:M + 1], ps[banks[q]][:, 0:1], col[:, 25:26], A.add, ["fix"], ["T%sd" % x], [banks[q]])
    TK = {x: num("T" + x, range(8)) + ["T%sd" % x, "T%se" % x] for x in "ab"}

    def sizes(k):
        b = (7, 4)[k // 2]
        mm([[(ps[b][:, 64 * h + i % 8:64 * h + 64:8], T.H[:, 256 * i + 128 * h:256 * i + 128 * h + 128], T.SZ[:])
             for i in range(4 * k, 4 * k + 4) for h in range(2)]], ["SZ"] + ho(k), b, False, False)

    def opening(u):
        b, o = (7, 4)[u], 512 + 256 * u
        mm([[(ps[b][:, 64 * h:64 * h + 64], T.L[:, 128 * h:128 * h + 128], T.I8[:, u::2, :]) for h in range(2)]],
           ["L", "I8"], b, False, u == 0)
        if u:
            sizes(2)
            fill(T.H[:, M:SO], -262144.0, "Hpad")
            cp(T.H[:, M:M + 1], T.H[:, HALF:HALF + 1], ho(2) + ["Hpad"], ["Hd"])
            fill(T.H[:, HALF:HALF + 1], -262144.0, "Ho2")
            sizes(3)
            mm([[(ps[b][:, 0:64], T.ZERO[:, 0:128], T.ZERO[:, 0:64])]], ["ZERO"], b, False, True)
        ts(T.Ca[:, o:o + 128], ps[b][:, 0:128], MAGIC, -MAGIC, A.add, A.add, [], ["Ca%d" % (2 + 2 * u)], [b])
        tt(T.Ca[:, o + 128:o + 256], ps[b][:, 0:128], T.Ca[:, o:o + 128], A.subtract, ["Ca%d" % (2 + 2 * u)],
           ["Ca%d" % (3 + 2 * u)], [b])

    sizes(0); sizes(1)
    opening(0); opening(1)
    rt = routes(core, dst, T, topo)
    for x in OPT["order"]:
        if x == "k":
            send(dst, T.Cb[:, 0:512], T.Ca[:, 0:512], "rk", ["Ca0", "Ca1"], ["Cb0", "Cb1"], 2.2)
        elif x in "st":
            o = 512 + 256 * "st".index(x)
            js = (o // 128 - 2, o // 128 - 1)
            send(dst, T.Cb[:, o:o + 256], T.Ca[:, o:o + 256], "r" + x, num("Ca", js), num("Cb", js), 2.0)
        else:
            q = quarter(int(x))
            rk = ho(int(x)) + (["Hd"] if x == "3" else [])
            if rt[int(x)] is None:
                send(dst, T.H[:, SO + q.start:SO + q.stop], T.H[:, q], "rh" + x, rk, ["Hf" + x], 5.0)
            else:
                send(rt[int(x)], T.H[:, q], T.H[:, q], "hi" + x, rk, ["Hf" + x], 7.5,
                     near_mask(core, rt[int(x)], dst, topo))
    for x in "ab":
        z = T["Z" + x]
        for h in range(2):
            act(zrow(x, 0, h), T.IDT[:, 128 * h:128 * h + 128], 1.0, ["IDT"], ["Z%s0_%d" % (x, h)])
        for r in (5, 6, 7):
            fill(z[:, r::8, :], 0.0, z.name + str(r))
        fill(z[:, 128:133, :], 0.0, z.name + "p")
        fill(TAB[x][:, HALF:HALF + 1], 0.0, "T%se" % x)
    t1(col[:, 25:26], oh[0], float(HALF), A.mult, ["oh"], ["fix"])
    for t, w in ((T.PQ, 1304), (T.PC0, 656), (T.PC1, 656)):
        act(t[:] if t is T.PQ else t[:, 0::2, :], T.Z[:, 0:w], 1.0, ["Z"], [t.name + "z"])
    act(T.GQ[:, 0::2, :], T.Z[:, 0:264], 1.0, ["Z"], ["GQz"])
    spread("S", "a", 0); spread("V", "a", 1)
    for u in range(2):
        spread_keys("VSVS", "a", u)
        table("a", u, (0, 1, 2, 3, 5, 6, 7, 4), "SVSVVSVS")
    spread("S", "b", 0); spread("V", "b", 1)
    clear(0)
    for u in range(2):
        spread_keys("VSVS", "b", u)
        table("b", u, (1, 2, 3, 5, 6, 7, 4, 1), "SVSVVSVS")
    op("S", lambda: S.activation(T.ZC[:], T.Z[:, 0:516], AF.Silu, bias=bias[LIFT]), ["Z", "bias"], ["ZC"], (), 2000)
    ts(T.st[:], T.sai[:], float(HALF), float(HALF), A.is_equal, A.mult, ["sa", "sb"], ["st"])
    tt(T.st[:], T.st[:], T.sai[:], A.add, ["st"], ["st"])
    cp(T.UAB[:, 0:32], T.st[:, 0:32], ["st"], ["Ua0"])
    cp(T.UAB[:, 128:160], T.st[:, 32:64], ["st"], ["Ub0"])
    tt(c_pp, c_p, oh[4], A.subtract, ["c_p", "oh"], ["c_pp"])
    ts(col[:, 24:25], c_pm, 2.5, -2.0, A.is_gt, A.mult, ["c_p"], ["sg"])
    t1(col[:, 24:25], col[:, 24:25], 1.0, A.add, ["sg"], ["sg"])
    t1(T.SA[:], T.JT[:, 0:32], c_pp, A.is_equal, ["JA", "c_pp"], ["SA"])
    ts(T.SB[:], T.JT[:, 32:64], c_pp, col[:, 24:25], A.is_equal, A.mult, ["JB", "c_pp", "sg"], ["SB"])
    for t, j, w in ((T.R2, T.J2, 1.0), (T.R2S, T.J2, SO), (T.R4, T.J4, 1.0), (T.R4S, T.J4, SO), (T.R4W, T.J4, 1 / SC),
                    (T.I256, J, 256.0), (T.IB, J, 1.0), (T.IP, J, SC), (T.IN, J, -SC)):
        ts(t[:], j[:, 0:128], c_p, float(w), A.is_equal, A.mult, [j.name, "c_p"], [t.name])
    ts(T.SF[:], J[:, 0:8], c_g, BIG, A.is_equal, A.mult, ["J", "c_p"], ["SF"])
    ts(T.LT[:], J[:, 0:128], c_p, SC, A.is_gt, A.mult, ["J", "c_p"], ["LT"])
    t1(T.CDS[:], T.CD[:], SC, A.mult, ["CD"], ["CDS"])
    ts(T.IDN[:], T.IDR[:], c_gm, float(HALF), A.add, A.add, ["IDR", "c_gm"], ["IDN"])
    for t, c, key in ((T.ON[:], SC, "ON"), (T.C25[:], -HALF * SC, "C25"), (T.ONE[:], 1.0, "ONE"), (T.M4[:], 1.0, "M4"),
                      (T.M16[:], 1.0, "M16"), (T.ZQ[:, 3::8, :], 0.0, "ZQz"), (T.ZP[:], 0.0, "ZPz"),
                      (T.M4[:, 0:128:4], 0.0, "M4"), (T.M16[:, 0:128:16], 0.0, "M16")):
        fill(t, c, key)
    op("G", lambda: g.affine_select(T.S2[:], T.ONE[:], [[128, 2], [-1, 2], [1, 128]], A.is_equal, 0.0, 0, -2),
       ["ONE"], ["S2"], (), 600, 2.0)
    EDGE = (15, 14, 13, -1, -2, -3)

    def bk(v, w):
        o = 908 * v + (140 + 128 * EDGE.index(w) if w in EDGE else 12 - w)
        return T.BK[:, o:o + 128]
    ts(c_g17, c_g, 16.0, 17.0, A.mult, A.add, ["c_p"], ["c_g17"])
    t1(col[:, 28:30], J[:, 0:2], c_v, A.is_equal, ["J", "c_p"], ["ov"])
    t1(col[:, 32:35], J[:, 0:3], c_r, A.is_ge, ["J", "c_p"], ["mle"])
    t1(col[:, 35:38], J[:, 1:4], c_r, A.is_le, ["J", "c_p"], ["mge"])
    tt(col[:, 26:27], c_g17, c_r, A.add, ["c_g17", "c_p"], ["tg0"])
    ts(col[:, 30:32], col[:, 28:30], col[:, 26:27], -1.0, A.mult, A.add, ["ov", "tg0"], ["tg"])
    for v in range(2):
        t1(T.BK[:, 908 * v:908 * v + 140], J[:, 4:144], col[:, 30 + v:31 + v], A.is_equal, ["J", "tg"], ["BK%d" % (7 * v)])
        for j, w in enumerate(EDGE):
            ts(bk(v, w), J[:, 16 - w:144 - w], col[:, 30 + v:31 + v], col[:, 32 + j:33 + j], A.is_equal, A.mult,
               ["J", "tg", "mle", "mge"], ["BK%d" % (7 * v + 1 + j)])

    def true_sizes(j, x):
        C, out = T["C" + x], ps[2 + j]
        ts(T.LF[:, 256 * j:256 * j + 256], C[:, 256:512], 0.0, PEN, A.is_equal, A.mult, ["C%s1" % x], ["LF" + x])
        for k in range(4):
            cp(T.KC[:, 512 * j + 128 * k:512 * j + 128 * k + 128], zrow(x, 3 + k // 2, k % 2),
               ["Y%s%d_%d" % (x, u, k) for u in range(2)], ["KC%s%d" % (x, k)])
        mm([[(out[:, 128 * h:128 * h + 128], t[:, o + 128 * h:o + 128 * h + 128], T.I256[:])
             for t, o in ((T.KC, 512 * j), (T.KC, 512 * j + 256), (T.LF, 256 * j))] for h in range(2)],
           ["I256", "LF" + x] + num("KC" + x, range(4)), 2 + j)
        act(T.SZU[:, 256 * j:256 * (j + 1)], out[:, 0:256], 1.0, [], ["SZU" + x], [2 + j])

    def refill(after=()):
        for k in range(4):
            dma("Y", T.W[:, 516 * k:516 * (k + 1)], T.ZC[:], ["ZC"] + list(after), ["Wz%d" % k], 2.2 + 0.9 * k)

    NB, CH = (8, 8, 4, 8), (0, 1, 0, 0)
    PT = (T.PC0, T.PC1, T.PQ, T.PC0)
    NFO, FLO = (0, 1024, 2048, 2560), (0, 2048, 4096, 5120)
    MX, UO = {"a": T.MA, "b": T.MB}, {"a": 0, "b": 128}
    LB = {"b": (6, 2), "a": (7, 3)}

    def ulist(e, x, ch):
        add(e, T.UAB[:, UO[x] + 64 * ch:UO[x] + 64 * ch + 64], ps[LB[x][ch]][:, 448:512], COL, [], ["U%s%d" % (x, ch)],
            [LB[x][ch]])

    def tab(x, ch, lo, hi):
        u = UO[x] + 64 * ch
        return TAB[x][:, 0:M + 1].indirect(T.UAB[:, u + lo:u + hi])

    def rows(e, x, ch, lo, hi):
        o = 1024 * ch
        move(e, MX[x][:, o + 16 * lo:o + 16 * hi], tab(x, ch, lo, hi), TK[x] + ["U%s%d" % (x, ch)],
             keys("M%s%d" % (x, ch), lo, hi))

    def turn(s, x, closes):
        B, ch = NB[s], CH[s]
        o, c = 1024 * ch, (24 * B if x == "b" else 0)
        mm([[(ps[ch][:, c + b:c + 32 * B:B], MX[x][:, o + b:o + 128 * B:B], (T.SB if x == "b" else T.SA)[:])
             for b in range(B)]], keys("M%s%d" % (x, ch), 0, 8 * B) + ["SA", "SB"], ch, False, closes)

    def pk(s, k, side):
        return "%s_%d_%d" % (PT[s].name, k, side)

    def pw(s, k, side):
        U = 16 // NB[s]
        return PT[s][:, 8 * U * k + U - 1:8 * U * (k + 1):U, side::2]

    MASK, KA, KB, XA, XB = range(5)
    STAY, LEFT, RIGHT = ((XB, 0), (XA, 0)), ((KA, 0), (KB, 0)), ((KA, 1), (KB, 1))

    def val(s, v):
        return ps[CH[s]][:, 8 * NB[s] * v:8 * NB[s] * (v + 1)]

    def masks(s):
        z = [PT[s].name + "z"]
        t1(pw(s, MASK, 0), val(s, 3), 0.0, A.is_ge, z, [pk(s, MASK, 0)], [CH[s]])
        t1(pw(s, MASK, 1), val(s, 3), 0.0, A.is_lt, z, [pk(s, MASK, 1)], [CH[s]])

    def prods(s, which, next_lists=False):
        for k, side in which:
            v, m = {KA: (1 + side, 0), KB: (5 - side, 1), XA: (0, 1), XB: (6, 0)}[k]
            out, key = pw(s, k, side), pk(s, k, side)
            if next_lists:
                out = T.GQ[:, 16 * k - 15:16 * k:2, side::2] if s == 2 else T.GC[:, 128 * k - 128 + side:128 * k:2]
                key = "G%d_%d_%d" % (s, k, side)
            tt(out, val(s, v), pw(s, MASK, m), A.mult, [pk(s, MASK, m), "GQz"], [key], [CH[s]])

    def tlist(s, j, b):
        B = NB[s]
        U, N = 16 // B, 8 * B
        r1, rs = ((T.R2, T.R2S) if U == 2 else (T.R4, T.R4S))
        terms = ((MASK, 0, rs), (XB, 0, r1), (XA, 0, r1)) if j == 2 else ((MASK, 1, rs), (KA, j, r1), (KB, j, r1))
        mm([[(ps[b][:, 64 * j:64 * j + N], PT[s][:, 8 * U * k + U - 1 - i:8 * U * (k + 1) + U - 1 - i, side::2],
              r[:, N * i:N * (i + 1)]) for k, side, r in terms for i in range(U)]],
           [pk(s, k, side) for k, side, r in terms] + [r1.name, rs.name], b)

    def ut(e, s, j, b):
        N = 8 * NB[s]
        add(e, T.UL[:, 192 * s + 64 * j:192 * s + 64 * j + N], ps[b][:, 64 * j:64 * j + N], COL, [],
            ["UL%d_%d" % (s, j)], [b])

    def grow(s, x, to):
        ks = (KA, XA) if x == "a" else (KB, XB)
        if s == 2:
            terms = [(T.GQ[:, 16 * k - 15 - i:16 * k + 1 - i, :], T.R2[:, 64 * i:64 * i + 64]) for k in ks for i in range(2)]
        else:
            terms = [(T.GC[:, 128 * k - 128:128 * k], T.I16[:, 64 * to:64 * to + 64]) for k in ks]
        mm([[(ps[LB[x][to]][:, 448:512], l, r) for l, r in terms]],
           ["G%d_%d_%d" % (s, k, side) for k in ks for side in range(2)] + ["R2", "I16"], LB[x][to])

    def cands(s):
        js = [((KA, 0), (XA, 0)), ((KA, 1), (XA, 0)), ((KB, 0), (XB, 0)), ((KB, 1), (XB, 0))]
        mm([[(ps[2 + s][:, 64 * j:64 * j + 64], T.I16[:], pw(s, k, side)) for k, side in x] for j, x in enumerate(js)],
           [pk(s, k, side) for x in js for k, side in x] + ["I16"], 2 + s)

    def fixed(s, lo, hi):
        o, u = NFO[s], 192 * s + 128
        move("S", T.NF[:, o + 16 * lo:o + 16 * hi], T.H[:, :].indirect(T.UL[:, u + lo:u + hi]),
             HALL + ["UL%d_2" % s], keys("NF%d" % s, lo, hi), (), -1.0)

    def test(s, side, lo, hi):
        o, u, f = NFO[s], 192 * s + 64 * side, FLO[s] + 128 * NB[s] * side
        tt(T.FL[:, f + 16 * lo:f + 16 * hi], T.H[:, :].indirect(T.UL[:, u + lo:u + hi]), T.NF[:, o + 16 * lo:o + 16 * hi],
           A.is_lt, HALL + ["UL%d_%d" % (s, side)] + keys("NF%d" % s, lo, hi), keys("FL%d_%d" % (s, side), lo, hi))

    def test_s(s, side, lo, hi, b):
        o, u, f, w = NFO[s] + 16 * lo, 192 * s + 64 * side, FLO[s] + 128 * NB[s] * side + 16 * lo, 16 * (hi - lo)
        kb, out = T.KB[:, 512 * b:512 * b + w], ps[b][:, 0:w]
        act(kb, T.H[:, :].indirect(T.UL[:, u + lo:u + hi]), -1.0, HALL + ["UL%d_%d" % (s, side)], ["KB%d" % b])
        mm([[(out, T.IB[:], T.NF[:, o:o + w]), (out, T.IB[:], kb)]], ["KB%d" % b, "IB"] + keys("NF%d" % s, lo, hi), b)
        return lambda: op("S", lambda: S.activation(T.FL[:, f:f + w], out, AF.Relu), [],
                          keys("FL%d_%d" % (s, side), lo, hi), [b], w)

    def carry(b, terms, reads):
        mm([[(ps[b][:, 0:128], T.IB[:], T.Z[:, 0:128])]
            + [(ps[b][:, side:128:2], l, r) for side in range(2) for l, r in terms]], ["IB", "Z"] + reads, b, True, False)

    def fails(s, side, b, alone, closes):
        B = NB[s]
        f = FLO[s] + 128 * B * side
        x = [(ps[b][:, 2 * j + side:16 * B:2 * B], T.FL[:, f + j:f + 128 * B:B], T.SF[:]) for j in range(B)]
        rk = keys("FL%d_%d" % (s, side), 0, 8 * B) + ["SF"]
        if alone:
            mm([[y] for y in x], rk, b)
        else:
            mm([x], rk, b, False, closes)

    def kept(s):
        f = ps[4 + s][:, 0:128]
        op("V", {"V": lambda: V.tensor_scalar(T.K[:], f, 0.0, None, A.is_equal),
                 "S": lambda: S.activation(T.K[:], f, AF.Relu, bias=bias[1.0], scale=-1.0)}, ["bias"], ["K"], [4 + s], 128)

    def counts(s):
        for out, m, key in ((T.C4[:], T.M4, "C4"), (T.C16[:, 128 * s:128 * (s + 1)], T.M16, "C16_%d" % s)):
            op("V", lambda out=out, m=m: V.tensor_tensor_scan(out, m[:], T.K[:], 0.0, A.mult, A.add), ["K", m.name], [key])

    def codes(s):
        p = ps[6 + s]
        if s == 0:
            tt(T.CODE[:], ps[4][:, 0:128], T.C4[:], A.add, ["C4"], ["CODE"], [4])
        else:
            for j in range(4):
                c = ps[3][:, 64 * j:64 * j + 64]
                tt(c, c, T.K[:, j % 2:128:2], A.mult, ["K"], ["CV%d" % j], [3])
        tt(T.E[:], T.CDS[:], T.C4[:, 3:128:4], A.subtract, ["CDS", "C4"], ["E"])
        x = [(p[:, 0:32], T.I16[:], T.C25[:]), (p[:, 0:32], T.IP[:], T.C16[:, 128 * s + 3:128 * s + 128:4]),
             (p[:, 0:32], T.IN[:], T.C4[:, 3:128:4])]
        for t in range(s + 1):
            x += [(p[:, j:32:4], (T.LT if t == s else T.ON)[:], T.C16[:, 128 * t + 15:128 * t + 128:16]) for j in range(4)]
        mm([x], ["I16", "C25", "IP", "IN", "LT", "ON", "C4"] + num("C16_", range(s + 1)), 6 + s)

    def ranks(s):
        for r in range(4):
            o = 512 * s + 128 * r
            c = (T.CODE, T.C4)[s]
            t1(T.MR[:, o:o + 128], c[:], r + 1.0, A.is_equal, [c.name], ["MR%d_%d" % (s, r)])

    ROWS = [(r, side, v) for r in range(4) for side in range(2) for v in range(2) if r < 3 or side]

    def pack(s, lo, hi):
        for r, side, v in ROWS[lo:hi]:
            row, o, c = 8 * v + 4 * side + r, 512 * s + 128 * r, 128 * v + 64 * side
            tt(T.ZQ[:, 128 * s + row:128 * (s + 1):16, :], ps[2 + s][:, c:c + 64], T.MR[:, o + side:o + 128:2], A.mult,
               ["MR%d_%d" % (s, r), "ZQz"] + ["CV%d" % (c // 64)] * s, ["ZQ%d_%d" % (s, row)], [2 + s])

    def places(s):
        p = ps[6 + s]
        tt(T.ZP[:, 3::4, :], p[:, 0:32], T.E[:], A.max, ["E", "ZPz"], ["ZP"], [6 + s])
        mm([[(p[:, 64:96], T.ZP[:, 3 - i:35 - i, :], T.R4W[:, 32 * i:32 * (i + 1)]) for i in range(4)]],
           ["ZP", "R4W"], 6 + s)
        add("SV"[s], T.UP[:, 32 * s:32 * (s + 1)], p[:, 64:96], COL + 16, [], ["UP%d" % s], [6 + s])

    def scatter(s):
        zk = ["ZQ%d_%d" % (s, 8 * v + 4 * side + r) for r, side, v in ROWS]
        rk = ["UP%d" % s] + num("Wz", range(4))
        for lo, hi, b in ((0, 64, s), (64, 128, 4 + s)):
            mm([[(ps[b][:, 4 * lo + j:4 * hi:4], T.ZQ[:, 128 * s:128 * (s + 1), 2 * j + u], T.I16[:, lo:hi])
                 for u in range(2)] for j in range(4)], zk + ["I16"], b)
            rk.append("D%d_%d" % (s, lo))
            add("S" if b == 4 else "V", T.D[:, 512 * s + 4 * lo:512 * s + 4 * hi], ps[b][:, 4 * lo:4 * hi], LIFT, [], rk[-1:], [b])
        win, d = T.W[:, :].indirect(T.UP[:, 32 * s:32 * (s + 1)]), T.D[:, 512 * s:512 * (s + 1)]
        if s == 0:
            op("S", lambda: S.activation(win, d, AF.Silu), rk, ["W"], (), 512)
        else:
            op("V", lambda: V.tensor_copy(win, d), rk, ["W"], (), 512)

    def back(x, ch):
        v, o = "ab".index(x), 16 + 1024 * ch
        mm([[(ps[LB[x][ch]][:, 448:512], bk(v, w), T.W16[:, o + w:o + w + 1009:16]) for w in range(-3, 16)]],
           num("W16_", range(max(2 * ch - 1, 0), 2 * ch + 2)) + num("BK", range(7 * v, 7 * v + 7)), LB[x][ch])

    def reopen(more):
        if more:
            clear(0)
        for k, e in enumerate("VSVS"):
            lo, hi = (16 + 512 * k if k else 0), 528 + 512 * k
            add(e, T.W16[:, lo:hi], T.W[:, lo:hi], -LIFT, ["W"] + num("Wz", range(4)), ["W16_%d" % k])
        if more:
            refill()
        back("b", 0); back("a", 0); back("b", 1)

    def decide(s):
        masks(s); prods(s, STAY); tlist(s, 2, 6)
        prods(s, LEFT); prods(s, RIGHT)
        tlist(s, 0, 7); tlist(s, 1, 7)

    def last_rows():
        for j, x in enumerate("ab"):
            t, rk = TAB[x], ["T%s0" % x, "T%s1" % x]
            dma("Y", t[5 + j::16, 0:M], T.IDN[:], ["IDN"], rk[:1])
            dma("Y", t[7::16, 0:M], T.SZU[:, 256 * j:256 * (j + 1)], ["SZU" + x], rk[1:])

    def last_columns():
        for j, x in enumerate("ab"):
            t, rk = TAB[x], ["T%s0" % x, "T%s1" % x]
            cp(t[:, M:M + 1], t[:, HALF:HALF + 1], rk, ["T%sd" % x])
            t1(t[:, HALF:HALF + 1], oh[5 + j], -1.0, A.mult, rk + ["T%sd" % x], ["T%se" % x])

    def full(last):
        ulist("S", "b", 0); rows("S", "b", 0, 0, 40); rows("V", "b", 0, 40, 48)
        ulist("V", "a", 0); rows("V", "b", 0, 48, 64); rows("V", "a", 0, 0, 40); rows("S", "a", 0, 40, 64)
        turn(0, "b", False); turn(0, "a", True)
        back("a", 1)
        ulist("S", "b", 1)
        rows("V", "b", 1, 0, 24); rows("S", "b", 1, 24, 64)
        masks(0)
        ulist("S", "a", 1)
        prods(0, STAY); tlist(0, 2, 6)
        prods(0, LEFT); prods(0, RIGHT)
        tlist(0, 0, 7); tlist(0, 1, 7)
        rows("S", "a", 1, 48, 64); rows("V", "a", 1, 0, 24)
        ut("S", 0, 2, 6)
        ut("V", 0, 0, 7); ut("V", 0, 1, 7)
        rows("V", "a", 1, 24, 48)
        fixed(0, 0, 16); fixed(0, 16, 32); fixed(0, 32, 64)
        clear(1); turn(1, "b", False); turn(1, "a", True)
        cands(0)
        if last:
            last_rows()
        test(0, 0, 0, 16); test(0, 1, 0, 16)
        masks(1)
        test(0, 1, 16, 24)
        prods(1, STAY); tlist(1, 2, 6)
        prods(1, LEFT); prods(1, RIGHT)
        x = test_s(0, 1, 32, 64, 0)
        ut("S", 1, 2, 6)
        tlist(1, 0, 7); tlist(1, 1, 7)
        cands(1)
        fixed(1, 32, 64)
        test(0, 0, 16, 32); test(0, 1, 24, 32)
        finish(True, x)
        if last:
            last_columns()

    def finish(alone, x):
        test(0, 0, 32, 64)
        ut("V", 1, 0, 7); ut("V", 1, 1, 7)
        fails(0, 0, 4, alone, False)
        x()
        fails(0, 1, 4, alone, True)
        fixed(1, 0, 32)
        test(1, 0, 32, 64); test(1, 1, 32, 48)
        kept(0); test(1, 1, 48, 56)
        y = test_s(1, 1, 0, 32, 1)
        counts(0); test(1, 1, 56, 64)
        z = test_s(1, 0, 0, 16, 0)
        codes(0)
        y(); z()
        ranks(0)
        places(0); pack(0, 0, 8)
        test(1, 0, 16, 32)
        fails(1, 1, 5, alone, False); fails(1, 0, 5, alone, True)
        pack(0, 8, 14)
        scatter(0)
        kept(1); counts(1); codes(1); ranks(1)
        pack(1, 0, 4); places(1); pack(1, 4, 14)
        scatter(1)

    def doubled(s, tos):
        masks(s)
        prods(s, ((KB, 0), (KB, 1), (XB, 0), (XB, 1)), True)
        grow(s, "b", 0)
        prods(s, ((KA, 0), (KA, 1), (XA, 0), (XA, 1)), True)
        grow(s, "a", 0)
        for to in tos:
            grow(s, "b", to); grow(s, "a", to)
        prods(s, STAY + LEFT + RIGHT)
        clear(0)
        for j in (2, 0, 1):
            tlist(s, j, 4 + (j == 2))

    rows("S", "a", 0, 0, 32)
    turn(2, "a", False)
    rows("V", "b", 0, 16, 32); rows("S", "b", 0, 0, 16); turn(2, "b", True)
    true_sizes(0, "a"); true_sizes(1, "b")
    doubled(2, ())
    ulist("S", "b", 0); rows("S", "b", 0, 0, 64)
    ulist("V", "a", 0); rows("V", "a", 0, 0, 64)
    turn(3, "b", False); turn(3, "a", True)
    ut("S", 2, 2, 5); ut("S", 2, 0, 4); ut("S", 2, 1, 4)
    fixed(2, 0, 32)
    doubled(3, (1,))
    refill(["UL2_0"])
    ulist("S", "b", 0); rows("S", "b", 0, 0, 64)
    ulist("V", "a", 0); rows("V", "a", 0, 0, 64)
    turn(0, "b", False); turn(0, "a", True)
    ut("S", 3, 2, 5); ut("S", 3, 0, 4); ut("S", 3, 1, 4)
    test(2, 0, 0, 32)
    fixed(3, 0, 32)
    ulist("S", "b", 1); rows("S", "b", 1, 0, 64)
    decide(0)
    test(2, 1, 0, 32)
    ut("S", 0, 2, 6); ut("S", 0, 0, 7); ut("S", 0, 1, 7)
    fails(2, 0, 4, True, True); fails(2, 1, 4, True, True)
    cands(0); clear(1)
    turn(1, "b", False)
    fixed(0, 0, 32)
    act(T.F1[:], ps[4][:, 0:64], 1.0, [], ["F1"], [4])
    ulist("S", "a", 1)
    fixed(3, 32, 64)
    rows("S", "a", 1, 0, 64)
    test(3, 0, 0, 32); test(3, 1, 0, 32)
    fixed(0, 32, 64)
    test(0, 0, 0, 32); test(0, 1, 0, 24)
    test(3, 0, 32, 64); test(3, 1, 32, 64)
    turn(1, "a", True)
    carry(4, [(T.IB[:], T.F1[:])], ["F1"])
    fails(3, 0, 4, False, False); fails(3, 1, 4, False, True)
    masks(1)
    test(0, 1, 24, 32)
    prods(1, STAY); tlist(1, 2, 6)
    prods(1, LEFT); prods(1, RIGHT)
    x = test_s(0, 1, 32, 64, 0)
    act(T.F2[:], ps[4][:, 0:128], 1.0, [], ["F2"], [4])
    ut("S", 1, 2, 6)
    tlist(1, 0, 7); tlist(1, 1, 7)
    cands(1)
    fixed(1, 32, 64)
    for s in range(2):
        carry(4 + s, [(T.S2[:, 256 * s + 128 * i:256 * s + 128 * (i + 1)], T.F2[:, i::2, :]) for i in range(2)],
              ["S2", "F2"])
    finish(False, x)
    for rnd in (4, 5):
        reopen(True)
        full(rnd == 5)
    reopen(False)
    back("a", 1)

    def get(ch, lo, hi, e="S"):
        o, w = 1024 * ch + 16 * lo, 16 * (hi - lo)
        move(e, T.OB[:, o:o + w], tab("b", ch, lo, hi), TK["b"] + ["Ub%d" % ch], keys("OB%d" % ch, lo, hi))
        tt(T.OUT[:, o:o + w], tab("a", ch, lo, hi), T.OB[:, o:o + w], A.add,
           TK["a"] + ["Ua%d" % ch] + keys("OB%d" % ch, lo, hi), keys("OUT%d" % ch, lo, hi))

    def put(ch, qs):
        for r, y in enumerate((T.ya, T.yb, T.ys)):
            dma(qs[r], y[:, 1024 * ch:1024 * (ch + 1)], T.OUT[5 + r::16, 1024 * ch:1024 * (ch + 1)],
                keys("OUT%d" % ch, 0, 64), [])
    ulist("S", "b", 0); ulist("V", "a", 0)
    get(0, 0, 8, "V"); get(0, 8, 32); get(0, 32, 48)
    ulist("S", "b", 1); ulist("V", "a", 1)
    get(0, 48, 64)
    put(0, "YYY")
    get(1, 0, 32); get(1, 32, 64)
    put(1, "YSY")
    if not ORDER:
        ORDER.extend(order(calls))
    for j, e in ORDER:
        calls[j][1](e)
    ends["sent"] = sent[0]
    for s, v in ends.items():
        if max(x.get(s, 0) for x in seen.values()) < v:
            g.wait_ge(T.sem[s], v)
